import numpy as np
import ml_dtypes


def mxq(x, axis, fmt="e4m3"):
    dtype, down = {"e4m3": (ml_dtypes.float8_e4m3fn, 7), "e5m2": (ml_dtypes.float8_e5m2, 14)}[fmt]
    v = np.moveaxis(np.asarray(x, np.float32).astype(ml_dtypes.bfloat16).astype(np.float64), axis, -1)
    blocks = v.reshape(v.shape[:-1] + (-1, 32))
    amax = np.abs(blocks).max(-1, keepdims=True)
    byte = np.maximum(np.where(amax > 0, np.frexp(amax)[1] - 1 + 127, 0) - down, 1)
    scale = np.exp2(byte - 127.0)
    codes = (blocks / scale).astype(np.float32).astype(dtype).astype(np.float64)
    return np.moveaxis((codes * scale).reshape(v.shape), -1, axis)


WIDE = False


def mx_kscale(k):
    if not WIDE:
        return np.ones(k)
    levels = np.array([10, -10, 5, -5, 0])
    if k % 512:
        return np.exp2(np.random.permutation(np.resize(levels, k // 32))).repeat(32)
    a = np.empty((k // 512, 16))
    for p in range(k // 512):
        a[p, :8] = np.random.permutation(np.resize(levels, 8))
        for g in range(8):
            far = levels[np.abs(levels - a[p, g]) >= 10]
            a[p, g + 8] = far[np.random.randint(len(far))]
    return np.exp2(a.ravel()).repeat(32)


def f64(x):
    return np.asarray(x).astype(np.float64)


def striped(idx):
    return np.tile(idx.reshape(-1, 16).T, (8, 1)).astype(np.uint16)


def unstriped(offs):
    return offs[:16].T.reshape(-1).astype(np.int64)


E2M1 = np.array([0.0, 0.5, 1.0, 1.5, 2.0, 3.0, 4.0, 6.0, -0.0, -0.5, -1.0, -1.5, -2.0, -3.0, -4.0, -6.0])


def pack_weight(w, fmt):
    k, n = w.shape
    w = f64(np.asarray(w, np.float32).astype(ml_dtypes.bfloat16)).reshape(k // 32, 32, n)
    amax = np.abs(w).max(1)
    if fmt == "e4m3":
        byte = np.frexp(amax)[1] - 1 + 127 - 7
    else:
        mant, ex = np.frexp(amax / 6.0)
        byte = np.where(mant > 0.5, ex, ex - 1) + 127
    byte = np.clip(np.where(amax > 0, byte, 1), 1, 254)
    scaled = (w * np.exp2(127.0 - byte)[:, None, :]).reshape(k, n).astype(np.float32)
    by_word = np.ascontiguousarray(scaled.reshape(k // 512, 128, 4, n).transpose(0, 1, 3, 2))
    if fmt == "e4m3":
        words = by_word.astype(ml_dtypes.float8_e4m3fn).view(np.uint8)
    else:
        c = by_word.astype(ml_dtypes.float4_e2m1fn).view(np.uint8) & 0xF
        words = (c[..., 0::2] | (c[..., 1::2] << 4)).reshape(k // 512, 128, 2 * n)
    return np.ascontiguousarray(words), np.ascontiguousarray(byte.astype(np.uint8).reshape(k // 512, 16, n))


def unpack_weight(words, scales, fmt):
    g, _, n = scales.shape
    words = np.ascontiguousarray(words).reshape(g, 128, n, -1)
    if fmt == "e4m3":
        vals = words.view(ml_dtypes.float8_e4m3fn).astype(np.float64)
    else:
        nib = np.empty((g, 128, n, 4), np.uint8)
        nib[..., 0::2] = words & 0xF
        nib[..., 1::2] = words >> 4
        vals = E2M1[nib]
    vals = vals * np.repeat(np.exp2(scales.astype(np.float64) - 127.0), 8, axis=1)[..., None]
    return vals.transpose(0, 1, 3, 2).reshape(g * 512, n)


def gelu(v):
    return 0.5 * v * (1.0 + np.tanh(np.sqrt(2.0 / np.pi) * (v + 0.044715 * v**3)))


K, T, S, M, N = 1024, 2048, 1024, 1024, 512

def setup_inputs():
    n = np.random.standard_normal
    s = mx_kscale(K)[:, None]
    u = mx_kscale(S)
    idx = np.random.permutation(T)[:S]
    tab_words, tab_scales = pack_weight(n((K, T)) * s / np.sqrt(K), "e4m3")
    tab2_words, tab2_scales = pack_weight(n((K, T)) * s / np.sqrt(K), "e4m3")
    x_words, x_scales = pack_weight(n((K, M)) / s, "e4m3")
    wdT = n((N, T)) / np.sqrt(S)
    wdT[:, idx] /= u
    return {
        "tab_words": tab_words, "tab_scales": tab_scales,
        "tab2_words": tab2_words, "tab2_scales": tab2_scales,
        "offs": striped(idx),
        "x_words": x_words, "x_scales": x_scales,
        "wdT": wdT.astype(np.float32),
        "g": (np.exp(0.3 * n(S)) * u).astype(np.float32),
        "p": (1.0 / (1.0 + np.exp(-n(M)))).astype(np.float32),
    }

def reference(tab_words, tab_scales, tab2_words, tab2_scales, offs, x_words, x_scales, wdT, g, p):
    v = unpack_weight(tab_words, tab_scales, "e4m3")[:, unstriped(offs)]
    v2 = unpack_weight(tab2_words, tab2_scales, "e4m3")[:, unstriped(offs)]
    x = unpack_weight(x_words, x_scales, "e4m3")
    wd = f64(wdT)[:, unstriped(offs)]
    a = v.T @ x
    b = v2.T @ x
    h = a * (1.0 / (1.0 + np.exp(-a))) * b * f64(g)[:, None]
    y = mxq(wd, 1, "e4m3") @ mxq(h, 0, "e4m3")
    return y * f64(p)[None, :]

@@ -1,0 +1,228 @@
+from contextlib import ExitStack
+
+import concourse.mybir as mybir
+from concourse.masks import make_identity
+
+K, T, S, M, N = 1024, 2048, 1024, 1024, 512
+FLOPS = 2 * K * S * M * 2 + 2 * S * N * M
+
+F32 = mybir.dt.float32
+BF16 = mybir.dt.bfloat16
+I32 = mybir.dt.int32
+U32 = mybir.dt.uint32
+U16 = mybir.dt.uint16
+U8 = mybir.dt.uint8
+FP8X4 = mybir.dt.float8_e4m3fn_x4
+MULT = mybir.AluOpType.mult
+SILU = mybir.ActivationFunctionType.Silu
+COPY = mybir.ActivationFunctionType.Copy
+
+P = 128
+HALF = 512
+QUART = 256
+
+
+def tile_list_routed_swiglu_expert_kernel(
+    tc, tab_words, tab_scales, tab2_words, tab2_scales, offs, x_words, x_scales, wdT, g, p, out
+):
+    nc = tc.nc
+    with ExitStack() as ctx:
+        keep = ctx.enter_context(tc.tile_pool(name="keep", bufs=1))
+        ring = ctx.enter_context(tc.tile_pool(name="ring", bufs=3))
+        ps_ab = ctx.enter_context(tc.psum_pool(name="ps_ab", bufs=4))
+        ps_tr = ctx.enter_context(tc.psum_pool(name="ps_tr", bufs=2))
+        ps_y = ctx.enter_context(tc.psum_pool(name="ps_y", bufs=2))
+
+        offsets = keep.tile([P, S // 16], U16, name="offsets")
+        gate_sc = keep.tile([P, T // 4], I32, name="gate_sc", align_bytes=64)
+        up_sc = keep.tile([P, T // 4], I32, name="up_sc", align_bytes=64)
+        x_sc = keep.tile([P, M // 4], I32, name="x_sc", align_bytes=64)
+        g_rows = keep.tile([P, 2 * P], F32, name="g_rows")
+        ident = keep.tile([P, P], F32, name="ident")
+        nc.vector.memset(gate_sc[:], 0)
+        nc.vector.memset(up_sc[:], 0)
+        nc.vector.memset(x_sc[:], 0)
+        nc.gpsimd.memset(g_rows[:], 0.0)
+        make_identity(nc, ident[:])
+
+        def load_scales(plane, scales):
+            for q in range(4):
+                nc.sync.dma_start(
+                    out=plane[32 * q : 32 * q + 8, :], in_=scales[:, 4 * q : 4 * q + 4, :].bitcast(I32)
+                )
+
+        def load_words(name, words, a):
+            win = keep.tile([P, T], I32, name=name)
+            nc.sync.dma_start(out=win[:], in_=words[a].rearrange("p n i -> p (n i)").bitcast(I32))
+            return win
+
+        nc.sync.dma_start(offsets[:], offs)
+        load_scales(gate_sc, tab_scales)
+        gate_win = [load_words("gate_win%d" % a, tab_words, a) for a in range(2)]
+        up_win = [load_words("up_win0", tab2_words, 0)]
+        load_scales(up_sc, tab2_scales)
+        x_w = keep.tile([P, 2, M], I32, name="x_w", align_bytes=64)
+        nc.sync.dma_start(out=x_w[:], in_=x_words.rearrange("a p n i -> p a (n i)").bitcast(I32))
+        load_scales(x_sc, x_scales)
+        up_win.append(load_words("up_win1", tab2_words, 1))
+        nc.sync.dma_start(out=g_rows[0:4, :].rearrange("t (x r) -> t x r", r=8), in_=g.rearrange("(x t r) -> t x r", t=4, r=8))
+        wd_win = []
+        for nt in range(4):
+            win = keep.tile([P, T], F32, name="wd_win%d" % nt)
+            nc.sync.dma_start(out=win[:], in_=wdT[nt * P : (nt + 1) * P, :])
+            wd_win.append(win)
+        p_all = keep.tile([P, M], F32, name="p_all")
+        nc.sync.dma_start(out=p_all[:], in_=p.partition_broadcast(P))
+
+        def gather_words(name, win, dtype):
+            picked = keep.tile([P, S], dtype, name=name, align_bytes=64)
+            nc.vector.tensor_copy(
+                out=picked[:].bitcast(U32).rearrange("p (t x r) -> p x t r", t=4, r=8),
+                in_=win[:].bitcast(U32).indirect(offsets[:]),
+            )
+            return picked
+
+        def gather_scales(name, plane):
+            listed = keep.tile([P, S], U8, name=name + "_listed", align_bytes=64)
+            nc.vector.tensor_copy(out=listed[:], in_=plane[:].bitcast(U8).indirect(offsets[:]))
+            return listed
+
+        def reorder_scales(name, listed):
+            picked = keep.tile([P, S // 4], I32, name=name, align_bytes=64)
+            nc.vector.tensor_copy(
+                out=picked[:].rearrange("p (t x w) -> p t x w", t=4, w=2),
+                in_=listed[:].bitcast(I32).rearrange("p (x t w) -> p t x w", t=4, w=2),
+            )
+            return picked
+
+        gate_listed = gather_scales("gate_s", gate_sc)
+        gate_w = [gather_words("gate_w0", gate_win[0], I32)]
+        gate_s = reorder_scales("gate_s", gate_listed)
+        gate_w.append(gather_words("gate_w1", gate_win[1], I32))
+        up_w = [gather_words("up_w0", up_win[0], I32)]
+        up_listed = gather_scales("up_s", up_sc)
+        up_w.append(gather_words("up_w1", up_win[1], I32))
+        up_s = reorder_scales("up_s", up_listed)
+        wd_picked = [gather_words("wd_picked%d" % nt, wd_win[nt], F32) for nt in range(4)]
+
+        g_ps = ps_tr.tile([P, 4, P], F32, name="tr_bank")
+        for b in range(2):
+            nc.tensor.transpose(g_ps[:, b, :], g_rows[:, b * P : (b + 1) * P], ident[:])
+        gain = keep.tile([P, 2, 4], F32, name="gain")
+        nc.scalar.copy(out=gain[:], in_=g_ps[:, 0:2, 0:4])
+
+        def first_product(words, scales, b, t, mh):
+            bank = ps_ab.tile([P, HALF], F32, name="ab_bank")
+            cols = slice(2 * P * t + P * b, 2 * P * t + P * b + P)
+            toks = slice(HALF * mh, HALF * (mh + 1))
+            for a in range(2):
+                nc.tensor.matmul_mx(
+                    out=bank[:],
+                    lhsT=words[a][:, cols].bitcast(FP8X4),
+                    lhsT_scale=scales[:].bitcast(U8)[4 * a :, cols],
+                    rhs=x_w[:, a, toks].bitcast(FP8X4),
+                    rhs_scale=x_sc[:].bitcast(U8)[4 * a :, toks],
+                    start=(a == 0),
+                    stop=(a == 1),
+                )
+            return bank[:].rearrange("p (h m) -> p h m", h=2)
+
+        act = [keep.tile([P, 4, 2, HALF], F32, name="act%d" % mh) for mh in range(2)]
+        lin = [keep.tile([P, 4, 2, HALF], F32, name="lin%d" % mh) for mh in range(2)]
+
+        def gate_half(mh):
+            for b in range(2):
+                for t in range(4):
+                    bank = first_product(gate_w, gate_s, b, t, mh)
+                    nc.scalar.activation(out=act[mh][:, t, :, QUART * b : QUART * (b + 1)], in_=bank, func=SILU)
+
+        def up_half(mh):
+            for b in range(2):
+                for t in range(4):
+                    bank = first_product(up_w, up_s, b, t, mh)
+                    nc.scalar.activation(
+                        out=lin[mh][:, t, :, QUART * b : QUART * (b + 1)], in_=bank, func=COPY, scale=gain[:, b, t : t + 1]
+                    )
+
+        wd_bf = [keep.tile([P, 2, 2, HALF], BF16, name="wd_bf%d" % u, align_bytes=64) for u in range(2)]
+        wd_c = [keep.tile([P, HALF], U32, name="wd_c%d" % u, align_bytes=64) for u in range(2)]
+        wd_s = [keep.tile([P, HALF], U8, name="wd_s%d" % u, align_bytes=64) for u in range(2)]
+
+        def turn_wd(nt):
+            for b in range(2):
+                bank = ps_tr.tile([P, 4, P], F32, name="tr_bank")
+                for t in range(4):
+                    c0 = 2 * P * t + P * b
+                    nc.tensor.transpose(bank[:, t, :], wd_picked[nt][:, c0 : c0 + P], ident[:])
+                nc.scalar.copy(
+                    out=wd_bf[nt // 2][:, nt % 2, b, :].rearrange("p (c i t) -> p c t i", i=2, t=4),
+                    in_=bank[:].rearrange("p t (c i) -> p c t i", i=2),
+                )
+
+        def quantize_wd(u):
+            nc.vector.quantize_mx(
+                out=wd_c[u][:].bitcast(FP8X4), scales=wd_s[u][:], in_=wd_bf[u][:].rearrange("p n b c -> p (n b c)")
+            )
+
+        h_bf = [keep.tile([P, 4 * HALF], BF16, name="h_bf%d" % mq, align_bytes=64) for mq in range(4)]
+        h_c = [keep.tile([P, HALF], U32, name="h_c%d" % mq, align_bytes=64) for mq in range(4)]
+        h_s = [keep.tile([P, HALF], U8, name="h_s%d" % mq, align_bytes=64) for mq in range(4)]
+
+        def make_h(mq):
+            nc.vector.tensor_tensor(
+                out=h_bf[mq][:].rearrange("p (c i t) -> p c t i", i=2, t=4),
+                in0=act[mq // 2][:, :, mq % 2, :].rearrange("p t (c i) -> p c t i", i=2),
+                in1=lin[mq // 2][:, :, mq % 2, :].rearrange("p t (c i) -> p c t i", i=2),
+                op=MULT,
+            )
+
+        def quantize_h(mq):
+            nc.vector.quantize_mx(out=h_c[mq][:].bitcast(FP8X4), scales=h_s[mq][:], in_=h_bf[mq][:])
+
+        def down_product(mq):
+            toks = slice(QUART * mq, QUART * (mq + 1))
+            for u in range(2):
+                bank = ps_y.tile([P, 2, QUART], F32, name="y_bank")
+                for v in range(2):
+                    for b in range(2):
+                        cols = slice(2 * P * v + P * b, 2 * P * v + P * b + P)
+                        hcols = slice(QUART * b, QUART * (b + 1))
+                        nc.tensor.matmul_mx(
+                            out=bank[:, v, :],
+                            lhsT=wd_c[u][:, cols].bitcast(FP8X4),
+                            lhsT_scale=wd_s[u][:, cols],
+                            rhs=h_c[mq][:, hcols].bitcast(FP8X4),
+                            rhs_scale=h_s[mq][:, hcols],
+                            start=(b == 0),
+                            stop=(b == 1),
+                        )
+                y = ring.tile([P, 2, QUART], F32, name="y")
+                nc.vector.tensor_tensor(
+                    out=y[:], in0=bank[:], in1=p_all[:, toks].unsqueeze(1).to_broadcast([P, 2, QUART]), op=MULT
+                )
+                nc.sync.dma_start(
+                    out=out[2 * P * u : 2 * P * (u + 1), toks].rearrange("(v p) m -> p v m", v=2), in_=y[:]
+                )
+
+        gate_half(0)
+        up_half(0)
+        turn_wd(0)
+        turn_wd(1)
+        gate_half(1)
+        turn_wd(2)
+        turn_wd(3)
+        up_half(1)
+        make_h(0)
+        make_h(1)
+        quantize_h(0)
+        quantize_wd(0)
+        quantize_h(1)
+        quantize_wd(1)
+        down_product(0)
+        make_h(2)
+        down_product(1)
+        quantize_h(2)
+        make_h(3)
+        down_product(2)
+        quantize_h(3)
+        down_product(3)

@@ -29,9 +29,9 @@ def tile_list_routed_swiglu_expert_kernel(
     with ExitStack() as ctx:
         keep = ctx.enter_context(tc.tile_pool(name="keep", bufs=1))
         ring = ctx.enter_context(tc.tile_pool(name="ring", bufs=3))
-        ps_ab = ctx.enter_context(tc.psum_pool(name="ps_ab", bufs=4))
-        ps_tr = ctx.enter_context(tc.psum_pool(name="ps_tr", bufs=2))
-        ps_y = ctx.enter_context(tc.psum_pool(name="ps_y", bufs=2))
+        wins = ctx.enter_context(tc.tile_pool(name="wins", bufs=6))
+        hring = ctx.enter_context(tc.tile_pool(name="hring", bufs=4))
+        psum = ctx.enter_context(tc.psum_pool(name="psum", bufs=8))
 
         offsets = keep.tile([P, S // 16], U16, name="offsets")
         gate_sc = keep.tile([P, T // 4], I32, name="gate_sc", align_bytes=64)
@@ -45,34 +45,36 @@ def tile_list_routed_swiglu_expert_kernel(
         nc.gpsimd.memset(g_rows[:], 0.0)
         make_identity(nc, ident[:])
 
-        def load_scales(plane, scales):
+        def load_scales(queue, plane, scales):
             for q in range(4):
-                nc.sync.dma_start(
+                queue.dma_start(
                     out=plane[32 * q : 32 * q + 8, :], in_=scales[:, 4 * q : 4 * q + 4, :].bitcast(I32)
                 )
 
         def load_words(name, words, a):
-            win = keep.tile([P, T], I32, name=name)
+            win = wins.tile([P, T], I32, name=name, tag="win")
             nc.sync.dma_start(out=win[:], in_=words[a].rearrange("p n i -> p (n i)").bitcast(I32))
             return win
 
         nc.sync.dma_start(offsets[:], offs)
-        load_scales(gate_sc, tab_scales)
+        load_scales(nc.sync, gate_sc, tab_scales)
         gate_win = [load_words("gate_win%d" % a, tab_words, a) for a in range(2)]
-        up_win = [load_words("up_win0", tab2_words, 0)]
-        load_scales(up_sc, tab2_scales)
-        x_w = keep.tile([P, 2, M], I32, name="x_w", align_bytes=64)
-        nc.sync.dma_start(out=x_w[:], in_=x_words.rearrange("a p n i -> p a (n i)").bitcast(I32))
-        load_scales(x_sc, x_scales)
-        up_win.append(load_words("up_win1", tab2_words, 1))
+        load_scales(nc.sync, x_sc, x_scales)
+        x_all = x_words.rearrange("a p n i -> p a (n i)").bitcast(I32)
+        x_w = [keep.tile([P, 2, HALF], I32, name="x_w%d" % mh, align_bytes=64) for mh in range(2)]
+        for mh in range(2):
+            nc.sync.dma_start(out=x_w[mh][:], in_=x_all[:, :, HALF * mh : HALF * (mh + 1)])
         nc.sync.dma_start(out=g_rows[0:4, :].rearrange("t (x r) -> t x r", r=8), in_=g.rearrange("(x t r) -> t x r", t=4, r=8))
+        nc.sync.dma_start(out=g_rows[4:6, :], in_=p[0:HALF].rearrange("(q m) -> q m", q=2))
+        load_scales(nc.sync, up_sc, tab2_scales)
+        up_win = [load_words("up_win%d" % a, tab2_words, a) for a in range(2)]
         wd_win = []
         for nt in range(4):
-            win = keep.tile([P, T], F32, name="wd_win%d" % nt)
+            win = wins.tile([P, T], F32, name="wd_win%d" % nt, tag="win")
             nc.sync.dma_start(out=win[:], in_=wdT[nt * P : (nt + 1) * P, :])
             wd_win.append(win)
-        p_all = keep.tile([P, M], F32, name="p_all")
-        nc.sync.dma_start(out=p_all[:], in_=p.partition_broadcast(P))
+        p_all = keep.tile([P, HALF], F32, name="p_all")
+        nc.sync.dma_start(out=p_all[:], in_=p[HALF:M].partition_broadcast(P))
 
         def gather_words(name, win, dtype):
             picked = keep.tile([P, S], dtype, name=name, align_bytes=64)
@@ -95,80 +97,107 @@ def tile_list_routed_swiglu_expert_kernel(
             )
             return picked
 
-        gate_listed = gather_scales("gate_s", gate_sc)
-        gate_w = [gather_words("gate_w0", gate_win[0], I32)]
-        gate_s = reorder_scales("gate_s", gate_listed)
-        gate_w.append(gather_words("gate_w1", gate_win[1], I32))
-        up_w = [gather_words("up_w0", up_win[0], I32)]
+        gate_s = [keep.tile([P, HALF // 4], I32, name="gate_s%d" % b, align_bytes=64) for b in range(2)]
+        gate_w = [[keep.tile([P, HALF], I32, name="gate_w%d%d" % (a, b), align_bytes=64) for b in range(2)] for a in range(2)]
+        for b in range(2):
+            part = offsets[:, 32 * b : 32 * (b + 1)]
+            listed = keep.tile([P, HALF], U8, name="gate_listed%d" % b, align_bytes=64)
+            nc.vector.tensor_copy(out=listed[:], in_=gate_sc[:].bitcast(U8).indirect(part))
+            for a in range(2):
+                nc.vector.tensor_copy(
+                    out=gate_w[a][b][:].bitcast(U32).rearrange("p (t q r) -> p q t r", t=4, r=8),
+                    in_=gate_win[a][:].bitcast(U32).indirect(part),
+                )
+                if a == 0:
+                    nc.vector.tensor_copy(
+                        out=gate_s[b][:].rearrange("p (t q w) -> p t q w", t=4, w=2),
+                        in_=listed[:].bitcast(I32).rearrange("p (q t w) -> p t q w", t=4, w=2),
+                    )
         up_listed = gather_scales("up_s", up_sc)
-        up_w.append(gather_words("up_w1", up_win[1], I32))
+        up_w = [gather_words("up_w0", up_win[0], I32)]
         up_s = reorder_scales("up_s", up_listed)
+        up_w.append(gather_words("up_w1", up_win[1], I32))
         wd_picked = [gather_words("wd_picked%d" % nt, wd_win[nt], F32) for nt in range(4)]
 
-        g_ps = ps_tr.tile([P, 4, P], F32, name="tr_bank")
-        for b in range(2):
-            nc.tensor.transpose(g_ps[:, b, :], g_rows[:, b * P : (b + 1) * P], ident[:])
-        gain = keep.tile([P, 2, 4], F32, name="gain")
-        nc.scalar.copy(out=gain[:], in_=g_ps[:, 0:2, 0:4])
-
-        def first_product(words, scales, b, t, mh):
-            bank = ps_ab.tile([P, HALF], F32, name="ab_bank")
-            cols = slice(2 * P * t + P * b, 2 * P * t + P * b + P)
-            toks = slice(HALF * mh, HALF * (mh + 1))
+        def first_product(dst, words, scales, cols, toks):
             for a in range(2):
                 nc.tensor.matmul_mx(
-                    out=bank[:],
+                    out=dst,
                     lhsT=words[a][:, cols].bitcast(FP8X4),
                     lhsT_scale=scales[:].bitcast(U8)[4 * a :, cols],
-                    rhs=x_w[:, a, toks].bitcast(FP8X4),
+                    rhs=x_w[toks.start // HALF][:, a, toks.start % HALF : toks.start % HALF + toks.stop - toks.start].bitcast(FP8X4),
                     rhs_scale=x_sc[:].bitcast(U8)[4 * a :, toks],
                     start=(a == 0),
                     stop=(a == 1),
                 )
-            return bank[:].rearrange("p (h m) -> p h m", h=2)
 
         act = [keep.tile([P, 4, 2, HALF], F32, name="act%d" % mh) for mh in range(2)]
         lin = [keep.tile([P, 4, 2, HALF], F32, name="lin%d" % mh) for mh in range(2)]
 
-        def gate_half(mh):
-            for b in range(2):
+        def gate_half(b):
+            for mh in range(2):
                 for t in range(4):
-                    bank = first_product(gate_w, gate_s, b, t, mh)
-                    nc.scalar.activation(out=act[mh][:, t, :, QUART * b : QUART * (b + 1)], in_=bank, func=SILU)
+                    bank = psum.tile([P, HALF], F32, name="bank")
+                    first_product(bank[:], [gate_w[0][b], gate_w[1][b]], gate_s[b], slice(P * t, P * (t + 1)), slice(HALF * mh, HALF * (mh + 1)))
+                    nc.scalar.activation(
+                        out=act[mh][:, t, :, QUART * b : QUART * (b + 1)],
+                        in_=bank[:].rearrange("p (h m) -> p h m", h=2),
+                        func=SILU,
+                    )
 
         def up_half(mh):
             for b in range(2):
                 for t in range(4):
-                    bank = first_product(up_w, up_s, b, t, mh)
+                    bank = psum.tile([P, HALF], F32, name="bank")
+                    first_product(bank[:], up_w, up_s, slice(2 * P * t + P * b, 2 * P * t + P * b + P), slice(HALF * mh, HALF * (mh + 1)))
                     nc.scalar.activation(
-                        out=lin[mh][:, t, :, QUART * b : QUART * (b + 1)], in_=bank, func=COPY, scale=gain[:, b, t : t + 1]
+                        out=lin[mh][:, t, :, QUART * b : QUART * (b + 1)],
+                        in_=bank[:].rearrange("p (h m) -> p h m", h=2),
+                        func=COPY,
+                        scale=gain[:, b, t : t + 1],
                     )
 
-        wd_bf = [keep.tile([P, 2, 2, HALF], BF16, name="wd_bf%d" % u, align_bytes=64) for u in range(2)]
+        def up_quarter(mq):
+            for t in range(4):
+                bank = psum.tile([P, HALF], F32, name="bank")
+                for b in range(2):
+                    first_product(
+                        bank[:, QUART * b : QUART * (b + 1)], up_w, up_s, slice(2 * P * t + P * b, 2 * P * t + P * b + P), slice(QUART * mq, QUART * (mq + 1))
+                    )
+                for b in range(2):
+                    nc.scalar.activation(
+                        out=lin[mq // 2][:, t, mq % 2, QUART * b : QUART * (b + 1)],
+                        in_=bank[:, QUART * b : QUART * (b + 1)],
+                        func=COPY,
+                        scale=gain[:, b, t : t + 1],
+                    )
+
+        wd_bf = [keep.tile([P, 4, HALF], BF16, name="wd_bf%d" % u, align_bytes=64) for u in range(2)]
         wd_c = [keep.tile([P, HALF], U32, name="wd_c%d" % u, align_bytes=64) for u in range(2)]
         wd_s = [keep.tile([P, HALF], U8, name="wd_s%d" % u, align_bytes=64) for u in range(2)]
 
         def turn_wd(nt):
             for b in range(2):
-                bank = ps_tr.tile([P, 4, P], F32, name="tr_bank")
+                bank = psum.tile([P, 4, P], F32, name="bank")
                 for t in range(4):
                     c0 = 2 * P * t + P * b
                     nc.tensor.transpose(bank[:, t, :], wd_picked[nt][:, c0 : c0 + P], ident[:])
                 nc.scalar.copy(
-                    out=wd_bf[nt // 2][:, nt % 2, b, :].rearrange("p (c i t) -> p c t i", i=2, t=4),
+                    out=wd_bf[b][:, nt, :].rearrange("p (c i t) -> p c t i", i=2, t=4),
                     in_=bank[:].rearrange("p t (c i) -> p c t i", i=2),
                 )
 
         def quantize_wd(u):
             nc.vector.quantize_mx(
-                out=wd_c[u][:].bitcast(FP8X4), scales=wd_s[u][:], in_=wd_bf[u][:].rearrange("p n b c -> p (n b c)")
+                out=wd_c[u][:].bitcast(FP8X4), scales=wd_s[u][:], in_=wd_bf[u][:].rearrange("p n c -> p (n c)")
             )
 
-        h_bf = [keep.tile([P, 4 * HALF], BF16, name="h_bf%d" % mq, align_bytes=64) for mq in range(4)]
+        h_bf = {}
         h_c = [keep.tile([P, HALF], U32, name="h_c%d" % mq, align_bytes=64) for mq in range(4)]
         h_s = [keep.tile([P, HALF], U8, name="h_s%d" % mq, align_bytes=64) for mq in range(4)]
 
         def make_h(mq):
+            h_bf[mq] = hring.tile([P, 4 * HALF], BF16, name="h_bf", align_bytes=64)
             nc.vector.tensor_tensor(
                 out=h_bf[mq][:].rearrange("p (c i t) -> p c t i", i=2, t=4),
                 in0=act[mq // 2][:, :, mq % 2, :].rearrange("p t (c i) -> p c t i", i=2),
@@ -182,47 +211,87 @@ def tile_list_routed_swiglu_expert_kernel(
         def down_product(mq):
             toks = slice(QUART * mq, QUART * (mq + 1))
             for u in range(2):
-                bank = ps_y.tile([P, 2, QUART], F32, name="y_bank")
+                bank = psum.tile([P, 2, QUART], F32, name="bank")
                 for v in range(2):
                     for b in range(2):
-                        cols = slice(2 * P * v + P * b, 2 * P * v + P * b + P)
+                        cols = slice(2 * P * u + P * v, 2 * P * u + P * v + P)
                         hcols = slice(QUART * b, QUART * (b + 1))
                         nc.tensor.matmul_mx(
                             out=bank[:, v, :],
-                            lhsT=wd_c[u][:, cols].bitcast(FP8X4),
-                            lhsT_scale=wd_s[u][:, cols],
+                            lhsT=wd_c[b][:, cols].bitcast(FP8X4),
+                            lhsT_scale=wd_s[b][:, cols],
                             rhs=h_c[mq][:, hcols].bitcast(FP8X4),
                             rhs_scale=h_s[mq][:, hcols],
                             start=(b == 0),
                             stop=(b == 1),
                         )
-                y = ring.tile([P, 2, QUART], F32, name="y")
+                y = ring.tile([P, 2, QUART], F32, name="y", bufs=4)
                 nc.vector.tensor_tensor(
-                    out=y[:], in0=bank[:], in1=p_all[:, toks].unsqueeze(1).to_broadcast([P, 2, QUART]), op=MULT
+                    out=y[:], in0=bank[:], in1=p_all[:, QUART * (mq - 2) : QUART * (mq - 1)].unsqueeze(1).to_broadcast([P, 2, QUART]), op=MULT
                 )
                 nc.sync.dma_start(
                     out=out[2 * P * u : 2 * P * (u + 1), toks].rearrange("(v p) m -> p v m", v=2), in_=y[:]
                 )
 
+        def down_product_turned(mq):
+            scaled_tiles = []
+            for mt in range(2):
+                bank = psum.tile([P, HALF], F32, name="bank")
+                for b in range(2):
+                    hcols = slice(QUART * b + P * mt, QUART * b + P * (mt + 1))
+                    nc.tensor.matmul_mx(
+                        out=bank[:],
+                        lhsT=h_c[mq][:, hcols].bitcast(FP8X4),
+                        lhsT_scale=h_s[mq][:, hcols],
+                        rhs=wd_c[b][:].bitcast(FP8X4),
+                        rhs_scale=wd_s[b][:],
+                        start=(b == 0),
+                        stop=(b == 1),
+                    )
+                scaled = ring.tile([P, N], F32, name="scaled", bufs=4)
+                nc.scalar.activation(out=scaled[:], in_=bank[:], func=COPY, scale=gain[:, mt, 4 + mq : 5 + mq])
+                scaled_tiles.append(scaled)
+            return scaled_tiles
+
+        def turn_back(mq, scaled_tiles):
+            y = ring.tile([P, 4, QUART], F32, name="y_turned", bufs=2)
+            for mt in range(2):
+                scaled = scaled_tiles[mt]
+                back = psum.tile([P, 4, P], F32, name="bank")
+                for nt in range(4):
+                    nc.tensor.transpose(back[:, nt, :], scaled[:, P * nt : P * (nt + 1)], ident[:])
+                nc.scalar.copy(out=y[:, :, P * mt : P * (mt + 1)], in_=back[:])
+            nc.sync.dma_start(
+                out=out[:, QUART * mq : QUART * (mq + 1)].rearrange("(v p) m -> p v m", v=4), in_=y[:]
+            )
+
         gate_half(0)
+        gate_half(1)
+        g_ps = psum.tile([P, 4, P], F32, name="bank")
+        for b in range(2):
+            nc.tensor.transpose(g_ps[:, b, :], g_rows[:, b * P : (b + 1) * P], ident[:])
+        gain = keep.tile([P, 2, 6], F32, name="gain")
+        nc.scalar.copy(out=gain[:], in_=g_ps[:, 0:2, 0:6])
+
         up_half(0)
         turn_wd(0)
         turn_wd(1)
-        gate_half(1)
+        up_quarter(2)
         turn_wd(2)
         turn_wd(3)
-        up_half(1)
+        up_quarter(3)
         make_h(0)
         make_h(1)
         quantize_h(0)
         quantize_wd(0)
         quantize_h(1)
         quantize_wd(1)
-        down_product(0)
         make_h(2)
-        down_product(1)
-        quantize_h(2)
+        turned = [down_product_turned(mq) for mq in range(2)]
         make_h(3)
-        down_product(2)
+        quantize_h(2)
+        for mq in range(2):
+            turn_back(mq, turned[mq])
         quantize_h(3)
+        down_product(2)
         down_product(3)

@@ -29,9 +29,13 @@ def tile_list_routed_swiglu_expert_kernel(
     with ExitStack() as ctx:
         keep = ctx.enter_context(tc.tile_pool(name="keep", bufs=1))
         ring = ctx.enter_context(tc.tile_pool(name="ring", bufs=3))
-        wins = ctx.enter_context(tc.tile_pool(name="wins", bufs=6))
-        hring = ctx.enter_context(tc.tile_pool(name="hring", bufs=4))
-        psum = ctx.enter_context(tc.psum_pool(name="psum", bufs=8))
+        psum = ctx.enter_context(tc.psum_pool(name="psum", bufs=1))
+        taken = []
+
+        def new_bank(shape):
+            taken.append(shape)
+            return psum.tile(shape, F32, name="bank%d" % (len(taken) % 8))
+
 
         offsets = keep.tile([P, S // 16], U16, name="offsets")
         gate_sc = keep.tile([P, T // 4], I32, name="gate_sc", align_bytes=64)
@@ -44,6 +48,8 @@ def tile_list_routed_swiglu_expert_kernel(
         nc.vector.memset(x_sc[:], 0)
         nc.gpsimd.memset(g_rows[:], 0.0)
         make_identity(nc, ident[:])
+        warm = keep.tile([P, 1], F32, name="warm")
+        nc.scalar.activation(out=warm[:], in_=g_rows[:, 0:1], func=SILU)
 
         def load_scales(queue, plane, scales):
             for q in range(4):
@@ -52,7 +58,7 @@ def tile_list_routed_swiglu_expert_kernel(
                 )
 
         def load_words(name, words, a):
-            win = wins.tile([P, T], I32, name=name, tag="win")
+            win = keep.tile([P, T], I32, name=name)
             nc.sync.dma_start(out=win[:], in_=words[a].rearrange("p n i -> p (n i)").bitcast(I32))
             return win
 
@@ -62,19 +68,21 @@ def tile_list_routed_swiglu_expert_kernel(
         load_scales(nc.sync, x_sc, x_scales)
         x_all = x_words.rearrange("a p n i -> p a (n i)").bitcast(I32)
         x_w = [keep.tile([P, 2, HALF], I32, name="x_w%d" % mh, align_bytes=64) for mh in range(2)]
-        for mh in range(2):
-            nc.sync.dma_start(out=x_w[mh][:], in_=x_all[:, :, HALF * mh : HALF * (mh + 1)])
-        nc.sync.dma_start(out=g_rows[0:4, :].rearrange("t (x r) -> t x r", r=8), in_=g.rearrange("(x t r) -> t x r", t=4, r=8))
-        nc.sync.dma_start(out=g_rows[4:6, :], in_=p[0:HALF].rearrange("(q m) -> q m", q=2))
+        nc.sync.dma_start(out=x_w[0][:], in_=x_all[:, :, 0:HALF])
         load_scales(nc.sync, up_sc, tab2_scales)
+        nc.sync.dma_start(out=x_w[1][:], in_=x_all[:, :, HALF:M])
         up_win = [load_words("up_win%d" % a, tab2_words, a) for a in range(2)]
+        nc.sync.dma_start(out=g_rows[0:4, :].rearrange("t (x r) -> t x r", r=8), in_=g.rearrange("(x t r) -> t x r", t=4, r=8))
+        nc.sync.dma_start(out=g_rows[4:6, :], in_=p[QUART : 3 * QUART].rearrange("(q m) -> q m", q=2))
         wd_win = []
         for nt in range(4):
-            win = wins.tile([P, T], F32, name="wd_win%d" % nt, tag="win")
+            win = keep.tile([P, T], F32, name="wd_win%d" % nt, align_bytes=64)
             nc.sync.dma_start(out=win[:], in_=wdT[nt * P : (nt + 1) * P, :])
             wd_win.append(win)
-        p_all = keep.tile([P, HALF], F32, name="p_all")
-        nc.sync.dma_start(out=p_all[:], in_=p[HALF:M].partition_broadcast(P))
+        p_all = {}
+        for mq in (0, 3):
+            p_all[mq] = keep.tile([P, QUART], F32, name="p_all%d" % mq)
+            nc.sync.dma_start(out=p_all[mq][:], in_=p[QUART * mq : QUART * (mq + 1)].partition_broadcast(P))
 
         def gather_words(name, win, dtype):
             picked = keep.tile([P, S], dtype, name=name, align_bytes=64)
@@ -137,7 +145,7 @@ def tile_list_routed_swiglu_expert_kernel(
         def gate_half(b):
             for mh in range(2):
                 for t in range(4):
-                    bank = psum.tile([P, HALF], F32, name="bank")
+                    bank = new_bank([P, HALF])
                     first_product(bank[:], [gate_w[0][b], gate_w[1][b]], gate_s[b], slice(P * t, P * (t + 1)), slice(HALF * mh, HALF * (mh + 1)))
                     nc.scalar.activation(
                         out=act[mh][:, t, :, QUART * b : QUART * (b + 1)],
@@ -148,7 +156,7 @@ def tile_list_routed_swiglu_expert_kernel(
         def up_half(mh):
             for b in range(2):
                 for t in range(4):
-                    bank = psum.tile([P, HALF], F32, name="bank")
+                    bank = new_bank([P, HALF])
                     first_product(bank[:], up_w, up_s, slice(2 * P * t + P * b, 2 * P * t + P * b + P), slice(HALF * mh, HALF * (mh + 1)))
                     nc.scalar.activation(
                         out=lin[mh][:, t, :, QUART * b : QUART * (b + 1)],
@@ -159,7 +167,7 @@ def tile_list_routed_swiglu_expert_kernel(
 
         def up_quarter(mq):
             for t in range(4):
-                bank = psum.tile([P, HALF], F32, name="bank")
+                bank = new_bank([P, HALF])
                 for b in range(2):
                     first_product(
                         bank[:, QUART * b : QUART * (b + 1)], up_w, up_s, slice(2 * P * t + P * b, 2 * P * t + P * b + P), slice(QUART * mq, QUART * (mq + 1))
@@ -178,7 +186,7 @@ def tile_list_routed_swiglu_expert_kernel(
 
         def turn_wd(nt):
             for b in range(2):
-                bank = psum.tile([P, 4, P], F32, name="bank")
+                bank = new_bank([P, 4, P])
                 for t in range(4):
                     c0 = 2 * P * t + P * b
                     nc.tensor.transpose(bank[:, t, :], wd_picked[nt][:, c0 : c0 + P], ident[:])
@@ -197,7 +205,7 @@ def tile_list_routed_swiglu_expert_kernel(
         h_s = [keep.tile([P, HALF], U8, name="h_s%d" % mq, align_bytes=64) for mq in range(4)]
 
         def make_h(mq):
-            h_bf[mq] = hring.tile([P, 4 * HALF], BF16, name="h_bf", align_bytes=64)
+            h_bf[mq] = keep.tile([P, 4 * HALF], BF16, name="h_bf%d" % mq, tag="wd_win%d" % (3 - mq), align_bytes=64)
             nc.vector.tensor_tensor(
                 out=h_bf[mq][:].rearrange("p (c i t) -> p c t i", i=2, t=4),
                 in0=act[mq // 2][:, :, mq % 2, :].rearrange("p t (c i) -> p c t i", i=2),
@@ -211,7 +219,7 @@ def tile_list_routed_swiglu_expert_kernel(
         def down_product(mq):
             toks = slice(QUART * mq, QUART * (mq + 1))
             for u in range(2):
-                bank = psum.tile([P, 2, QUART], F32, name="bank")
+                bank = new_bank([P, 2, QUART])
                 for v in range(2):
                     for b in range(2):
                         cols = slice(2 * P * u + P * v, 2 * P * u + P * v + P)
@@ -227,7 +235,7 @@ def tile_list_routed_swiglu_expert_kernel(
                         )
                 y = ring.tile([P, 2, QUART], F32, name="y", bufs=4)
                 nc.vector.tensor_tensor(
-                    out=y[:], in0=bank[:], in1=p_all[:, QUART * (mq - 2) : QUART * (mq - 1)].unsqueeze(1).to_broadcast([P, 2, QUART]), op=MULT
+                    out=y[:], in0=bank[:], in1=p_all[mq][:].unsqueeze(1).to_broadcast([P, 2, QUART]), op=MULT
                 )
                 nc.sync.dma_start(
                     out=out[2 * P * u : 2 * P * (u + 1), toks].rearrange("(v p) m -> p v m", v=2), in_=y[:]
@@ -236,7 +244,7 @@ def tile_list_routed_swiglu_expert_kernel(
         def down_product_turned(mq):
             scaled_tiles = []
             for mt in range(2):
-                bank = psum.tile([P, HALF], F32, name="bank")
+                bank = new_bank([P, HALF])
                 for b in range(2):
                     hcols = slice(QUART * b + P * mt, QUART * b + P * (mt + 1))
                     nc.tensor.matmul_mx(
@@ -249,7 +257,7 @@ def tile_list_routed_swiglu_expert_kernel(
                         stop=(b == 1),
                     )
                 scaled = ring.tile([P, N], F32, name="scaled", bufs=4)
-                nc.scalar.activation(out=scaled[:], in_=bank[:], func=COPY, scale=gain[:, mt, 4 + mq : 5 + mq])
+                nc.scalar.activation(out=scaled[:], in_=bank[:], func=COPY, scale=gain[:, mt, 3 + mq : 4 + mq])
                 scaled_tiles.append(scaled)
             return scaled_tiles
 
@@ -257,7 +265,7 @@ def tile_list_routed_swiglu_expert_kernel(
             y = ring.tile([P, 4, QUART], F32, name="y_turned", bufs=2)
             for mt in range(2):
                 scaled = scaled_tiles[mt]
-                back = psum.tile([P, 4, P], F32, name="bank")
+                back = new_bank([P, 4, P])
                 for nt in range(4):
                     nc.tensor.transpose(back[:, nt, :], scaled[:, P * nt : P * (nt + 1)], ident[:])
                 nc.scalar.copy(out=y[:, :, P * mt : P * (mt + 1)], in_=back[:])
@@ -267,7 +275,7 @@ def tile_list_routed_swiglu_expert_kernel(
 
         gate_half(0)
         gate_half(1)
-        g_ps = psum.tile([P, 4, P], F32, name="bank")
+        g_ps = new_bank([P, 4, P])
         for b in range(2):
             nc.tensor.transpose(g_ps[:, b, :], g_rows[:, b * P : (b + 1) * P], ident[:])
         gain = keep.tile([P, 2, 6], F32, name="gain")
@@ -287,11 +295,12 @@ def tile_list_routed_swiglu_expert_kernel(
         quantize_h(1)
         quantize_wd(1)
         make_h(2)
-        turned = [down_product_turned(mq) for mq in range(2)]
-        make_h(3)
+        down_product(0)
+        turned = down_product_turned(1)
         quantize_h(2)
-        for mq in range(2):
-            turn_back(mq, turned[mq])
+        turn_back(1, turned)
+        make_h(3)
+        turned = down_product_turned(2)
         quantize_h(3)
-        down_product(2)
         down_product(3)
+        turn_back(2, turned)

@@ -20,6 +20,7 @@ COPY = mybir.ActivationFunctionType.Copy
 P = 128
 HALF = 512
 QUART = 256
+WINS_BYTES = 8 * 4 * T + 2 * 4 * M + 3 * 4 * QUART
 
 
 def tile_list_routed_swiglu_expert_kernel(
@@ -28,6 +29,7 @@ def tile_list_routed_swiglu_expert_kernel(
     nc = tc.nc
     with ExitStack() as ctx:
         keep = ctx.enter_context(tc.tile_pool(name="keep", bufs=1))
+        wins = ctx.enter_context(tc.tile_pool(name="wins", bufs=1))
         ring = ctx.enter_context(tc.tile_pool(name="ring", bufs=3))
         psum = ctx.enter_context(tc.psum_pool(name="psum", bufs=1))
         taken = []
@@ -41,15 +43,25 @@ def tile_list_routed_swiglu_expert_kernel(
         gate_sc = keep.tile([P, T // 4], I32, name="gate_sc", align_bytes=64)
         up_sc = keep.tile([P, T // 4], I32, name="up_sc", align_bytes=64)
         x_sc = keep.tile([P, M // 4], I32, name="x_sc", align_bytes=64)
-        g_rows = keep.tile([P, 2 * P], F32, name="g_rows")
         ident = keep.tile([P, P], F32, name="ident")
         nc.vector.memset(gate_sc[:], 0)
         nc.vector.memset(up_sc[:], 0)
         nc.vector.memset(x_sc[:], 0)
-        nc.gpsimd.memset(g_rows[:], 0.0)
-        make_identity(nc, ident[:])
+        warm_in = wins.tile([P, WINS_BYTES // 4], F32, name="warm_in", offset=0)
+        nc.gpsimd.memset(warm_in[:, 0:1], 0.0)
         warm = keep.tile([P, 1], F32, name="warm")
-        nc.scalar.activation(out=warm[:], in_=g_rows[:, 0:1], func=SILU)
+        nc.scalar.activation(out=warm[:], in_=warm_in[:, 0:1], func=SILU)
+        make_identity(nc, ident[:])
+        placed = {}
+
+        def place(name, shape, dtype, size):
+            placed[name] = sum(sizes)
+            sizes.append(size)
+            return wins.tile(shape, dtype, name=name, offset=placed[name])
+
+        sizes = []
+        g_rows = place("g_rows", [P, 2 * P], F32, 8 * P)
+        nc.gpsimd.memset(g_rows[:], 0.0)
 
         def load_scales(queue, plane, scales):
             for q in range(4):
@@ -58,30 +70,31 @@ def tile_list_routed_swiglu_expert_kernel(
                 )
 
         def load_words(name, words, a):
-            win = keep.tile([P, T], I32, name=name)
+            win = place(name, [P, T], I32, 4 * T)
             nc.sync.dma_start(out=win[:], in_=words[a].rearrange("p n i -> p (n i)").bitcast(I32))
             return win
 
         nc.sync.dma_start(offsets[:], offs)
         load_scales(nc.sync, gate_sc, tab_scales)
-        gate_win = [load_words("gate_win%d" % a, tab_words, a) for a in range(2)]
-        load_scales(nc.sync, x_sc, x_scales)
-        x_all = x_words.rearrange("a p n i -> p a (n i)").bitcast(I32)
-        x_w = [keep.tile([P, 2, HALF], I32, name="x_w%d" % mh, align_bytes=64) for mh in range(2)]
-        nc.sync.dma_start(out=x_w[0][:], in_=x_all[:, :, 0:HALF])
         load_scales(nc.sync, up_sc, tab2_scales)
-        nc.sync.dma_start(out=x_w[1][:], in_=x_all[:, :, HALF:M])
+        load_scales(nc.sync, x_sc, x_scales)
+        gate_win = [load_words("gate_win0", tab_words, 0)]
+        x_all = x_words.rearrange("a p n i -> p a (n i)").bitcast(I32)
+        x_w = [place("x_w%d" % mh, [P, 2, HALF], I32, 8 * HALF) for mh in range(2)]
+        nc.sync.dma_start(out=x_w[0][:], in_=x_all[:, :, 0:HALF])
+        gate_win.append(load_words("gate_win1", tab_words, 1))
         up_win = [load_words("up_win%d" % a, tab2_words, a) for a in range(2)]
+        nc.sync.dma_start(out=x_w[1][:], in_=x_all[:, :, HALF:M])
         nc.sync.dma_start(out=g_rows[0:4, :].rearrange("t (x r) -> t x r", r=8), in_=g.rearrange("(x t r) -> t x r", t=4, r=8))
         nc.sync.dma_start(out=g_rows[4:6, :], in_=p[QUART : 3 * QUART].rearrange("(q m) -> q m", q=2))
         wd_win = []
         for nt in range(4):
-            win = keep.tile([P, T], F32, name="wd_win%d" % nt, align_bytes=64)
+            win = place("wd_win%d" % nt, [P, T], F32, 4 * T)
             nc.sync.dma_start(out=win[:], in_=wdT[nt * P : (nt + 1) * P, :])
             wd_win.append(win)
         p_all = {}
         for mq in (0, 3):
-            p_all[mq] = keep.tile([P, QUART], F32, name="p_all%d" % mq)
+            p_all[mq] = place("p_all%d" % mq, [P, QUART], F32, 4 * QUART)
             nc.sync.dma_start(out=p_all[mq][:], in_=p[QUART * mq : QUART * (mq + 1)].partition_broadcast(P))
 
         def gather_words(name, win, dtype):
@@ -105,59 +118,72 @@ def tile_list_routed_swiglu_expert_kernel(
             )
             return picked
 
-        gate_s = [keep.tile([P, HALF // 4], I32, name="gate_s%d" % b, align_bytes=64) for b in range(2)]
         gate_w = [[keep.tile([P, HALF], I32, name="gate_w%d%d" % (a, b), align_bytes=64) for b in range(2)] for a in range(2)]
-        for b in range(2):
-            part = offsets[:, 32 * b : 32 * (b + 1)]
-            listed = keep.tile([P, HALF], U8, name="gate_listed%d" % b, align_bytes=64)
-            nc.vector.tensor_copy(out=listed[:], in_=gate_sc[:].bitcast(U8).indirect(part))
-            for a in range(2):
-                nc.vector.tensor_copy(
-                    out=gate_w[a][b][:].bitcast(U32).rearrange("p (t q r) -> p q t r", t=4, r=8),
-                    in_=gate_win[a][:].bitcast(U32).indirect(part),
-                )
-                if a == 0:
-                    nc.vector.tensor_copy(
-                        out=gate_s[b][:].rearrange("p (t q w) -> p t q w", t=4, w=2),
-                        in_=listed[:].bitcast(I32).rearrange("p (q t w) -> p t q w", t=4, w=2),
-                    )
+
+        def gather_gate_half(a, b):
+            nc.vector.tensor_copy(
+                out=gate_w[a][b][:].bitcast(U32).rearrange("p (t q r) -> p q t r", t=4, r=8),
+                in_=gate_win[a][:].bitcast(U32).indirect(offsets[:, 32 * b : 32 * (b + 1)]),
+            )
+
+        gate_listed = gather_scales("gate_s", gate_sc)
         up_listed = gather_scales("up_s", up_sc)
-        up_w = [gather_words("up_w0", up_win[0], I32)]
+        gate_s = reorder_scales("gate_s", gate_listed)
+        gather_gate_half(0, 0)
         up_s = reorder_scales("up_s", up_listed)
-        up_w.append(gather_words("up_w1", up_win[1], I32))
+        gather_gate_half(0, 1)
+        gather_gate_half(1, 0)
+        gather_gate_half(1, 1)
+        up_w = [gather_words("up_w%d" % a, up_win[a], I32) for a in range(2)]
         wd_picked = [gather_words("wd_picked%d" % nt, wd_win[nt], F32) for nt in range(4)]
 
-        def first_product(dst, words, scales, cols, toks):
+        def list_cols(b, t):
+            return slice(2 * P * t + P * b, 2 * P * t + P * b + P)
+
+        def first_pass(dst, a, words, scales, m0, width):
+            nc.tensor.matmul_mx(
+                out=dst,
+                lhsT=words.bitcast(FP8X4),
+                lhsT_scale=scales,
+                rhs=x_w[m0 // HALF][:, a, m0 % HALF : m0 % HALF + width].bitcast(FP8X4),
+                rhs_scale=x_sc[:].bitcast(U8)[4 * a :, m0 : m0 + width],
+                start=(a == 0),
+                stop=(a == 1),
+            )
+
+        def gate_pass(dst, a, b, t, mh):
+            first_pass(
+                dst, a, gate_w[a][b][:, P * t : P * (t + 1)], gate_s[:].bitcast(U8)[4 * a :, list_cols(b, t)], HALF * mh, HALF
+            )
+
+        def up_product(dst, b, t, m0, width):
             for a in range(2):
-                nc.tensor.matmul_mx(
-                    out=dst,
-                    lhsT=words[a][:, cols].bitcast(FP8X4),
-                    lhsT_scale=scales[:].bitcast(U8)[4 * a :, cols],
-                    rhs=x_w[toks.start // HALF][:, a, toks.start % HALF : toks.start % HALF + toks.stop - toks.start].bitcast(FP8X4),
-                    rhs_scale=x_sc[:].bitcast(U8)[4 * a :, toks],
-                    start=(a == 0),
-                    stop=(a == 1),
-                )
+                first_pass(dst, a, up_w[a][:, list_cols(b, t)], up_s[:].bitcast(U8)[4 * a :, list_cols(b, t)], m0, width)
 
         act = [keep.tile([P, 4, 2, HALF], F32, name="act%d" % mh) for mh in range(2)]
         lin = [keep.tile([P, 4, 2, HALF], F32, name="lin%d" % mh) for mh in range(2)]
 
-        def gate_half(b):
-            for mh in range(2):
-                for t in range(4):
-                    bank = new_bank([P, HALF])
-                    first_product(bank[:], [gate_w[0][b], gate_w[1][b]], gate_s[b], slice(P * t, P * (t + 1)), slice(HALF * mh, HALF * (mh + 1)))
-                    nc.scalar.activation(
-                        out=act[mh][:, t, :, QUART * b : QUART * (b + 1)],
-                        in_=bank[:].rearrange("p (h m) -> p h m", h=2),
-                        func=SILU,
-                    )
+        def gate_half(mh):
+            tiles = [(b, t) for b in range(2) for t in range(4)]
+            banks = [new_bank([P, HALF]) for b, t in tiles]
+            if mh == 0:
+                for (b, t), bank in zip(tiles, banks):
+                    gate_pass(bank[:], 0, b, t, mh)
+            for (b, t), bank in zip(tiles, banks):
+                if mh == 1:
+                    gate_pass(bank[:], 0, b, t, mh)
+                gate_pass(bank[:], 1, b, t, mh)
+                nc.scalar.activation(
+                    out=act[mh][:, t, :, QUART * b : QUART * (b + 1)],
+                    in_=bank[:].rearrange("p (h m) -> p h m", h=2),
+                    func=SILU,
+                )
 
         def up_half(mh):
             for b in range(2):
                 for t in range(4):
                     bank = new_bank([P, HALF])
-                    first_product(bank[:], up_w, up_s, slice(2 * P * t + P * b, 2 * P * t + P * b + P), slice(HALF * mh, HALF * (mh + 1)))
+                    up_product(bank[:], b, t, HALF * mh, HALF)
                     nc.scalar.activation(
                         out=lin[mh][:, t, :, QUART * b : QUART * (b + 1)],
                         in_=bank[:].rearrange("p (h m) -> p h m", h=2),
@@ -169,9 +195,7 @@ def tile_list_routed_swiglu_expert_kernel(
             for t in range(4):
                 bank = new_bank([P, HALF])
                 for b in range(2):
-                    first_product(
-                        bank[:, QUART * b : QUART * (b + 1)], up_w, up_s, slice(2 * P * t + P * b, 2 * P * t + P * b + P), slice(QUART * mq, QUART * (mq + 1))
-                    )
+                    up_product(bank[:, QUART * b : QUART * (b + 1)], b, t, QUART * mq, QUART)
                 for b in range(2):
                     nc.scalar.activation(
                         out=lin[mq // 2][:, t, mq % 2, QUART * b : QUART * (b + 1)],
@@ -180,9 +204,9 @@ def tile_list_routed_swiglu_expert_kernel(
                         scale=gain[:, b, t : t + 1],
                     )
 
-        wd_bf = [keep.tile([P, 4, HALF], BF16, name="wd_bf%d" % u, align_bytes=64) for u in range(2)]
-        wd_c = [keep.tile([P, HALF], U32, name="wd_c%d" % u, align_bytes=64) for u in range(2)]
-        wd_s = [keep.tile([P, HALF], U8, name="wd_s%d" % u, align_bytes=64) for u in range(2)]
+        wd_bf = keep.tile([P, 2, 4, HALF], BF16, name="wd_bf", align_bytes=64)
+        wd_c = keep.tile([P, 2, N], U32, name="wd_c", align_bytes=64)
+        wd_s = keep.tile([P, 2, N], U8, name="wd_s", align_bytes=64)
 
         def turn_wd(nt):
             for b in range(2):
@@ -191,13 +215,15 @@ def tile_list_routed_swiglu_expert_kernel(
                     c0 = 2 * P * t + P * b
                     nc.tensor.transpose(bank[:, t, :], wd_picked[nt][:, c0 : c0 + P], ident[:])
                 nc.scalar.copy(
-                    out=wd_bf[b][:, nt, :].rearrange("p (c i t) -> p c t i", i=2, t=4),
+                    out=wd_bf[:, b, nt, :].rearrange("p (c i t) -> p c t i", i=2, t=4),
                     in_=bank[:].rearrange("p t (c i) -> p c t i", i=2),
                 )
 
-        def quantize_wd(u):
+        def quantize_wd():
             nc.vector.quantize_mx(
-                out=wd_c[u][:].bitcast(FP8X4), scales=wd_s[u][:], in_=wd_bf[u][:].rearrange("p n c -> p (n c)")
+                out=wd_c[:].rearrange("p b n -> p (b n)").bitcast(FP8X4),
+                scales=wd_s[:].rearrange("p b n -> p (b n)"),
+                in_=wd_bf[:].rearrange("p b n c -> p (b n c)"),
             )
 
         h_bf = {}
@@ -205,7 +231,7 @@ def tile_list_routed_swiglu_expert_kernel(
         h_s = [keep.tile([P, HALF], U8, name="h_s%d" % mq, align_bytes=64) for mq in range(4)]
 
         def make_h(mq):
-            h_bf[mq] = keep.tile([P, 4 * HALF], BF16, name="h_bf%d" % mq, tag="wd_win%d" % (3 - mq), align_bytes=64)
+            h_bf[mq] = wins.tile([P, 4 * HALF], BF16, name="h_bf%d" % mq, offset=placed["wd_win%d" % (3 - mq)], align_bytes=64)
             nc.vector.tensor_tensor(
                 out=h_bf[mq][:].rearrange("p (c i t) -> p c t i", i=2, t=4),
                 in0=act[mq // 2][:, :, mq % 2, :].rearrange("p t (c i) -> p c t i", i=2),
@@ -226,8 +252,8 @@ def tile_list_routed_swiglu_expert_kernel(
                         hcols = slice(QUART * b, QUART * (b + 1))
                         nc.tensor.matmul_mx(
                             out=bank[:, v, :],
-                            lhsT=wd_c[b][:, cols].bitcast(FP8X4),
-                            lhsT_scale=wd_s[b][:, cols],
+                            lhsT=wd_c[:, b, cols].bitcast(FP8X4),
+                            lhsT_scale=wd_s[:, b, cols],
                             rhs=h_c[mq][:, hcols].bitcast(FP8X4),
                             rhs_scale=h_s[mq][:, hcols],
                             start=(b == 0),
@@ -251,8 +277,8 @@ def tile_list_routed_swiglu_expert_kernel(
                         out=bank[:],
                         lhsT=h_c[mq][:, hcols].bitcast(FP8X4),
                         lhsT_scale=h_s[mq][:, hcols],
-                        rhs=wd_c[b][:].bitcast(FP8X4),
-                        rhs_scale=wd_s[b][:],
+                        rhs=wd_c[:, b, :].bitcast(FP8X4),
+                        rhs_scale=wd_s[:, b, :],
                         start=(b == 0),
                         stop=(b == 1),
                     )
@@ -291,9 +317,8 @@ def tile_list_routed_swiglu_expert_kernel(
         make_h(0)
         make_h(1)
         quantize_h(0)
-        quantize_wd(0)
+        quantize_wd()
         quantize_h(1)
-        quantize_wd(1)
         make_h(2)
         down_product(0)
         turned = down_product_turned(1)

@@ -166,11 +166,11 @@ def tile_list_routed_swiglu_expert_kernel(
         def gate_half(mh):
             tiles = [(b, t) for b in range(2) for t in range(4)]
             banks = [new_bank([P, HALF]) for b, t in tiles]
-            if mh == 0:
-                for (b, t), bank in zip(tiles, banks):
-                    gate_pass(bank[:], 0, b, t, mh)
-            for (b, t), bank in zip(tiles, banks):
-                if mh == 1:
+            early = 4 if mh == 0 else 0
+            for (b, t), bank in zip(tiles[:early], banks[:early]):
+                gate_pass(bank[:], 0, b, t, mh)
+            for i, ((b, t), bank) in enumerate(zip(tiles, banks)):
+                if i >= early:
                     gate_pass(bank[:], 0, b, t, mh)
                 gate_pass(bank[:], 1, b, t, mh)
                 nc.scalar.activation(
@@ -317,12 +317,12 @@ def tile_list_routed_swiglu_expert_kernel(
         make_h(0)
         make_h(1)
         quantize_h(0)
-        quantize_wd()
         quantize_h(1)
         make_h(2)
+        quantize_wd()
+        quantize_h(2)
         down_product(0)
         turned = down_product_turned(1)
-        quantize_h(2)
         turn_back(1, turned)
         make_h(3)
         turned = down_product_turned(2)

@@ -1,7 +1,6 @@
 from contextlib import ExitStack
 
 import concourse.mybir as mybir
-from concourse.masks import make_identity
 
 K, T, S, M, N = 1024, 2048, 1024, 1024, 512
 FLOPS = 2 * K * S * M * 2 + 2 * S * N * M
@@ -14,13 +13,17 @@ U16 = mybir.dt.uint16
 U8 = mybir.dt.uint8
 FP8X4 = mybir.dt.float8_e4m3fn_x4
 MULT = mybir.AluOpType.mult
+ADD = mybir.AluOpType.add
 SILU = mybir.ActivationFunctionType.Silu
 COPY = mybir.ActivationFunctionType.Copy
 
 P = 128
 HALF = 512
 QUART = 256
-WINS_BYTES = 8 * 4 * T + 2 * 4 * M + 3 * 4 * QUART
+PAD = 256
+FIRST_BYTES = 2 * 4 * T + 8 * HALF + M
+SECOND_BYTES = PAD + 4 * T + T
+LATE_BYTES = PAD + 5 * 4 * T + 8 * HALF
 
 
 def tile_list_routed_swiglu_expert_kernel(
@@ -39,29 +42,43 @@ def tile_list_routed_swiglu_expert_kernel(
             return psum.tile(shape, F32, name="bank%d" % (len(taken) % 8))
 
 
-        offsets = keep.tile([P, S // 16], U16, name="offsets")
-        gate_sc = keep.tile([P, T // 4], I32, name="gate_sc", align_bytes=64)
-        up_sc = keep.tile([P, T // 4], I32, name="up_sc", align_bytes=64)
-        x_sc = keep.tile([P, M // 4], I32, name="x_sc", align_bytes=64)
-        ident = keep.tile([P, P], F32, name="ident")
-        nc.vector.memset(gate_sc[:], 0)
-        nc.vector.memset(up_sc[:], 0)
-        nc.vector.memset(x_sc[:], 0)
-        warm_in = wins.tile([P, WINS_BYTES // 4], F32, name="warm_in", offset=0)
-        nc.gpsimd.memset(warm_in[:, 0:1], 0.0)
-        warm = keep.tile([P, 1], F32, name="warm")
-        nc.scalar.activation(out=warm[:], in_=warm_in[:, 0:1], func=SILU)
-        make_identity(nc, ident[:])
         placed = {}
+        sizes = []
 
         def place(name, shape, dtype, size):
             placed[name] = sum(sizes)
             sizes.append(size)
-            return wins.tile(shape, dtype, name=name, offset=placed[name])
+            return wins.tile(shape, dtype, name=name, offset=placed[name], align_bytes=64)
 
-        sizes = []
-        g_rows = place("g_rows", [P, 2 * P], F32, 8 * P)
-        nc.gpsimd.memset(g_rows[:], 0.0)
+        offsets = keep.tile([P, S // 16], U16, name="offsets")
+        ident = keep.tile([P, P], F32, name="ident")
+        gate_sc = keep.tile([P, T // 4], I32, name="gate_sc", align_bytes=64)
+        nc.gpsimd.memset(gate_sc[:], 0)
+
+        def identity_part(engine, name, c0, c1, offset, size):
+            zeros = wins.tile([P, size // 4], F32, name=name, offset=offset, align_bytes=64)
+            engine.memset(zeros[:, 0 : c1 - c0], 0.0)
+            nc.gpsimd.affine_select(
+                out=ident[:, c0:c1],
+                in_=zeros[:, 0 : c1 - c0],
+                compare_op=mybir.AluOpType.not_equal,
+                fill=1.0,
+                base=-c0,
+                pattern=[[-1, c1 - c0]],
+                channel_multiplier=1,
+            )
+
+        g_rows = keep.tile([P, 2 * P], F32, name="g_rows")
+        nc.vector.memset(g_rows[:], 0.0)
+        identity_part(nc.vector, "zeros0", 0, 32, 4 * T, FIRST_BYTES + PAD - 4 * T)
+        x_sc = wins.tile([P, M // 4], I32, name="x_sc", offset=FIRST_BYTES - M, align_bytes=64)
+        nc.gpsimd.memset(x_sc[:], 0)
+        identity_part(nc.gpsimd, "zeros1", 32, 64, FIRST_BYTES, SECOND_BYTES + PAD)
+        up_sc = wins.tile([P, T // 4], I32, name="up_sc", offset=FIRST_BYTES + SECOND_BYTES - T, align_bytes=64)
+        nc.gpsimd.memset(up_sc[:], 0)
+        identity_part(nc.gpsimd, "zeros2", 64, P, FIRST_BYTES + SECOND_BYTES, LATE_BYTES)
+        warm = keep.tile([P, 1], F32, name="warm")
+        nc.scalar.activation(out=warm[:], in_=ident[:, 0:1], func=SILU)
 
         def load_scales(queue, plane, scales):
             for q in range(4):
@@ -75,39 +92,45 @@ def tile_list_routed_swiglu_expert_kernel(
             return win
 
         nc.sync.dma_start(offsets[:], offs)
-        load_scales(nc.sync, gate_sc, tab_scales)
-        load_scales(nc.sync, up_sc, tab2_scales)
-        load_scales(nc.sync, x_sc, x_scales)
         gate_win = [load_words("gate_win0", tab_words, 0)]
-        x_all = x_words.rearrange("a p n i -> p a (n i)").bitcast(I32)
-        x_w = [place("x_w%d" % mh, [P, 2, HALF], I32, 8 * HALF) for mh in range(2)]
-        nc.sync.dma_start(out=x_w[0][:], in_=x_all[:, :, 0:HALF])
-        gate_win.append(load_words("gate_win1", tab_words, 1))
-        up_win = [load_words("up_win%d" % a, tab2_words, a) for a in range(2)]
-        nc.sync.dma_start(out=x_w[1][:], in_=x_all[:, :, HALF:M])
+        load_scales(nc.sync, gate_sc, tab_scales)
         nc.sync.dma_start(out=g_rows[0:4, :].rearrange("t (x r) -> t x r", r=8), in_=g.rearrange("(x t r) -> t x r", t=4, r=8))
-        nc.sync.dma_start(out=g_rows[4:6, :], in_=p[QUART : 3 * QUART].rearrange("(q m) -> q m", q=2))
-        wd_win = []
-        for nt in range(4):
-            win = place("wd_win%d" % nt, [P, T], F32, 4 * T)
-            nc.sync.dma_start(out=win[:], in_=wdT[nt * P : (nt + 1) * P, :])
-            wd_win.append(win)
-        p_all = {}
-        for mq in (0, 3):
-            p_all[mq] = place("p_all%d" % mq, [P, QUART], F32, 4 * QUART)
-            nc.sync.dma_start(out=p_all[mq][:], in_=p[QUART * mq : QUART * (mq + 1)].partition_broadcast(P))
+        nc.sync.dma_start(out=g_rows[4:8, :], in_=p.rearrange("(q m) -> q m", q=4))
+        gate_win.append(load_words("gate_win1", tab_words, 1))
+        x_all = x_words.rearrange("a p n i -> p a (n i)").bitcast(I32)
+        x_w = [place("x_w0", [P, 2, HALF], I32, 8 * HALF)]
+        nc.sync.dma_start(out=x_w[0][:], in_=x_all[:, :, 0:HALF])
+        load_scales(nc.sync, x_sc, x_scales)
+        sizes.append(M + PAD)
+        up_win = [load_words("up_win0", tab2_words, 0)]
+        load_scales(nc.sync, up_sc, tab2_scales)
+        sizes.append(T + PAD)
+        x_w.append(place("x_w1", [P, 2, HALF], I32, 8 * HALF))
+        nc.sync.dma_start(out=x_w[1][:], in_=x_all[:, :, HALF:M])
+        up_win.append(load_words("up_win1", tab2_words, 1))
+        wd_raw = {}
+        for u in range(2):
+            rows = wdT[2 * P * u : 2 * P * (u + 1), :].rearrange("(p i) t -> p i t", i=2)
+            for c in range(2):
+                wd_raw[u, c] = place("wd_raw%d%d" % (u, c), [P, 2, T // 2], F32, 4 * T)
+                nc.sync.dma_start(out=wd_raw[u, c][:], in_=rows[:, :, T // 2 * c : T // 2 * (c + 1)])
+
+        placed["spare"] = sum(sizes)
+        wd_pair = [
+            wins.tile([P, T, 2], BF16, name="wd_pair%d" % u, offset=placed[on], align_bytes=64)
+            for u, on in enumerate(("gate_win1", "spare"))
+        ]
 
         def gather_words(name, win, dtype):
             picked = keep.tile([P, S], dtype, name=name, align_bytes=64)
             nc.vector.tensor_copy(
                 out=picked[:].bitcast(U32).rearrange("p (t x r) -> p x t r", t=4, r=8),
-                in_=win[:].bitcast(U32).indirect(offsets[:]),
+                in_=win.bitcast(U32).indirect(offsets[:]),
             )
             return picked
 
-        def gather_scales(name, plane):
-            listed = keep.tile([P, S], U8, name=name + "_listed", align_bytes=64)
-            nc.vector.tensor_copy(out=listed[:], in_=plane[:].bitcast(U8).indirect(offsets[:]))
+        def gather_scales(listed, plane):
+            nc.vector.tensor_copy(out=listed[:], in_=plane.bitcast(U8).indirect(offsets[:]))
             return listed
 
         def reorder_scales(name, listed):
@@ -118,24 +141,30 @@ def tile_list_routed_swiglu_expert_kernel(
             )
             return picked
 
-        gate_w = [[keep.tile([P, HALF], I32, name="gate_w%d%d" % (a, b), align_bytes=64) for b in range(2)] for a in range(2)]
-
-        def gather_gate_half(a, b):
+        def gather_half(name, win, b, on=None):
+            if on is None:
+                picked = keep.tile([P, HALF], I32, name=name, align_bytes=64)
+            else:
+                picked = wins.tile([P, HALF], I32, name=name, offset=placed[on], align_bytes=64)
             nc.vector.tensor_copy(
-                out=gate_w[a][b][:].bitcast(U32).rearrange("p (t q r) -> p q t r", t=4, r=8),
-                in_=gate_win[a][:].bitcast(U32).indirect(offsets[:, 32 * b : 32 * (b + 1)]),
+                out=picked[:].bitcast(U32).rearrange("p (t q r) -> p q t r", t=4, r=8),
+                in_=win[:].bitcast(U32).indirect(offsets[:, 32 * b : 32 * (b + 1)]),
             )
+            return picked
 
-        gate_listed = gather_scales("gate_s", gate_sc)
-        up_listed = gather_scales("up_s", up_sc)
+        gate_listed = keep.tile([P, S], U8, name="gate_listed", align_bytes=64)
+        gate_w = {(0, 0): gather_half("gate_w00", gate_win[0], 0)}
+        gather_scales(gate_listed, gate_sc[:])
+        gate_w[1, 0] = gather_half("gate_w10", gate_win[1], 0)
         gate_s = reorder_scales("gate_s", gate_listed)
-        gather_gate_half(0, 0)
+        gate_w[1, 1] = gather_half("gate_w11", gate_win[1], 1, "spare")
+        gate_w[0, 1] = gather_half("gate_w01", gate_win[0], 1, "gate_win1")
+        up_w = {(0, b): gather_half("up_w0%d" % b, up_win[0], b) for b in range(2)}
+        up_listed = wins.tile([P, S], U8, name="up_listed", offset=placed["up_win0"], align_bytes=64)
+        gather_scales(up_listed, up_sc[:])
+        up_w[1, 0] = gather_half("up_w10", up_win[1], 0)
         up_s = reorder_scales("up_s", up_listed)
-        gather_gate_half(0, 1)
-        gather_gate_half(1, 0)
-        gather_gate_half(1, 1)
-        up_w = [gather_words("up_w%d" % a, up_win[a], I32) for a in range(2)]
-        wd_picked = [gather_words("wd_picked%d" % nt, wd_win[nt], F32) for nt in range(4)]
+        up_w[1, 1] = gather_half("up_w11", up_win[1], 1)
 
         def list_cols(b, t):
             return slice(2 * P * t + P * b, 2 * P * t + P * b + P)
@@ -151,181 +180,148 @@ def tile_list_routed_swiglu_expert_kernel(
                 stop=(a == 1),
             )
 
-        def gate_pass(dst, a, b, t, mh):
-            first_pass(
-                dst, a, gate_w[a][b][:, P * t : P * (t + 1)], gate_s[:].bitcast(U8)[4 * a :, list_cols(b, t)], HALF * mh, HALF
-            )
+        act = {(mh, b): keep.tile([P, 4, HALF], F32, name="act%d%d" % (mh, b)) for mh in range(2) for b in range(2)}
 
-        def up_product(dst, b, t, m0, width):
-            for a in range(2):
-                first_pass(dst, a, up_w[a][:, list_cols(b, t)], up_s[:].bitcast(U8)[4 * a :, list_cols(b, t)], m0, width)
-
-        act = [keep.tile([P, 4, 2, HALF], F32, name="act%d" % mh) for mh in range(2)]
-        lin = [keep.tile([P, 4, 2, HALF], F32, name="lin%d" % mh) for mh in range(2)]
-
-        def gate_half(mh):
-            tiles = [(b, t) for b in range(2) for t in range(4)]
-            banks = [new_bank([P, HALF]) for b, t in tiles]
-            early = 4 if mh == 0 else 0
-            for (b, t), bank in zip(tiles[:early], banks[:early]):
-                gate_pass(bank[:], 0, b, t, mh)
-            for i, ((b, t), bank) in enumerate(zip(tiles, banks)):
-                if i >= early:
-                    gate_pass(bank[:], 0, b, t, mh)
-                gate_pass(bank[:], 1, b, t, mh)
-                nc.scalar.activation(
-                    out=act[mh][:, t, :, QUART * b : QUART * (b + 1)],
-                    in_=bank[:].rearrange("p (h m) -> p h m", h=2),
-                    func=SILU,
-                )
-
-        def up_half(mh):
-            for b in range(2):
-                for t in range(4):
-                    bank = new_bank([P, HALF])
-                    up_product(bank[:], b, t, HALF * mh, HALF)
-                    nc.scalar.activation(
-                        out=lin[mh][:, t, :, QUART * b : QUART * (b + 1)],
-                        in_=bank[:].rearrange("p (h m) -> p h m", h=2),
-                        func=COPY,
-                        scale=gain[:, b, t : t + 1],
-                    )
-
-        def up_quarter(mq):
+        def gate_part(mh, b):
             for t in range(4):
                 bank = new_bank([P, HALF])
-                for b in range(2):
-                    up_product(bank[:, QUART * b : QUART * (b + 1)], b, t, QUART * mq, QUART)
-                for b in range(2):
-                    nc.scalar.activation(
-                        out=lin[mq // 2][:, t, mq % 2, QUART * b : QUART * (b + 1)],
-                        in_=bank[:, QUART * b : QUART * (b + 1)],
-                        func=COPY,
-                        scale=gain[:, b, t : t + 1],
+                for a in range(2):
+                    first_pass(
+                        bank[:], a, gate_w[a, b][:, P * t : P * (t + 1)], gate_s[:].bitcast(U8)[4 * a :, list_cols(b, t)], HALF * mh, HALF
                     )
+                nc.scalar.activation(out=act[mh, b][:, t, :], in_=bank[:], func=SILU)
 
-        wd_bf = keep.tile([P, 2, 4, HALF], BF16, name="wd_bf", align_bytes=64)
-        wd_c = keep.tile([P, 2, N], U32, name="wd_c", align_bytes=64)
-        wd_s = keep.tile([P, 2, N], U8, name="wd_s", align_bytes=64)
+        def gain_part(mh, b):
+            for t in range(4):
+                nc.gpsimd.tensor_scalar(
+                    out=act[mh, b][:, t, :], in0=act[mh, b][:, t, :], scalar1=gain[:, b, t : t + 1], scalar2=0.0, op0=MULT, op1=ADD
+                )
 
-        def turn_wd(nt):
+        h_bf = {}
+        h_c = {key: keep.tile([P, HALF], U32, name="h_c%d%d" % key, align_bytes=64) for key in act}
+        h_s = {key: keep.tile([P, HALF], U8, name="h_s%d%d" % key, align_bytes=64) for key in act}
+
+        def up_part(mh, b, k):
+            banks = []
+            for mc in range(2 * k, 2 * k + 2):
+                bank = new_bank([P, 4, P])
+                for t in range(4):
+                    for a in range(2):
+                        first_pass(
+                            bank[:, t, :],
+                            a,
+                            up_w[a, b][:, P * t : P * (t + 1)],
+                            up_s[:].bitcast(U8)[4 * a :, list_cols(b, t)],
+                            HALF * mh + P * mc,
+                            P,
+                        )
+                banks.append(bank)
+            return banks
+
+        def make_h(mh, b, k, banks, on):
+            h_bf[mh, b, k] = wins.tile([P, 2, 4 * P], BF16, name="h_bf%d%d%d" % (mh, b, k), offset=on, align_bytes=64)
+            for mc in range(2 * k, 2 * k + 2):
+                nc.vector.tensor_tensor(
+                    out=h_bf[mh, b, k][:, mc % 2, :].rearrange("p (c i t) -> p c t i", i=2, t=4),
+                    in0=banks[mc % 2][:].rearrange("p t (c i) -> p c t i", i=2),
+                    in1=act[mh, b][:, :, P * mc : P * (mc + 1)].rearrange("p t (c i) -> p c t i", i=2),
+                    op=MULT,
+                )
+
+        def quantize_h(mh, b, k):
+            cols = slice(QUART * k, QUART * (k + 1))
+            nc.vector.quantize_mx(
+                out=h_c[mh, b][:, cols].bitcast(FP8X4), scales=h_s[mh, b][:, cols], in_=h_bf[mh, b, k][:].rearrange("p c w -> p (c w)")
+            )
+
+        def cast_wd(u, c):
+            nc.scalar.copy(
+                out=wd_pair[u][:, T // 2 * c : T // 2 * (c + 1), :], in_=wd_raw[u, c][:].rearrange("p i t -> p t i")
+            )
+
+        wd_bf = [keep.tile([P, 2, 8 * P], BF16, name="wd_bf%d" % u, align_bytes=64) for u in range(2)]
+        wd_c = [keep.tile([P, 2, 2 * P], U32, name="wd_c%d" % u, align_bytes=64) for u in range(2)]
+        wd_s = [keep.tile([P, 2, 2 * P], U8, name="wd_s%d" % u, align_bytes=64) for u in range(2)]
+
+        def turn_wd(u):
+            picked = gather_words("wd_picked%d" % u, wd_pair[u][:].rearrange("p t i -> p (t i)"), F32)
             for b in range(2):
                 bank = new_bank([P, 4, P])
                 for t in range(4):
-                    c0 = 2 * P * t + P * b
-                    nc.tensor.transpose(bank[:, t, :], wd_picked[nt][:, c0 : c0 + P], ident[:])
+                    nc.tensor.transpose(bank[:, t, :], picked[:, list_cols(b, t)], ident[:])
                 nc.scalar.copy(
-                    out=wd_bf[:, b, nt, :].rearrange("p (c i t) -> p c t i", i=2, t=4),
-                    in_=bank[:].rearrange("p t (c i) -> p c t i", i=2),
+                    out=wd_bf[u][:, b, :].rearrange("p (c i t) -> p c t i", i=4, t=4),
+                    in_=bank[:].bitcast(BF16).rearrange("p t (c i) -> p c t i", i=4),
                 )
 
-        def quantize_wd():
+        def quantize_wd(u):
             nc.vector.quantize_mx(
-                out=wd_c[:].rearrange("p b n -> p (b n)").bitcast(FP8X4),
-                scales=wd_s[:].rearrange("p b n -> p (b n)"),
-                in_=wd_bf[:].rearrange("p b n c -> p (b n c)"),
+                out=wd_c[u][:].rearrange("p b n -> p (b n)").bitcast(FP8X4),
+                scales=wd_s[u][:].rearrange("p b n -> p (b n)"),
+                in_=wd_bf[u][:].rearrange("p b c -> p (b c)"),
             )
 
-        h_bf = {}
-        h_c = [keep.tile([P, HALF], U32, name="h_c%d" % mq, align_bytes=64) for mq in range(4)]
-        h_s = [keep.tile([P, HALF], U8, name="h_s%d" % mq, align_bytes=64) for mq in range(4)]
-
-        def make_h(mq):
-            h_bf[mq] = wins.tile([P, 4 * HALF], BF16, name="h_bf%d" % mq, offset=placed["wd_win%d" % (3 - mq)], align_bytes=64)
-            nc.vector.tensor_tensor(
-                out=h_bf[mq][:].rearrange("p (c i t) -> p c t i", i=2, t=4),
-                in0=act[mq // 2][:, :, mq % 2, :].rearrange("p t (c i) -> p c t i", i=2),
-                in1=lin[mq // 2][:, :, mq % 2, :].rearrange("p t (c i) -> p c t i", i=2),
-                op=MULT,
-            )
-
-        def quantize_h(mq):
-            nc.vector.quantize_mx(out=h_c[mq][:].bitcast(FP8X4), scales=h_s[mq][:], in_=h_bf[mq][:])
-
-        def down_product(mq):
-            toks = slice(QUART * mq, QUART * (mq + 1))
-            for u in range(2):
-                bank = new_bank([P, 2, QUART])
-                for v in range(2):
-                    for b in range(2):
-                        cols = slice(2 * P * u + P * v, 2 * P * u + P * v + P)
-                        hcols = slice(QUART * b, QUART * (b + 1))
-                        nc.tensor.matmul_mx(
-                            out=bank[:, v, :],
-                            lhsT=wd_c[:, b, cols].bitcast(FP8X4),
-                            lhsT_scale=wd_s[:, b, cols],
-                            rhs=h_c[mq][:, hcols].bitcast(FP8X4),
-                            rhs_scale=h_s[mq][:, hcols],
-                            start=(b == 0),
-                            stop=(b == 1),
-                        )
-                y = ring.tile([P, 2, QUART], F32, name="y", bufs=4)
-                nc.vector.tensor_tensor(
-                    out=y[:], in0=bank[:], in1=p_all[mq][:].unsqueeze(1).to_broadcast([P, 2, QUART]), op=MULT
-                )
-                nc.sync.dma_start(
-                    out=out[2 * P * u : 2 * P * (u + 1), toks].rearrange("(v p) m -> p v m", v=2), in_=y[:]
-                )
-
-        def down_product_turned(mq):
-            scaled_tiles = []
-            for mt in range(2):
+        def down_product(mh, u):
+            for v in range(2):
                 bank = new_bank([P, HALF])
                 for b in range(2):
-                    hcols = slice(QUART * b + P * mt, QUART * b + P * (mt + 1))
                     nc.tensor.matmul_mx(
                         out=bank[:],
-                        lhsT=h_c[mq][:, hcols].bitcast(FP8X4),
-                        lhsT_scale=h_s[mq][:, hcols],
-                        rhs=wd_c[:, b, :].bitcast(FP8X4),
-                        rhs_scale=wd_s[:, b, :],
+                        lhsT=wd_c[u][:, b, P * v : P * (v + 1)].bitcast(FP8X4),
+                        lhsT_scale=wd_s[u][:, b, P * v : P * (v + 1)],
+                        rhs=h_c[mh, b][:].bitcast(FP8X4),
+                        rhs_scale=h_s[mh, b][:],
                         start=(b == 0),
                         stop=(b == 1),
                     )
-                scaled = ring.tile([P, N], F32, name="scaled", bufs=4)
-                nc.scalar.activation(out=scaled[:], in_=bank[:], func=COPY, scale=gain[:, mt, 3 + mq : 4 + mq])
-                scaled_tiles.append(scaled)
-            return scaled_tiles
+                y = ring.tile([P, HALF], F32, name="y", bufs=8)
+                nc.vector.tensor_tensor(out=y[:], in0=bank[:], in1=p_all[mh][:], op=MULT)
+                row = P * (2 * u + v)
+                nc.sync.dma_start(out=out[row : row + P, HALF * mh : HALF * (mh + 1)], in_=y[:])
 
-        def turn_back(mq, scaled_tiles):
-            y = ring.tile([P, 4, QUART], F32, name="y_turned", bufs=2)
-            for mt in range(2):
-                scaled = scaled_tiles[mt]
-                back = new_bank([P, 4, P])
-                for nt in range(4):
-                    nc.tensor.transpose(back[:, nt, :], scaled[:, P * nt : P * (nt + 1)], ident[:])
-                nc.scalar.copy(out=y[:, :, P * mt : P * (mt + 1)], in_=back[:])
-            nc.sync.dma_start(
-                out=out[:, QUART * mq : QUART * (mq + 1)].rearrange("(v p) m -> p v m", v=4), in_=y[:]
-            )
-
-        gate_half(0)
-        gate_half(1)
         g_ps = new_bank([P, 4, P])
         for b in range(2):
             nc.tensor.transpose(g_ps[:, b, :], g_rows[:, b * P : (b + 1) * P], ident[:])
-        gain = keep.tile([P, 2, 6], F32, name="gain")
-        nc.scalar.copy(out=gain[:], in_=g_ps[:, 0:2, 0:6])
+        gain = keep.tile([P, 2, 8], F32, name="gain")
+        nc.scalar.copy(out=gain[:], in_=g_ps[:, 0:2, 0:8])
+        p_all = []
+        for mh in range(2):
+            bank = new_bank([P, 4, P])
+            for mc in range(4):
+                col = 4 + 2 * mh + mc // 2
+                nc.tensor.transpose(bank[:, mc, :], gain[:, mc % 2, col : col + 1].to_broadcast([P, P]), ident[:])
+            p_all.append(keep.tile([P, HALF], F32, name="p_all%d" % mh))
+            nc.scalar.copy(out=p_all[mh][:], in_=bank[:].rearrange("p c m -> p (c m)"))
 
-        up_half(0)
+        for mh in range(2):
+            for b in range(2):
+                gate_part(mh, b)
+                gain_part(mh, b)
+        for u in range(2):
+            for c in range(2):
+                cast_wd(u, c)
+        free = placed["gate_win0"]
+        for b in range(2):
+            for k in range(2):
+                make_h(0, b, k, up_part(0, b, k), free + 2048 * (2 * b + k))
+        for b in range(2):
+            for k in range(2):
+                quantize_h(0, b, k)
+        banks = {k: up_part(1, 0, k) for k in range(2)}
         turn_wd(0)
+        make_h(1, 0, 0, banks[0], placed["gate_win1"])
+        later = up_part(1, 1, 0)
         turn_wd(1)
-        up_quarter(2)
-        turn_wd(2)
-        turn_wd(3)
-        up_quarter(3)
-        make_h(0)
-        make_h(1)
-        quantize_h(0)
-        quantize_h(1)
-        make_h(2)
-        quantize_wd()
-        quantize_h(2)
-        down_product(0)
-        turned = down_product_turned(1)
-        turn_back(1, turned)
-        make_h(3)
-        turned = down_product_turned(2)
-        quantize_h(3)
-        down_product(3)
-        turn_back(2, turned)
+        make_h(1, 0, 1, banks[1], placed["spare"])
+        quantize_h(1, 0, 0)
+        make_h(1, 1, 0, later, placed["spare"] + 2048)
+        quantize_h(1, 0, 1)
+        quantize_wd(0)
+        make_h(1, 1, 1, up_part(1, 1, 1), placed["spare"] + 4096)
+        quantize_h(1, 1, 0)
+        quantize_h(1, 1, 1)
+        down_product(0, 0)
+        quantize_wd(1)
+        down_product(1, 0)
+        down_product(0, 1)
+        down_product(1, 1)

@@ -77,8 +77,6 @@ def tile_list_routed_swiglu_expert_kernel(
         up_sc = wins.tile([P, T // 4], I32, name="up_sc", offset=FIRST_BYTES + SECOND_BYTES - T, align_bytes=64)
         nc.gpsimd.memset(up_sc[:], 0)
         identity_part(nc.gpsimd, "zeros2", 64, P, FIRST_BYTES + SECOND_BYTES, LATE_BYTES)
-        warm = keep.tile([P, 1], F32, name="warm")
-        nc.scalar.activation(out=warm[:], in_=ident[:, 0:1], func=SILU)
 
         def load_scales(queue, plane, scales):
             for q in range(4):
@@ -283,16 +281,7 @@ def tile_list_routed_swiglu_expert_kernel(
         for b in range(2):
             nc.tensor.transpose(g_ps[:, b, :], g_rows[:, b * P : (b + 1) * P], ident[:])
         gain = keep.tile([P, 2, 8], F32, name="gain")
-        nc.scalar.copy(out=gain[:], in_=g_ps[:, 0:2, 0:8])
-        p_all = []
-        for mh in range(2):
-            bank = new_bank([P, 4, P])
-            for mc in range(4):
-                col = 4 + 2 * mh + mc // 2
-                nc.tensor.transpose(bank[:, mc, :], gain[:, mc % 2, col : col + 1].to_broadcast([P, P]), ident[:])
-            p_all.append(keep.tile([P, HALF], F32, name="p_all%d" % mh))
-            nc.scalar.copy(out=p_all[mh][:], in_=bank[:].rearrange("p c m -> p (c m)"))
-
+        nc.vector.tensor_copy(out=gain[:], in_=g_ps[:, 0:2, 0:8])
         for mh in range(2):
             for b in range(2):
                 gate_part(mh, b)
@@ -317,7 +306,17 @@ def tile_list_routed_swiglu_expert_kernel(
         make_h(1, 1, 0, later, placed["spare"] + 2048)
         quantize_h(1, 0, 1)
         quantize_wd(0)
-        make_h(1, 1, 1, up_part(1, 1, 1), placed["spare"] + 4096)
+        last = up_part(1, 1, 1)
+        p_all = []
+        for mh in range(2):
+            bank = new_bank([P, 4, P])
+            for mc in range(4):
+                col = 4 + 2 * mh + mc // 2
+                nc.tensor.transpose(bank[:, mc, :], gain[:, mc % 2, col : col + 1].to_broadcast([P, P]), ident[:])
+            p_all.append(keep.tile([P, HALF], F32, name="p_all%d" % mh))
+            nc.scalar.copy(out=p_all[mh][:], in_=bank[:].rearrange("p c m -> p (c m)"))
+
+        make_h(1, 1, 1, last, placed["spare"] + 4096)
         quantize_h(1, 1, 0)
         quantize_h(1, 1, 1)
         down_product(0, 0)

@@ -15,15 +15,13 @@ FP8X4 = mybir.dt.float8_e4m3fn_x4
 MULT = mybir.AluOpType.mult
 ADD = mybir.AluOpType.add
 SILU = mybir.ActivationFunctionType.Silu
-COPY = mybir.ActivationFunctionType.Copy
 
 P = 128
 HALF = 512
-QUART = 256
 PAD = 256
-FIRST_BYTES = 2 * 4 * T + 8 * HALF + M
+FIRST_BYTES = 4 * T + 8 * HALF + 2 * M
 SECOND_BYTES = PAD + 4 * T + T
-LATE_BYTES = PAD + 5 * 4 * T + 8 * HALF
+LATE_BYTES = PAD + 6 * 4 * T + 8 * HALF + 4 * M
 
 
 def tile_list_routed_swiglu_expert_kernel(
@@ -33,31 +31,28 @@ def tile_list_routed_swiglu_expert_kernel(
     with ExitStack() as ctx:
         keep = ctx.enter_context(tc.tile_pool(name="keep", bufs=1))
         wins = ctx.enter_context(tc.tile_pool(name="wins", bufs=1))
-        ring = ctx.enter_context(tc.tile_pool(name="ring", bufs=3))
         psum = ctx.enter_context(tc.psum_pool(name="psum", bufs=1))
-        taken = []
 
-        def new_bank(shape):
-            taken.append(shape)
-            return psum.tile(shape, F32, name="bank%d" % (len(taken) % 8))
+        def bank(i, shape):
+            return psum.tile(shape, F32, name="bank%d" % i)
 
-
-        placed = {}
         sizes = []
 
         def place(name, shape, dtype, size):
-            placed[name] = sum(sizes)
+            at = sum(sizes)
             sizes.append(size)
-            return wins.tile(shape, dtype, name=name, offset=placed[name], align_bytes=64)
+            return wins.tile(shape, dtype, name=name, offset=at, align_bytes=64)
 
         offsets = keep.tile([P, S // 16], U16, name="offsets")
         ident = keep.tile([P, P], F32, name="ident")
         gate_sc = keep.tile([P, T // 4], I32, name="gate_sc", align_bytes=64)
         nc.gpsimd.memset(gate_sc[:], 0)
+        g_rows = keep.tile([P, 2 * P], F32, name="g_rows")
+        nc.vector.memset(g_rows[:], 0.0)
 
-        def identity_part(engine, name, c0, c1, offset, size):
+        def identity_part(name, c0, c1, offset, size):
             zeros = wins.tile([P, size // 4], F32, name=name, offset=offset, align_bytes=64)
-            engine.memset(zeros[:, 0 : c1 - c0], 0.0)
+            nc.gpsimd.memset(zeros[:, 0 : c1 - c0], 0.0)
             nc.gpsimd.affine_select(
                 out=ident[:, c0:c1],
                 in_=zeros[:, 0 : c1 - c0],
@@ -68,43 +63,46 @@ def tile_list_routed_swiglu_expert_kernel(
                 channel_multiplier=1,
             )
 
-        g_rows = keep.tile([P, 2 * P], F32, name="g_rows")
-        nc.vector.memset(g_rows[:], 0.0)
-        identity_part(nc.vector, "zeros0", 0, 32, 4 * T, FIRST_BYTES + PAD - 4 * T)
-        x_sc = wins.tile([P, M // 4], I32, name="x_sc", offset=FIRST_BYTES - M, align_bytes=64)
+        identity_part("zeros0", 0, 32, 0, FIRST_BYTES + PAD)
+        x_sc = wins.tile([P, 2, M // 4], I32, name="x_sc", offset=FIRST_BYTES - 2 * M, align_bytes=64)
         nc.gpsimd.memset(x_sc[:], 0)
-        identity_part(nc.gpsimd, "zeros1", 32, 64, FIRST_BYTES, SECOND_BYTES + PAD)
+        identity_part("zeros1", 32, 64, FIRST_BYTES, SECOND_BYTES + PAD)
         up_sc = wins.tile([P, T // 4], I32, name="up_sc", offset=FIRST_BYTES + SECOND_BYTES - T, align_bytes=64)
         nc.gpsimd.memset(up_sc[:], 0)
-        identity_part(nc.gpsimd, "zeros2", 64, P, FIRST_BYTES + SECOND_BYTES, LATE_BYTES)
+        identity_part("zeros2", 64, P, FIRST_BYTES + SECOND_BYTES, LATE_BYTES)
 
-        def load_scales(queue, plane, scales):
+        def load_scales(plane, scales):
             for q in range(4):
-                queue.dma_start(
-                    out=plane[32 * q : 32 * q + 8, :], in_=scales[:, 4 * q : 4 * q + 4, :].bitcast(I32)
-                )
+                nc.sync.dma_start(out=plane[32 * q : 32 * q + 8, :], in_=scales[:, 4 * q : 4 * q + 4, :].bitcast(I32))
 
         def load_words(name, words, a):
             win = place(name, [P, T], I32, 4 * T)
             nc.sync.dma_start(out=win[:], in_=words[a].rearrange("p n i -> p (n i)").bitcast(I32))
             return win
 
-        nc.sync.dma_start(offsets[:], offs)
-        gate_win = [load_words("gate_win0", tab_words, 0)]
-        load_scales(nc.sync, gate_sc, tab_scales)
-        nc.sync.dma_start(out=g_rows[0:4, :].rearrange("t (x r) -> t x r", r=8), in_=g.rearrange("(x t r) -> t x r", t=4, r=8))
-        nc.sync.dma_start(out=g_rows[4:8, :], in_=p.rearrange("(q m) -> q m", q=4))
-        gate_win.append(load_words("gate_win1", tab_words, 1))
         x_all = x_words.rearrange("a p n i -> p a (n i)").bitcast(I32)
-        x_w = [place("x_w0", [P, 2, HALF], I32, 8 * HALF)]
-        nc.sync.dma_start(out=x_w[0][:], in_=x_all[:, :, 0:HALF])
-        load_scales(nc.sync, x_sc, x_scales)
-        sizes.append(M + PAD)
-        up_win = [load_words("up_win0", tab2_words, 0)]
-        load_scales(nc.sync, up_sc, tab2_scales)
+
+        def load_x(mh):
+            half = place("x_w%d" % mh, [P, 2, HALF], I32, 8 * HALF)
+            nc.sync.dma_start(out=half[:], in_=x_all[:, :, HALF * mh : HALF * (mh + 1)])
+            return half
+
+        nc.sync.dma_start(offsets[:], offs)
+        load_scales(gate_sc, tab_scales)
+        nc.sync.dma_start(out=g_rows[0:4, :].rearrange("t (x r) -> t x r", r=8), in_=g.rearrange("(x t r) -> t x r", t=4, r=8))
+        gate_win = [load_words("gate_win0", tab_words, 0)]
+        x_w = [load_x(0)]
+        for q in range(4):
+            nc.sync.dma_start(
+                out=x_sc[32 * q : 32 * q + 4, :, :],
+                in_=x_scales[:, 4 * q : 4 * q + 4, :].rearrange("a r c -> r a c").bitcast(I32),
+            )
+        sizes.append(2 * M + PAD)
+        gate_win.append(load_words("gate_win1", tab_words, 1))
+        load_scales(up_sc, tab2_scales)
         sizes.append(T + PAD)
-        x_w.append(place("x_w1", [P, 2, HALF], I32, 8 * HALF))
-        nc.sync.dma_start(out=x_w[1][:], in_=x_all[:, :, HALF:M])
+        up_win = [load_words("up_win0", tab2_words, 0)]
+        x_w.append(load_x(1))
         up_win.append(load_words("up_win1", tab2_words, 1))
         wd_raw = {}
         for u in range(2):
@@ -112,144 +110,129 @@ def tile_list_routed_swiglu_expert_kernel(
             for c in range(2):
                 wd_raw[u, c] = place("wd_raw%d%d" % (u, c), [P, 2, T // 2], F32, 4 * T)
                 nc.sync.dma_start(out=wd_raw[u, c][:], in_=rows[:, :, T // 2 * c : T // 2 * (c + 1)])
+        p_all = place("p_all", [P, M], F32, 4 * M)
+        nc.sync.dma_start(out=p_all[:], in_=p.partition_broadcast(P))
 
-        placed["spare"] = sum(sizes)
-        wd_pair = [
-            wins.tile([P, T, 2], BF16, name="wd_pair%d" % u, offset=placed[on], align_bytes=64)
-            for u, on in enumerate(("gate_win1", "spare"))
-        ]
-
-        def gather_words(name, win, dtype):
-            picked = keep.tile([P, S], dtype, name=name, align_bytes=64)
-            nc.vector.tensor_copy(
-                out=picked[:].bitcast(U32).rearrange("p (t x r) -> p x t r", t=4, r=8),
-                in_=win.bitcast(U32).indirect(offsets[:]),
-            )
-            return picked
-
-        def gather_scales(listed, plane):
-            nc.vector.tensor_copy(out=listed[:], in_=plane.bitcast(U8).indirect(offsets[:]))
+        def pick_scales(name, plane):
+            listed = keep.tile([P, S], U8, name=name + "_listed", align_bytes=64)
+            nc.vector.tensor_copy(out=listed[:], in_=plane[:].bitcast(U8).indirect(offsets[:]))
             return listed
 
-        def reorder_scales(name, listed):
+        def order_scales(name, listed):
             picked = keep.tile([P, S // 4], I32, name=name, align_bytes=64)
             nc.vector.tensor_copy(
-                out=picked[:].rearrange("p (t x w) -> p t x w", t=4, w=2),
-                in_=listed[:].bitcast(I32).rearrange("p (x t w) -> p t x w", t=4, w=2),
+                out=picked[:].rearrange("p (b t q w) -> p b t q w", b=2, t=4, w=2),
+                in_=listed[:].bitcast(I32).rearrange("p (b q t w) -> p b t q w", b=2, t=4, w=2),
             )
-            return picked
+            return [picked[:, P * b : P * (b + 1)] for b in range(2)]
 
-        def gather_half(name, win, b, on=None):
-            if on is None:
-                picked = keep.tile([P, HALF], I32, name=name, align_bytes=64)
-            else:
-                picked = wins.tile([P, HALF], I32, name=name, offset=placed[on], align_bytes=64)
+        def order_half(listed, b, picked):
+            nc.vector.tensor_copy(
+                out=picked[:].rearrange("p (t q w) -> p t q w", t=4, w=2),
+                in_=listed[:, HALF * b : HALF * (b + 1)].bitcast(I32).rearrange("p (q t w) -> p t q w", t=4, w=2),
+            )
+            return picked[:]
+
+        def pick_half(name, win, b, dtype):
+            picked = keep.tile([P, HALF], dtype, name=name, align_bytes=64)
             nc.vector.tensor_copy(
                 out=picked[:].bitcast(U32).rearrange("p (t q r) -> p q t r", t=4, r=8),
-                in_=win[:].bitcast(U32).indirect(offsets[:, 32 * b : 32 * (b + 1)]),
+                in_=win.bitcast(U32).indirect(offsets[:, 32 * b : 32 * (b + 1)]),
             )
-            return picked
+            return picked[:]
 
-        gate_listed = keep.tile([P, S], U8, name="gate_listed", align_bytes=64)
-        gate_w = {(0, 0): gather_half("gate_w00", gate_win[0], 0)}
-        gather_scales(gate_listed, gate_sc[:])
-        gate_w[1, 0] = gather_half("gate_w10", gate_win[1], 0)
-        gate_s = reorder_scales("gate_s", gate_listed)
-        gate_w[1, 1] = gather_half("gate_w11", gate_win[1], 1, "spare")
-        gate_w[0, 1] = gather_half("gate_w01", gate_win[0], 1, "gate_win1")
-        up_w = {(0, b): gather_half("up_w0%d" % b, up_win[0], b) for b in range(2)}
-        up_listed = wins.tile([P, S], U8, name="up_listed", offset=placed["up_win0"], align_bytes=64)
-        gather_scales(up_listed, up_sc[:])
-        up_w[1, 0] = gather_half("up_w10", up_win[1], 0)
-        up_s = reorder_scales("up_s", up_listed)
-        up_w[1, 1] = gather_half("up_w11", up_win[1], 1)
+        def pick_all(name, win, dtype):
+            picked = keep.tile([P, 2, HALF], dtype, name=name, align_bytes=64)
+            nc.vector.tensor_copy(
+                out=picked[:].bitcast(U32).rearrange("p b (t q r) -> p b q t r", t=4, r=8),
+                in_=win.bitcast(U32).indirect(offsets[:]),
+            )
+            return [picked[:, b, :] for b in range(2)]
 
-        def list_cols(b, t):
-            return slice(2 * P * t + P * b, 2 * P * t + P * b + P)
+        gate_listed = pick_scales("gate_s", gate_sc)
+        gate_s = [order_half(gate_listed, 0, keep.tile([P, P], I32, name="gate_s0", align_bytes=64))]
+        gate_w = {(a, b): pick_half("gate_w%d%d" % (a, b), gate_win[a][:], b, I32) for a in range(2) for b in range(2)}
+        on_second_window = FIRST_BYTES + PAD
+        gate_s.append(order_half(gate_listed, 1, wins.tile([P, P], I32, name="gate_s1", offset=on_second_window, align_bytes=64)))
+        up_listed = pick_scales("up_s", up_sc)
+        up_w = {(0, b): half for b, half in enumerate(pick_all("up_w0", up_win[0][:], I32))}
+        up_s = order_scales("up_s", up_listed)
+        for b in range(2):
+            up_w[1, b] = pick_half("up_w1%d" % b, up_win[1][:], b, I32)
 
-        def first_pass(dst, a, words, scales, m0, width):
+        def first_pass(dst, a, words, scales, b, t, m0, width):
             nc.tensor.matmul_mx(
                 out=dst,
-                lhsT=words.bitcast(FP8X4),
-                lhsT_scale=scales,
+                lhsT=words[a, b][:, P * t : P * (t + 1)].bitcast(FP8X4),
+                lhsT_scale=scales[b].bitcast(U8)[4 * a :, P * t : P * (t + 1)],
                 rhs=x_w[m0 // HALF][:, a, m0 % HALF : m0 % HALF + width].bitcast(FP8X4),
-                rhs_scale=x_sc[:].bitcast(U8)[4 * a :, m0 : m0 + width],
+                rhs_scale=x_sc[:, a, :].bitcast(U8)[:, m0 : m0 + width],
                 start=(a == 0),
                 stop=(a == 1),
             )
 
-        act = {(mh, b): keep.tile([P, 4, HALF], F32, name="act%d%d" % (mh, b)) for mh in range(2) for b in range(2)}
+        quarters = [(mh, b) for mh in range(2) for b in range(2)]
+        act = {key: keep.tile([P, 4, HALF], F32, name="act%d%d" % key) for key in quarters}
+        h_bf = {key: keep.tile([P, 4, 4 * P], BF16, name="h_bf%d%d" % key, align_bytes=64) for key in quarters}
+        h_c = {key: keep.tile([P, HALF], U32, name="h_c%d%d" % key, align_bytes=64) for key in quarters}
+        h_s = {key: keep.tile([P, HALF], U8, name="h_s%d%d" % key, align_bytes=64) for key in quarters}
 
-        def gate_part(mh, b):
-            for t in range(4):
-                bank = new_bank([P, HALF])
-                for a in range(2):
-                    first_pass(
-                        bank[:], a, gate_w[a, b][:, P * t : P * (t + 1)], gate_s[:].bitcast(U8)[4 * a :, list_cols(b, t)], HALF * mh, HALF
-                    )
-                nc.scalar.activation(out=act[mh, b][:, t, :], in_=bank[:], func=SILU)
+        def activate(mh, b, t, sums):
+            nc.scalar.activation(out=act[mh, b][:, t, :], in_=sums[:], func=SILU)
+            apply_gain(mh, b, t)
 
-        def gain_part(mh, b):
-            for t in range(4):
-                nc.gpsimd.tensor_scalar(
-                    out=act[mh, b][:, t, :], in0=act[mh, b][:, t, :], scalar1=gain[:, b, t : t + 1], scalar2=0.0, op0=MULT, op1=ADD
-                )
-
-        h_bf = {}
-        h_c = {key: keep.tile([P, HALF], U32, name="h_c%d%d" % key, align_bytes=64) for key in act}
-        h_s = {key: keep.tile([P, HALF], U8, name="h_s%d%d" % key, align_bytes=64) for key in act}
-
-        def up_part(mh, b, k):
-            banks = []
-            for mc in range(2 * k, 2 * k + 2):
-                bank = new_bank([P, 4, P])
-                for t in range(4):
-                    for a in range(2):
-                        first_pass(
-                            bank[:, t, :],
-                            a,
-                            up_w[a, b][:, P * t : P * (t + 1)],
-                            up_s[:].bitcast(U8)[4 * a :, list_cols(b, t)],
-                            HALF * mh + P * mc,
-                            P,
-                        )
-                banks.append(bank)
-            return banks
-
-        def make_h(mh, b, k, banks, on):
-            h_bf[mh, b, k] = wins.tile([P, 2, 4 * P], BF16, name="h_bf%d%d%d" % (mh, b, k), offset=on, align_bytes=64)
-            for mc in range(2 * k, 2 * k + 2):
-                nc.vector.tensor_tensor(
-                    out=h_bf[mh, b, k][:, mc % 2, :].rearrange("p (c i t) -> p c t i", i=2, t=4),
-                    in0=banks[mc % 2][:].rearrange("p t (c i) -> p c t i", i=2),
-                    in1=act[mh, b][:, :, P * mc : P * (mc + 1)].rearrange("p t (c i) -> p c t i", i=2),
-                    op=MULT,
-                )
-
-        def quantize_h(mh, b, k):
-            cols = slice(QUART * k, QUART * (k + 1))
-            nc.vector.quantize_mx(
-                out=h_c[mh, b][:, cols].bitcast(FP8X4), scales=h_s[mh, b][:, cols], in_=h_bf[mh, b, k][:].rearrange("p c w -> p (c w)")
+        def apply_gain(mh, b, t):
+            nc.gpsimd.tensor_scalar(
+                out=act[mh, b][:, t, :], in0=act[mh, b][:, t, :], scalar1=gain[:, b, t : t + 1], scalar2=0.0, op0=MULT, op1=ADD
             )
+
+        def gate_product(mh, b, t, i):
+            sums = bank(i, [P, HALF])
+            for a in range(2):
+                first_pass(sums[:], a, gate_w, gate_s, b, t, HALF * mh, HALF)
+            return sums
+
+        def up_product(mh, b, mc, i):
+            sums = bank(i, [P, 4, P])
+            for t in range(4):
+                for a in range(2):
+                    first_pass(sums[:, t, :], a, up_w, up_s, b, t, HALF * mh + P * mc, P)
+            return sums
+
+        def make_h(mh, b, mc, sums):
+            nc.vector.tensor_tensor(
+                out=h_bf[mh, b][:, mc, :].rearrange("p (c i t) -> p c t i", i=2, t=4),
+                in0=sums[:].rearrange("p t (c i) -> p c t i", i=2),
+                in1=act[mh, b][:, :, P * mc : P * (mc + 1)].rearrange("p t (c i) -> p c t i", i=2),
+                op=MULT,
+            )
+
+        def quantize_h(mh, b):
+            nc.vector.quantize_mx(
+                out=h_c[mh, b][:].bitcast(FP8X4), scales=h_s[mh, b][:], in_=h_bf[mh, b][:].rearrange("p c w -> p (c w)")
+            )
+
+        wd_pair = [keep.tile([P, T, 2], BF16, name="wd_pair%d" % u, align_bytes=64) for u in range(2)]
+        wd_bf = [keep.tile([P, 2, 8 * P], BF16, name="wd_bf%d" % u, align_bytes=64) for u in range(2)]
+        wd_c = [keep.tile([P, 2, 2 * P], U32, name="wd_c%d" % u, align_bytes=64) for u in range(2)]
+        wd_s = [keep.tile([P, 2, 2 * P], U8, name="wd_s%d" % u, align_bytes=64) for u in range(2)]
 
         def cast_wd(u, c):
             nc.scalar.copy(
                 out=wd_pair[u][:, T // 2 * c : T // 2 * (c + 1), :], in_=wd_raw[u, c][:].rearrange("p i t -> p t i")
             )
 
-        wd_bf = [keep.tile([P, 2, 8 * P], BF16, name="wd_bf%d" % u, align_bytes=64) for u in range(2)]
-        wd_c = [keep.tile([P, 2, 2 * P], U32, name="wd_c%d" % u, align_bytes=64) for u in range(2)]
-        wd_s = [keep.tile([P, 2, 2 * P], U8, name="wd_s%d" % u, align_bytes=64) for u in range(2)]
+        def pick_wd(u):
+            return pick_all("wd_picked%d" % u, wd_pair[u][:].rearrange("p t i -> p (t i)"), F32)
 
-        def turn_wd(u):
-            picked = gather_words("wd_picked%d" % u, wd_pair[u][:].rearrange("p t i -> p (t i)"), F32)
+        def turn_wd(u, picked, first):
             for b in range(2):
-                bank = new_bank([P, 4, P])
+                turned = bank(first + b, [P, 4, P])
                 for t in range(4):
-                    nc.tensor.transpose(bank[:, t, :], picked[:, list_cols(b, t)], ident[:])
+                    nc.tensor.transpose(turned[:, t, :], picked[b][:, P * t : P * (t + 1)], ident[:])
                 nc.scalar.copy(
                     out=wd_bf[u][:, b, :].rearrange("p (c i t) -> p c t i", i=4, t=4),
-                    in_=bank[:].bitcast(BF16).rearrange("p t (c i) -> p c t i", i=4),
+                    in_=turned[:].bitcast(BF16).rearrange("p t (c i) -> p c t i", i=4),
                 )
 
         def quantize_wd(u):
@@ -259,68 +242,64 @@ def tile_list_routed_swiglu_expert_kernel(
                 in_=wd_bf[u][:].rearrange("p b c -> p (b c)"),
             )
 
-        def down_product(mh, u):
-            for v in range(2):
-                bank = new_bank([P, HALF])
-                for b in range(2):
-                    nc.tensor.matmul_mx(
-                        out=bank[:],
-                        lhsT=wd_c[u][:, b, P * v : P * (v + 1)].bitcast(FP8X4),
-                        lhsT_scale=wd_s[u][:, b, P * v : P * (v + 1)],
-                        rhs=h_c[mh, b][:].bitcast(FP8X4),
-                        rhs_scale=h_s[mh, b][:],
-                        start=(b == 0),
-                        stop=(b == 1),
-                    )
-                y = ring.tile([P, HALF], F32, name="y", bufs=8)
-                nc.vector.tensor_tensor(out=y[:], in0=bank[:], in1=p_all[mh][:], op=MULT)
-                row = P * (2 * u + v)
-                nc.sync.dma_start(out=out[row : row + P, HALF * mh : HALF * (mh + 1)], in_=y[:])
+        def down_product(mh, u, v, i):
+            sums = bank(i, [P, HALF])
+            for b in range(2):
+                nc.tensor.matmul_mx(
+                    out=sums[:],
+                    lhsT=wd_c[u][:, b, P * v : P * (v + 1)].bitcast(FP8X4),
+                    lhsT_scale=wd_s[u][:, b, P * v : P * (v + 1)],
+                    rhs=h_c[mh, b][:].bitcast(FP8X4),
+                    rhs_scale=h_s[mh, b][:],
+                    start=(b == 0),
+                    stop=(b == 1),
+                )
+            y = keep.tile([P, HALF], F32, name="y%d%d%d" % (mh, u, v))
+            nc.vector.tensor_tensor(out=y[:], in0=sums[:], in1=p_all[:, HALF * mh : HALF * (mh + 1)], op=MULT)
+            row = P * (2 * u + v)
+            nc.sync.dma_start(out=out[row : row + P, HALF * mh : HALF * (mh + 1)], in_=y[:])
 
-        g_ps = new_bank([P, 4, P])
+        g_ps = bank(7, [P, 4, P])
         for b in range(2):
             nc.tensor.transpose(g_ps[:, b, :], g_rows[:, b * P : (b + 1) * P], ident[:])
-        gain = keep.tile([P, 2, 8], F32, name="gain")
-        nc.vector.tensor_copy(out=gain[:], in_=g_ps[:, 0:2, 0:8])
-        for mh in range(2):
-            for b in range(2):
-                gate_part(mh, b)
-                gain_part(mh, b)
+        gain = keep.tile([P, 2, 4], F32, name="gain")
+        nc.vector.tensor_copy(out=gain[:], in_=g_ps[:, 0:2, 0:4])
+
+        opened = {(b, t): bank(4 * b + t, [P, HALF]) for b in range(2) for t in range(4)}
+        for b in range(2):
+            for a in range(2):
+                for t in range(4):
+                    first_pass(opened[b, t][:], a, gate_w, gate_s, b, t, 0, HALF)
+                    if a == 1:
+                        activate(0, b, t, opened[b, t])
+        for b in range(2):
+            for t in range(4):
+                activate(1, b, t, gate_product(1, b, t, 4 * b + t))
         for u in range(2):
             for c in range(2):
                 cast_wd(u, c)
-        free = placed["gate_win0"]
         for b in range(2):
-            for k in range(2):
-                make_h(0, b, k, up_part(0, b, k), free + 2048 * (2 * b + k))
-        for b in range(2):
-            for k in range(2):
-                quantize_h(0, b, k)
-        banks = {k: up_part(1, 0, k) for k in range(2)}
-        turn_wd(0)
-        make_h(1, 0, 0, banks[0], placed["gate_win1"])
-        later = up_part(1, 1, 0)
-        turn_wd(1)
-        make_h(1, 0, 1, banks[1], placed["spare"])
-        quantize_h(1, 0, 0)
-        make_h(1, 1, 0, later, placed["spare"] + 2048)
-        quantize_h(1, 0, 1)
-        quantize_wd(0)
-        last = up_part(1, 1, 1)
-        p_all = []
-        for mh in range(2):
-            bank = new_bank([P, 4, P])
             for mc in range(4):
-                col = 4 + 2 * mh + mc // 2
-                nc.tensor.transpose(bank[:, mc, :], gain[:, mc % 2, col : col + 1].to_broadcast([P, P]), ident[:])
-            p_all.append(keep.tile([P, HALF], F32, name="p_all%d" % mh))
-            nc.scalar.copy(out=p_all[mh][:], in_=bank[:].rearrange("p c m -> p (c m)"))
-
-        make_h(1, 1, 1, last, placed["spare"] + 4096)
-        quantize_h(1, 1, 0)
-        quantize_h(1, 1, 1)
-        down_product(0, 0)
+                make_h(0, b, mc, up_product(0, b, mc, 4 * b + mc))
+            quantize_h(0, b)
+        third = [up_product(1, 0, mc, mc) for mc in range(4)]
+        picked = pick_wd(0)
+        for mc in range(4):
+            make_h(1, 0, mc, third[mc])
+        turn_wd(0, picked, 4)
+        picked = pick_wd(1)
+        quantize_wd(0)
+        quantize_h(1, 0)
+        fourth = [up_product(1, 1, mc, (6 + mc) % 8) for mc in range(4)]
+        turn_wd(1, picked, 2)
+        for v in range(2):
+            down_product(0, 0, v, 4 + v)
         quantize_wd(1)
-        down_product(1, 0)
-        down_product(0, 1)
-        down_product(1, 1)
+        for mc in range(4):
+            make_h(1, 1, mc, fourth[mc])
+        quantize_h(1, 1)
+        for v in range(2):
+            down_product(0, 1, v, 2 + v)
+        for u in range(2):
+            for v in range(2):
+                down_product(1, u, v, (6 + 2 * u + v) % 8)

@@ -18,10 +18,7 @@ SILU = mybir.ActivationFunctionType.Silu
 
 P = 128
 HALF = 512
-PAD = 256
-FIRST_BYTES = 4 * T + 8 * HALF + 2 * M
-SECOND_BYTES = PAD + 4 * T + T
-LATE_BYTES = PAD + 6 * 4 * T + 8 * HALF + 4 * M
+HELD_BYTES = 8 * 4 * T + 2 * 8 * HALF + 4 * M
 
 
 def tile_list_routed_swiglu_expert_kernel(
@@ -46,30 +43,24 @@ def tile_list_routed_swiglu_expert_kernel(
         offsets = keep.tile([P, S // 16], U16, name="offsets")
         ident = keep.tile([P, P], F32, name="ident")
         gate_sc = keep.tile([P, T // 4], I32, name="gate_sc", align_bytes=64)
-        nc.gpsimd.memset(gate_sc[:], 0)
+        up_sc = keep.tile([P, T // 4], I32, name="up_sc", align_bytes=64)
+        x_sc = keep.tile([P, 2, M // 4], I32, name="x_sc", align_bytes=64)
         g_rows = keep.tile([P, 2 * P], F32, name="g_rows")
+        zeros = wins.tile([P, HELD_BYTES // 4], F32, name="zeros", offset=0, align_bytes=64)
+        nc.vector.memset(gate_sc[:], 0)
+        nc.vector.memset(up_sc[:], 0)
+        nc.vector.memset(x_sc[:], 0)
         nc.vector.memset(g_rows[:], 0.0)
-
-        def identity_part(name, c0, c1, offset, size):
-            zeros = wins.tile([P, size // 4], F32, name=name, offset=offset, align_bytes=64)
-            nc.gpsimd.memset(zeros[:, 0 : c1 - c0], 0.0)
-            nc.gpsimd.affine_select(
-                out=ident[:, c0:c1],
-                in_=zeros[:, 0 : c1 - c0],
-                compare_op=mybir.AluOpType.not_equal,
-                fill=1.0,
-                base=-c0,
-                pattern=[[-1, c1 - c0]],
-                channel_multiplier=1,
-            )
-
-        identity_part("zeros0", 0, 32, 0, FIRST_BYTES + PAD)
-        x_sc = wins.tile([P, 2, M // 4], I32, name="x_sc", offset=FIRST_BYTES - 2 * M, align_bytes=64)
-        nc.gpsimd.memset(x_sc[:], 0)
-        identity_part("zeros1", 32, 64, FIRST_BYTES, SECOND_BYTES + PAD)
-        up_sc = wins.tile([P, T // 4], I32, name="up_sc", offset=FIRST_BYTES + SECOND_BYTES - T, align_bytes=64)
-        nc.gpsimd.memset(up_sc[:], 0)
-        identity_part("zeros2", 64, P, FIRST_BYTES + SECOND_BYTES, LATE_BYTES)
+        nc.vector.memset(zeros[:, 0:P], 0.0)
+        nc.gpsimd.affine_select(
+            out=ident[:],
+            in_=zeros[:, 0:P],
+            compare_op=mybir.AluOpType.not_equal,
+            fill=1.0,
+            base=0,
+            pattern=[[-1, P]],
+            channel_multiplier=1,
+        )
 
         def load_scales(plane, scales):
             for q in range(4):
@@ -89,18 +80,16 @@ def tile_list_routed_swiglu_expert_kernel(
 
         nc.sync.dma_start(offsets[:], offs)
         load_scales(gate_sc, tab_scales)
-        nc.sync.dma_start(out=g_rows[0:4, :].rearrange("t (x r) -> t x r", r=8), in_=g.rearrange("(x t r) -> t x r", t=4, r=8))
-        gate_win = [load_words("gate_win0", tab_words, 0)]
-        x_w = [load_x(0)]
+        load_scales(up_sc, tab2_scales)
         for q in range(4):
             nc.sync.dma_start(
                 out=x_sc[32 * q : 32 * q + 4, :, :],
                 in_=x_scales[:, 4 * q : 4 * q + 4, :].rearrange("a r c -> r a c").bitcast(I32),
             )
-        sizes.append(2 * M + PAD)
+        nc.sync.dma_start(out=g_rows[0:4, :].rearrange("t (x r) -> t x r", r=8), in_=g.rearrange("(x t r) -> t x r", t=4, r=8))
+        gate_win = [load_words("gate_win0", tab_words, 0)]
+        x_w = [load_x(0)]
         gate_win.append(load_words("gate_win1", tab_words, 1))
-        load_scales(up_sc, tab2_scales)
-        sizes.append(T + PAD)
         up_win = [load_words("up_win0", tab2_words, 0)]
         x_w.append(load_x(1))
         up_win.append(load_words("up_win1", tab2_words, 1))
@@ -150,11 +139,11 @@ def tile_list_routed_swiglu_expert_kernel(
             return [picked[:, b, :] for b in range(2)]
 
         gate_listed = pick_scales("gate_s", gate_sc)
+        up_listed = pick_scales("up_s", up_sc)
         gate_s = [order_half(gate_listed, 0, keep.tile([P, P], I32, name="gate_s0", align_bytes=64))]
         gate_w = {(a, b): pick_half("gate_w%d%d" % (a, b), gate_win[a][:], b, I32) for a in range(2) for b in range(2)}
-        on_second_window = FIRST_BYTES + PAD
+        on_second_window = 4 * T + 8 * HALF
         gate_s.append(order_half(gate_listed, 1, wins.tile([P, P], I32, name="gate_s1", offset=on_second_window, align_bytes=64)))
-        up_listed = pick_scales("up_s", up_sc)
         up_w = {(0, b): half for b, half in enumerate(pick_all("up_w0", up_win[0][:], I32))}
         up_s = order_scales("up_s", up_listed)
         for b in range(2):
@@ -173,7 +162,7 @@ def tile_list_routed_swiglu_expert_kernel(
 
         quarters = [(mh, b) for mh in range(2) for b in range(2)]
         act = {key: keep.tile([P, 4, HALF], F32, name="act%d%d" % key) for key in quarters}
-        h_bf = {key: keep.tile([P, 4, 4 * P], BF16, name="h_bf%d%d" % key, align_bytes=64) for key in quarters}
+        h_bf = {key: keep.tile([P, 4, 4 * P], BF16, name="h_bf%d%d" % key, align_bytes=64) for key in quarters[:2]}
         h_c = {key: keep.tile([P, HALF], U32, name="h_c%d%d" % key, align_bytes=64) for key in quarters}
         h_s = {key: keep.tile([P, HALF], U8, name="h_s%d%d" % key, align_bytes=64) for key in quarters}
 
@@ -212,7 +201,8 @@ def tile_list_routed_swiglu_expert_kernel(
                 out=h_c[mh, b][:].bitcast(FP8X4), scales=h_s[mh, b][:], in_=h_bf[mh, b][:].rearrange("p c w -> p (c w)")
             )
 
-        wd_pair = [keep.tile([P, T, 2], BF16, name="wd_pair%d" % u, align_bytes=64) for u in range(2)]
+        pairs_at = [sum(sizes) + 4 * T * u for u in range(2)]
+        wd_pair = [place("wd_pair%d" % u, [P, T, 2], BF16, 4 * T) for u in range(2)]
         wd_bf = [keep.tile([P, 2, 8 * P], BF16, name="wd_bf%d" % u, align_bytes=64) for u in range(2)]
         wd_c = [keep.tile([P, 2, 2 * P], U32, name="wd_c%d" % u, align_bytes=64) for u in range(2)]
         wd_s = [keep.tile([P, 2, 2 * P], U8, name="wd_s%d" % u, align_bytes=64) for u in range(2)]
@@ -272,34 +262,38 @@ def tile_list_routed_swiglu_expert_kernel(
                     first_pass(opened[b, t][:], a, gate_w, gate_s, b, t, 0, HALF)
                     if a == 1:
                         activate(0, b, t, opened[b, t])
-        for b in range(2):
-            for t in range(4):
-                activate(1, b, t, gate_product(1, b, t, 4 * b + t))
-        for u in range(2):
-            for c in range(2):
-                cast_wd(u, c)
+        for t in range(4):
+            activate(1, 0, t, gate_product(1, 0, t, t))
+        for c in range(2):
+            cast_wd(0, c)
         for b in range(2):
             for mc in range(4):
-                make_h(0, b, mc, up_product(0, b, mc, 4 * b + mc))
+                make_h(0, b, mc, up_product(0, b, mc, 4 * (1 - b) + mc))
             quantize_h(0, b)
-        third = [up_product(1, 0, mc, mc) for mc in range(4)]
+        for t in range(4):
+            activate(1, 1, t, gate_product(1, 1, t, 4 + t))
+        for c in range(2):
+            cast_wd(1, c)
         picked = pick_wd(0)
+        h_bf[1, 0] = wins.tile([P, 4, 4 * P], BF16, name="h_bf10", offset=pairs_at[0], align_bytes=64)
+        third = [up_product(1, 0, mc, mc) for mc in range(4)]
+        fourth = [up_product(1, 1, mc, 4 + mc) for mc in range(2)]
+        turn_wd(0, picked, 6)
         for mc in range(4):
             make_h(1, 0, mc, third[mc])
-        turn_wd(0, picked, 4)
         picked = pick_wd(1)
-        quantize_wd(0)
+        h_bf[1, 1] = wins.tile([P, 4, 4 * P], BF16, name="h_bf11", offset=pairs_at[1], align_bytes=64)
         quantize_h(1, 0)
-        fourth = [up_product(1, 1, mc, (6 + mc) % 8) for mc in range(4)]
+        fourth.extend(up_product(1, 1, mc, mc - 2) for mc in range(2, 4))
         turn_wd(1, picked, 2)
-        for v in range(2):
-            down_product(0, 0, v, 4 + v)
-        quantize_wd(1)
         for mc in range(4):
             make_h(1, 1, mc, fourth[mc])
+        quantize_wd(0)
         quantize_h(1, 1)
-        for v in range(2):
-            down_product(0, 1, v, 2 + v)
-        for u in range(2):
+        for mh in range(2):
             for v in range(2):
-                down_product(1, u, v, (6 + 2 * u + v) % 8)
+                down_product(mh, 0, v, 4 + 2 * mh + v)
+        quantize_wd(1)
+        for mh in range(2):
+            for v in range(2):
+                down_product(mh, 1, v, 2 * mh + v)

@@ -47,11 +47,11 @@ def tile_list_routed_swiglu_expert_kernel(
         x_sc = keep.tile([P, 2, M // 4], I32, name="x_sc", align_bytes=64)
         g_rows = keep.tile([P, 2 * P], F32, name="g_rows")
         zeros = wins.tile([P, HELD_BYTES // 4], F32, name="zeros", offset=0, align_bytes=64)
-        nc.vector.memset(gate_sc[:], 0)
+        nc.gpsimd.memset(gate_sc[:], 0)
         nc.vector.memset(up_sc[:], 0)
         nc.vector.memset(x_sc[:], 0)
-        nc.vector.memset(g_rows[:], 0.0)
-        nc.vector.memset(zeros[:, 0:P], 0.0)
+        nc.gpsimd.memset(g_rows[:], 0.0)
+        nc.gpsimd.memset(zeros[:, 0:P], 0.0)
         nc.gpsimd.affine_select(
             out=ident[:],
             in_=zeros[:, 0:P],
@@ -286,14 +286,14 @@ def tile_list_routed_swiglu_expert_kernel(
         quantize_h(1, 0)
         fourth.extend(up_product(1, 1, mc, mc - 2) for mc in range(2, 4))
         turn_wd(1, picked, 2)
+        quantize_wd(0)
         for mc in range(4):
             make_h(1, 1, mc, fourth[mc])
-        quantize_wd(0)
         quantize_h(1, 1)
+        quantize_wd(1)
         for mh in range(2):
             for v in range(2):
-                down_product(mh, 0, v, 4 + 2 * mh + v)
-        quantize_wd(1)
+                down_product(mh, 0, v, 6 - 2 * mh + v)
         for mh in range(2):
             for v in range(2):
                 down_product(mh, 1, v, 2 * mh + v)

@@ -209,7 +209,8 @@ def tile_list_routed_swiglu_expert_kernel(
 
         def cast_wd(u, c):
             nc.scalar.copy(
-                out=wd_pair[u][:, T // 2 * c : T // 2 * (c + 1), :], in_=wd_raw[u, c][:].rearrange("p i t -> p t i")
+                out=wd_pair[u][:, T // 2 * c : T // 2 * (c + 1), :].rearrange("p (x k) i -> p x i k", k=4),
+                in_=wd_raw[u, c][:].rearrange("p i (x k) -> p x i k", k=4),
             )
 
         def pick_wd(u):

@@ -116,10 +116,11 @@ def tile_list_routed_swiglu_expert_kernel(
             return [picked[:, P * b : P * (b + 1)] for b in range(2)]
 
         def order_half(listed, b, picked):
-            nc.vector.tensor_copy(
-                out=picked[:].rearrange("p (t q w) -> p t q w", t=4, w=2),
-                in_=listed[:, HALF * b : HALF * (b + 1)].bitcast(I32).rearrange("p (q t w) -> p t q w", t=4, w=2),
-            )
+            for q0, q1 in ((0, 5), (5, 16)):
+                nc.vector.tensor_copy(
+                    out=picked[:].rearrange("p (t q w) -> p q t w", t=4, w=2)[:, q0:q1],
+                    in_=listed[:, HALF * b : HALF * (b + 1)].bitcast(I32).rearrange("p (q t w) -> p q t w", t=4, w=2)[:, q0:q1],
+                )
             return picked[:]
 
         def pick_half(name, win, b, dtype):
@@ -141,11 +142,11 @@ def tile_list_routed_swiglu_expert_kernel(
         gate_listed = pick_scales("gate_s", gate_sc)
         up_listed = pick_scales("up_s", up_sc)
         gate_s = [order_half(gate_listed, 0, keep.tile([P, P], I32, name="gate_s0", align_bytes=64))]
+        up_s = order_scales("up_s", up_listed)
         gate_w = {(a, b): pick_half("gate_w%d%d" % (a, b), gate_win[a][:], b, I32) for a in range(2) for b in range(2)}
         on_second_window = 4 * T + 8 * HALF
         gate_s.append(order_half(gate_listed, 1, wins.tile([P, P], I32, name="gate_s1", offset=on_second_window, align_bytes=64)))
         up_w = {(0, b): half for b, half in enumerate(pick_all("up_w0", up_win[0][:], I32))}
-        up_s = order_scales("up_s", up_listed)
         for b in range(2):
             up_w[1, b] = pick_half("up_w1%d" % b, up_win[1][:], b, I32)
 
@@ -163,7 +164,7 @@ def tile_list_routed_swiglu_expert_kernel(
         quarters = [(mh, b) for mh in range(2) for b in range(2)]
         act = {key: keep.tile([P, 4, HALF], F32, name="act%d%d" % key) for key in quarters}
         h_bf = {key: keep.tile([P, 4, 4 * P], BF16, name="h_bf%d%d" % key, align_bytes=64) for key in quarters[:2]}
-        h_c = {key: keep.tile([P, HALF], U32, name="h_c%d%d" % key, align_bytes=64) for key in quarters}
+        h_c = {key: keep.tile([P, HALF], U32, name="h_c%d%d" % key, align_bytes=64) for key in quarters if key != (0, 1)}
         h_s = {key: keep.tile([P, HALF], U8, name="h_s%d%d" % key, align_bytes=64) for key in quarters}
 
         def activate(mh, b, t, sums):
@@ -270,12 +271,15 @@ def tile_list_routed_swiglu_expert_kernel(
         for b in range(2):
             for mc in range(4):
                 make_h(0, b, mc, up_product(0, b, mc, 4 * (1 - b) + mc))
-            quantize_h(0, b)
+            if b == 0:
+                quantize_h(0, 0)
         for t in range(4):
             activate(1, 1, t, gate_product(1, 1, t, 4 + t))
         for c in range(2):
             cast_wd(1, c)
         picked = pick_wd(0)
+        h_c[0, 1] = wins.tile([P, HALF], U32, name="h_c01", offset=pairs_at[0] + 8 * HALF, align_bytes=64)
+        quantize_h(0, 1)
         h_bf[1, 0] = wins.tile([P, 4, 4 * P], BF16, name="h_bf10", offset=pairs_at[0], align_bytes=64)
         third = [up_product(1, 0, mc, mc) for mc in range(4)]
         fourth = [up_product(1, 1, mc, 4 + mc) for mc in range(2)]

@@ -18,7 +18,7 @@ SILU = mybir.ActivationFunctionType.Silu
 
 P = 128
 HALF = 512
-HELD_BYTES = 8 * 4 * T + 2 * 8 * HALF + 4 * M
+HELD_BYTES = 2 * M + 256 + 8 * 4 * T + 2 * 8 * HALF + 4 * M
 
 
 def tile_list_routed_swiglu_expert_kernel(
@@ -44,23 +44,33 @@ def tile_list_routed_swiglu_expert_kernel(
         ident = keep.tile([P, P], F32, name="ident")
         gate_sc = keep.tile([P, T // 4], I32, name="gate_sc", align_bytes=64)
         up_sc = keep.tile([P, T // 4], I32, name="up_sc", align_bytes=64)
-        x_sc = keep.tile([P, 2, M // 4], I32, name="x_sc", align_bytes=64)
         g_rows = keep.tile([P, 2 * P], F32, name="g_rows")
-        zeros = wins.tile([P, HELD_BYTES // 4], F32, name="zeros", offset=0, align_bytes=64)
+        first_bytes = 2 * M + 4 * T + 4 * HALF
+        zeros = [
+            wins.tile([P, first_bytes // 4 + 64], F32, name="zeros0", offset=0, align_bytes=64),
+            wins.tile([P, (HELD_BYTES - first_bytes) // 4], F32, name="zeros1", offset=first_bytes, align_bytes=64),
+        ]
         nc.gpsimd.memset(gate_sc[:], 0)
         nc.vector.memset(up_sc[:], 0)
-        nc.vector.memset(x_sc[:], 0)
-        nc.gpsimd.memset(g_rows[:], 0.0)
-        nc.gpsimd.memset(zeros[:, 0:P], 0.0)
-        nc.gpsimd.affine_select(
-            out=ident[:],
-            in_=zeros[:, 0:P],
-            compare_op=mybir.AluOpType.not_equal,
-            fill=1.0,
-            base=0,
-            pattern=[[-1, P]],
-            channel_multiplier=1,
-        )
+        nc.vector.memset(g_rows[:], 0.0)
+        nc.vector.memset(zeros[0][:, 0:64], 0.0)
+
+        def identity_half(i):
+            nc.gpsimd.affine_select(
+                out=ident[:, 64 * i : 64 * (i + 1)],
+                in_=zeros[i][:, 0:64],
+                compare_op=mybir.AluOpType.not_equal,
+                fill=1.0,
+                base=-64 * i,
+                pattern=[[-1, 64]],
+                channel_multiplier=1,
+            )
+
+        identity_half(0)
+        x_sc = place("x_sc", [P, 2, M // 4], I32, 2 * M)
+        nc.gpsimd.memset(x_sc[:], 0)
+        nc.gpsimd.memset(zeros[1][:, 0:64], 0.0)
+        identity_half(1)
 
         def load_scales(plane, scales):
             for q in range(4):
@@ -73,25 +83,30 @@ def tile_list_routed_swiglu_expert_kernel(
 
         x_all = x_words.rearrange("a p n i -> p a (n i)").bitcast(I32)
 
-        def load_x(mh):
-            half = place("x_w%d" % mh, [P, 2, HALF], I32, 8 * HALF)
-            nc.sync.dma_start(out=half[:], in_=x_all[:, :, HALF * mh : HALF * (mh + 1)])
-            return half
+        def load_x(mh, a0, passes):
+            part = place("x_w%d%d" % (mh, a0), [P, passes, HALF], I32, 4 * HALF * passes)
+            nc.sync.dma_start(out=part[:], in_=x_all[:, a0 : a0 + passes, HALF * mh : HALF * (mh + 1)])
+            for a in range(passes):
+                x_w[mh, a0 + a] = part[:, a, :]
+
+        x_w = {}
 
         nc.sync.dma_start(offsets[:], offs)
         load_scales(gate_sc, tab_scales)
         load_scales(up_sc, tab2_scales)
+        nc.sync.dma_start(out=g_rows[0:4, :].rearrange("t (x r) -> t x r", r=8), in_=g.rearrange("(x t r) -> t x r", t=4, r=8))
+        gate_win = [load_words("gate_win0", tab_words, 0)]
+        load_x(0, 0, 1)
         for q in range(4):
             nc.sync.dma_start(
                 out=x_sc[32 * q : 32 * q + 4, :, :],
                 in_=x_scales[:, 4 * q : 4 * q + 4, :].rearrange("a r c -> r a c").bitcast(I32),
             )
-        nc.sync.dma_start(out=g_rows[0:4, :].rearrange("t (x r) -> t x r", r=8), in_=g.rearrange("(x t r) -> t x r", t=4, r=8))
-        gate_win = [load_words("gate_win0", tab_words, 0)]
-        x_w = [load_x(0)]
+        sizes.append(256)
         gate_win.append(load_words("gate_win1", tab_words, 1))
+        load_x(0, 1, 1)
         up_win = [load_words("up_win0", tab2_words, 0)]
-        x_w.append(load_x(1))
+        load_x(1, 0, 2)
         up_win.append(load_words("up_win1", tab2_words, 1))
         wd_raw = {}
         for u in range(2):
@@ -144,7 +159,7 @@ def tile_list_routed_swiglu_expert_kernel(
         gate_s = [order_half(gate_listed, 0, keep.tile([P, P], I32, name="gate_s0", align_bytes=64))]
         up_s = order_scales("up_s", up_listed)
         gate_w = {(a, b): pick_half("gate_w%d%d" % (a, b), gate_win[a][:], b, I32) for a in range(2) for b in range(2)}
-        on_second_window = 4 * T + 8 * HALF
+        on_second_window = first_bytes + 256
         gate_s.append(order_half(gate_listed, 1, wins.tile([P, P], I32, name="gate_s1", offset=on_second_window, align_bytes=64)))
         up_w = {(0, b): half for b, half in enumerate(pick_all("up_w0", up_win[0][:], I32))}
         for b in range(2):
@@ -155,7 +170,7 @@ def tile_list_routed_swiglu_expert_kernel(
                 out=dst,
                 lhsT=words[a, b][:, P * t : P * (t + 1)].bitcast(FP8X4),
                 lhsT_scale=scales[b].bitcast(U8)[4 * a :, P * t : P * (t + 1)],
-                rhs=x_w[m0 // HALF][:, a, m0 % HALF : m0 % HALF + width].bitcast(FP8X4),
+                rhs=x_w[m0 // HALF, a][:, m0 % HALF : m0 % HALF + width].bitcast(FP8X4),
                 rhs_scale=x_sc[:, a, :].bitcast(U8)[:, m0 : m0 + width],
                 start=(a == 0),
                 stop=(a == 1),

@@ -130,16 +130,7 @@ def tile_list_routed_swiglu_expert_kernel(
             )
             return [picked[:, P * b : P * (b + 1)] for b in range(2)]
 
-        def order_half(listed, b, picked):
-            for q0, q1 in ((0, 5), (5, 16)):
-                nc.vector.tensor_copy(
-                    out=picked[:].rearrange("p (t q w) -> p q t w", t=4, w=2)[:, q0:q1],
-                    in_=listed[:, HALF * b : HALF * (b + 1)].bitcast(I32).rearrange("p (q t w) -> p q t w", t=4, w=2)[:, q0:q1],
-                )
-            return picked[:]
-
-        def pick_half(name, win, b, dtype):
-            picked = keep.tile([P, HALF], dtype, name=name, align_bytes=64)
+        def pick_half(picked, win, b):
             nc.vector.tensor_copy(
                 out=picked[:].bitcast(U32).rearrange("p (t q r) -> p q t r", t=4, r=8),
                 in_=win.bitcast(U32).indirect(offsets[:, 32 * b : 32 * (b + 1)]),
@@ -156,24 +147,27 @@ def tile_list_routed_swiglu_expert_kernel(
 
         gate_listed = pick_scales("gate_s", gate_sc)
         up_listed = pick_scales("up_s", up_sc)
-        gate_s = [order_half(gate_listed, 0, keep.tile([P, P], I32, name="gate_s0", align_bytes=64))]
+        gate_s = order_scales("gate_s", gate_listed)
         up_s = order_scales("up_s", up_listed)
-        gate_w = {(a, b): pick_half("gate_w%d%d" % (a, b), gate_win[a][:], b, I32) for a in range(2) for b in range(2)}
-        on_second_window = first_bytes + 256
-        gate_s.append(order_half(gate_listed, 1, wins.tile([P, P], I32, name="gate_s1", offset=on_second_window, align_bytes=64)))
+        def half_tile(name):
+            return keep.tile([P, HALF], I32, name=name, align_bytes=64)
+
+        gate_w = {(a, b): pick_half(half_tile("gate_w%d%d" % (a, b)), gate_win[a][:], b) for a, b in ((0, 0), (1, 0), (1, 1))}
+        on_second_window = wins.tile([P, HALF], I32, name="gate_w01", offset=first_bytes + 256, align_bytes=64)
+        gate_w[0, 1] = pick_half(on_second_window, gate_win[0][:], 1)
         up_w = {(0, b): half for b, half in enumerate(pick_all("up_w0", up_win[0][:], I32))}
         for b in range(2):
-            up_w[1, b] = pick_half("up_w1%d" % b, up_win[1][:], b, I32)
+            up_w[1, b] = pick_half(half_tile("up_w1%d" % b), up_win[1][:], b)
 
-        def first_pass(dst, a, words, scales, b, t, m0, width):
+        def first_pass(dst, a, words, scales, b, t, m0, width, opens=0):
             nc.tensor.matmul_mx(
                 out=dst,
                 lhsT=words[a, b][:, P * t : P * (t + 1)].bitcast(FP8X4),
                 lhsT_scale=scales[b].bitcast(U8)[4 * a :, P * t : P * (t + 1)],
                 rhs=x_w[m0 // HALF, a][:, m0 % HALF : m0 % HALF + width].bitcast(FP8X4),
                 rhs_scale=x_sc[:, a, :].bitcast(U8)[:, m0 : m0 + width],
-                start=(a == 0),
-                stop=(a == 1),
+                start=(a == opens),
+                stop=(a != opens),
             )
 
         quarters = [(mh, b) for mh in range(2) for b in range(2)]
@@ -219,7 +213,7 @@ def tile_list_routed_swiglu_expert_kernel(
 
         pairs_at = [sum(sizes) + 4 * T * u for u in range(2)]
         wd_pair = [place("wd_pair%d" % u, [P, T, 2], BF16, 4 * T) for u in range(2)]
-        wd_bf = [keep.tile([P, 2, 8 * P], BF16, name="wd_bf%d" % u, align_bytes=64) for u in range(2)]
+        wd_bf = [place("wd_bf%d" % u, [P, 2, 8 * P], BF16, 32 * P) for u in range(2)]
         wd_c = [keep.tile([P, 2, 2 * P], U32, name="wd_c%d" % u, align_bytes=64) for u in range(2)]
         wd_s = [keep.tile([P, 2, 2 * P], U8, name="wd_s%d" % u, align_bytes=64) for u in range(2)]
 
@@ -232,9 +226,9 @@ def tile_list_routed_swiglu_expert_kernel(
         def pick_wd(u):
             return pick_all("wd_picked%d" % u, wd_pair[u][:].rearrange("p t i -> p (t i)"), F32)
 
-        def turn_wd(u, picked, first):
+        def turn_wd(u, picked, banks):
             for b in range(2):
-                turned = bank(first + b, [P, 4, P])
+                turned = bank(banks[b], [P, 4, P])
                 for t in range(4):
                     nc.tensor.transpose(turned[:, t, :], picked[b][:, P * t : P * (t + 1)], ident[:])
                 nc.scalar.copy(
@@ -249,7 +243,7 @@ def tile_list_routed_swiglu_expert_kernel(
                 in_=wd_bf[u][:].rearrange("p b c -> p (b c)"),
             )
 
-        def down_product(mh, u, v, i):
+        def down_sums(mh, u, v, i):
             sums = bank(i, [P, HALF])
             for b in range(2):
                 nc.tensor.matmul_mx(
@@ -261,10 +255,20 @@ def tile_list_routed_swiglu_expert_kernel(
                     start=(b == 0),
                     stop=(b == 1),
                 )
-            y = keep.tile([P, HALF], F32, name="y%d%d%d" % (mh, u, v))
-            nc.vector.tensor_tensor(out=y[:], in0=sums[:], in1=p_all[:, HALF * mh : HALF * (mh + 1)], op=MULT)
+            return sums
+
+        def store(mh, u, v, y, c0, width):
             row = P * (2 * u + v)
-            nc.sync.dma_start(out=out[row : row + P, HALF * mh : HALF * (mh + 1)], in_=y[:])
+            nc.sync.dma_start(out=out[row : row + P, HALF * mh + c0 : HALF * mh + c0 + width], in_=y[:])
+
+        def finish(mh, u, v, sums, parts):
+            width = HALF // parts
+            for c0 in range(0, HALF, width):
+                y = keep.tile([P, width], F32, name="y%d%d%d_%d" % (mh, u, v, c0))
+                nc.vector.tensor_tensor(
+                    out=y[:], in0=sums[:, c0 : c0 + width], in1=p_all[:, HALF * mh + c0 : HALF * mh + c0 + width], op=MULT
+                )
+                store(mh, u, v, y, c0, width)
 
         g_ps = bank(7, [P, 4, P])
         for b in range(2):
@@ -274,10 +278,10 @@ def tile_list_routed_swiglu_expert_kernel(
 
         opened = {(b, t): bank(4 * b + t, [P, HALF]) for b in range(2) for t in range(4)}
         for b in range(2):
-            for a in range(2):
+            for a in (b, 1 - b):
                 for t in range(4):
-                    first_pass(opened[b, t][:], a, gate_w, gate_s, b, t, 0, HALF)
-                    if a == 1:
+                    first_pass(opened[b, t][:], a, gate_w, gate_s, b, t, 0, HALF, b)
+                    if a != b:
                         activate(0, b, t, opened[b, t])
         for t in range(4):
             activate(1, 0, t, gate_product(1, 0, t, t))
@@ -298,22 +302,24 @@ def tile_list_routed_swiglu_expert_kernel(
         h_bf[1, 0] = wins.tile([P, 4, 4 * P], BF16, name="h_bf10", offset=pairs_at[0], align_bytes=64)
         third = [up_product(1, 0, mc, mc) for mc in range(4)]
         fourth = [up_product(1, 1, mc, 4 + mc) for mc in range(2)]
-        turn_wd(0, picked, 6)
+        turn_wd(0, picked, (6, 7))
         for mc in range(4):
             make_h(1, 0, mc, third[mc])
         picked = pick_wd(1)
-        h_bf[1, 1] = wins.tile([P, 4, 4 * P], BF16, name="h_bf11", offset=pairs_at[1], align_bytes=64)
         quantize_h(1, 0)
-        fourth.extend(up_product(1, 1, mc, mc - 2) for mc in range(2, 4))
-        turn_wd(1, picked, 2)
         quantize_wd(0)
+        h_bf[1, 1] = wins.tile([P, 4, 4 * P], BF16, name="h_bf11", offset=pairs_at[1] + 4 * T - 4 * HALF, align_bytes=64)
+        early = [down_sums(0, 0, v, 6 + v) for v in range(2)]
+        fourth.extend(up_product(1, 1, mc, mc - 2) for mc in range(2, 4))
+        turn_wd(1, picked, (2, 3))
         for mc in range(4):
             make_h(1, 1, mc, fourth[mc])
+        finish(0, 0, 0, early[0], 1)
         quantize_h(1, 1)
         quantize_wd(1)
+        finish(0, 0, 1, early[1], 1)
+        for v in range(2):
+            finish(1, 0, v, down_sums(1, 0, v, 4 + v), 1)
         for mh in range(2):
             for v in range(2):
-                down_product(mh, 0, v, 6 - 2 * mh + v)
-        for mh in range(2):
-            for v in range(2):
-                down_product(mh, 1, v, 2 * mh + v)
+                finish(mh, 1, v, down_sums(mh, 1, v, 2 * mh + v), 1 + mh * v)

@@ -18,7 +18,7 @@ SILU = mybir.ActivationFunctionType.Silu
 
 P = 128
 HALF = 512
-HELD_BYTES = 2 * M + 256 + 8 * 4 * T + 2 * 8 * HALF + 4 * M
+HELD_BYTES = 2 * M + 256 + 8 * 4 * T + 3 * 4 * HALF + 4 * M
 
 
 def tile_list_routed_swiglu_expert_kernel(
@@ -28,6 +28,7 @@ def tile_list_routed_swiglu_expert_kernel(
     with ExitStack() as ctx:
         keep = ctx.enter_context(tc.tile_pool(name="keep", bufs=1))
         wins = ctx.enter_context(tc.tile_pool(name="wins", bufs=1))
+        head = ctx.enter_context(tc.tile_pool(name="head", bufs=1))
         psum = ctx.enter_context(tc.psum_pool(name="psum", bufs=1))
 
         def bank(i, shape):
@@ -43,9 +44,9 @@ def tile_list_routed_swiglu_expert_kernel(
         offsets = keep.tile([P, S // 16], U16, name="offsets")
         ident = keep.tile([P, P], F32, name="ident")
         gate_sc = keep.tile([P, T // 4], I32, name="gate_sc", align_bytes=64)
-        up_sc = keep.tile([P, T // 4], I32, name="up_sc", align_bytes=64)
+        up_sc = head.tile([P, T // 4], I32, name="up_sc", offset=0, align_bytes=64)
         g_rows = keep.tile([P, 2 * P], F32, name="g_rows")
-        first_bytes = 2 * M + 4 * T + 4 * HALF
+        first_bytes = 2 * M + 8 * T
         zeros = [
             wins.tile([P, first_bytes // 4 + 64], F32, name="zeros0", offset=0, align_bytes=64),
             wins.tile([P, (HELD_BYTES - first_bytes) // 4], F32, name="zeros1", offset=first_bytes, align_bytes=64),
@@ -83,8 +84,7 @@ def tile_list_routed_swiglu_expert_kernel(
 
         x_all = x_words.rearrange("a p n i -> p a (n i)").bitcast(I32)
 
-        def load_x(mh, a0, passes):
-            part = place("x_w%d%d" % (mh, a0), [P, passes, HALF], I32, 4 * HALF * passes)
+        def load_x(mh, a0, passes, part):
             nc.sync.dma_start(out=part[:], in_=x_all[:, a0 : a0 + passes, HALF * mh : HALF * (mh + 1)])
             for a in range(passes):
                 x_w[mh, a0 + a] = part[:, a, :]
@@ -92,26 +92,28 @@ def tile_list_routed_swiglu_expert_kernel(
         x_w = {}
 
         nc.sync.dma_start(offsets[:], offs)
+        load_x(0, 0, 1, keep.tile([P, 1, HALF], I32, name="x_w00", align_bytes=64))
         load_scales(gate_sc, tab_scales)
         load_scales(up_sc, tab2_scales)
         nc.sync.dma_start(out=g_rows[0:4, :].rearrange("t (x r) -> t x r", r=8), in_=g.rearrange("(x t r) -> t x r", t=4, r=8))
-        gate_win = [load_words("gate_win0", tab_words, 0)]
-        load_x(0, 0, 1)
+        gate_win = [load_words("gate_win%d" % a, tab_words, a) for a in range(2)]
         for q in range(4):
             nc.sync.dma_start(
                 out=x_sc[32 * q : 32 * q + 4, :, :],
                 in_=x_scales[:, 4 * q : 4 * q + 4, :].rearrange("a r c -> r a c").bitcast(I32),
             )
         sizes.append(256)
-        gate_win.append(load_words("gate_win1", tab_words, 1))
-        load_x(0, 1, 1)
+        second_pass_at = sum(sizes)
+        load_x(0, 1, 1, place("x_w01", [P, 1, HALF], I32, 4 * HALF))
         up_win = [load_words("up_win0", tab2_words, 0)]
-        load_x(1, 0, 2)
+        load_x(1, 0, 2, place("x_w1", [P, 2, HALF], I32, 8 * HALF))
         up_win.append(load_words("up_win1", tab2_words, 1))
         wd_raw = {}
+        raw_at = {}
         for u in range(2):
             rows = wdT[2 * P * u : 2 * P * (u + 1), :].rearrange("(p i) t -> p i t", i=2)
             for c in range(2):
+                raw_at[u, c] = sum(sizes)
                 wd_raw[u, c] = place("wd_raw%d%d" % (u, c), [P, 2, T // 2], F32, 4 * T)
                 nc.sync.dma_start(out=wd_raw[u, c][:], in_=rows[:, :, T // 2 * c : T // 2 * (c + 1)])
         p_all = place("p_all", [P, M], F32, 4 * M)
@@ -122,8 +124,7 @@ def tile_list_routed_swiglu_expert_kernel(
             nc.vector.tensor_copy(out=listed[:], in_=plane[:].bitcast(U8).indirect(offsets[:]))
             return listed
 
-        def order_scales(name, listed):
-            picked = keep.tile([P, S // 4], I32, name=name, align_bytes=64)
+        def order_scales(picked, listed):
             nc.vector.tensor_copy(
                 out=picked[:].rearrange("p (b t q w) -> p b t q w", b=2, t=4, w=2),
                 in_=listed[:].bitcast(I32).rearrange("p (b q t w) -> p b t q w", b=2, t=4, w=2),
@@ -147,13 +148,19 @@ def tile_list_routed_swiglu_expert_kernel(
 
         gate_listed = pick_scales("gate_s", gate_sc)
         up_listed = pick_scales("up_s", up_sc)
-        gate_s = order_scales("gate_s", gate_listed)
-        up_s = order_scales("up_s", up_listed)
+        gate_s = order_scales(head.tile([P, S // 4], I32, name="gate_s", offset=0, align_bytes=64), gate_listed)
+        g_ps = bank(7, [P, 4, P])
+        for b in range(2):
+            nc.tensor.transpose(g_ps[:, b, :], g_rows[:, b * P : (b + 1) * P], ident[:])
+        gain = head.tile([P, 2, 4], F32, name="gain", offset=S, align_bytes=64)
+        nc.vector.tensor_copy(out=gain[:], in_=g_ps[:, 0:2, 0:4])
+
+        up_s = order_scales(keep.tile([P, S // 4], I32, name="up_s", align_bytes=64), up_listed)
         def half_tile(name):
             return keep.tile([P, HALF], I32, name=name, align_bytes=64)
 
         gate_w = {(a, b): pick_half(half_tile("gate_w%d%d" % (a, b)), gate_win[a][:], b) for a, b in ((0, 0), (1, 0), (1, 1))}
-        on_second_window = wins.tile([P, HALF], I32, name="gate_w01", offset=first_bytes + 256, align_bytes=64)
+        on_second_window = wins.tile([P, HALF], I32, name="gate_w01", offset=first_bytes - 4 * T, align_bytes=64)
         gate_w[0, 1] = pick_half(on_second_window, gate_win[0][:], 1)
         up_w = {(0, b): half for b, half in enumerate(pick_all("up_w0", up_win[0][:], I32))}
         for b in range(2):
@@ -172,23 +179,24 @@ def tile_list_routed_swiglu_expert_kernel(
 
         quarters = [(mh, b) for mh in range(2) for b in range(2)]
         act = {key: keep.tile([P, 4, HALF], F32, name="act%d%d" % key) for key in quarters}
-        h_bf = {key: keep.tile([P, 4, 4 * P], BF16, name="h_bf%d%d" % key, align_bytes=64) for key in quarters[:2]}
-        h_c = {key: keep.tile([P, HALF], U32, name="h_c%d%d" % key, align_bytes=64) for key in quarters if key != (0, 1)}
+        h_bf = {key: keep.tile([P, 4, 4 * P], BF16, name="h_bf%d%d" % key, align_bytes=64)[:] for key in quarters[:2]}
+        h_c = {key: keep.tile([P, HALF], U32, name="h_c%d%d" % key, align_bytes=64) for key in quarters[3:]}
         h_s = {key: keep.tile([P, HALF], U8, name="h_s%d%d" % key, align_bytes=64) for key in quarters}
 
-        def activate(mh, b, t, sums):
-            nc.scalar.activation(out=act[mh, b][:, t, :], in_=sums[:], func=SILU)
-            apply_gain(mh, b, t)
+        last_silu_at = sum(sizes)
+        last_silu = place("last_silu", [P, HALF], F32, 4 * HALF)
 
-        def apply_gain(mh, b, t):
+        def activate(mh, b, t, sums):
+            plain = last_silu[:] if (mh, b, t) == (1, 1, 3) else act[mh, b][:, t, :]
+            nc.scalar.activation(out=plain, in_=sums[:], func=SILU)
             nc.gpsimd.tensor_scalar(
-                out=act[mh, b][:, t, :], in0=act[mh, b][:, t, :], scalar1=gain[:, b, t : t + 1], scalar2=0.0, op0=MULT, op1=ADD
+                out=act[mh, b][:, t, :], in0=plain, scalar1=gain[:, b, t : t + 1], scalar2=0.0, op0=MULT, op1=ADD
             )
 
-        def gate_product(mh, b, t, i):
+        def gate_product(mh, b, t, i, opens=0):
             sums = bank(i, [P, HALF])
-            for a in range(2):
-                first_pass(sums[:], a, gate_w, gate_s, b, t, HALF * mh, HALF)
+            for a in (opens, 1 - opens):
+                first_pass(sums[:], a, gate_w, gate_s, b, t, HALF * mh, HALF, opens)
             return sums
 
         def up_product(mh, b, mc, i):
@@ -208,12 +216,16 @@ def tile_list_routed_swiglu_expert_kernel(
 
         def quantize_h(mh, b):
             nc.vector.quantize_mx(
-                out=h_c[mh, b][:].bitcast(FP8X4), scales=h_s[mh, b][:], in_=h_bf[mh, b][:].rearrange("p c w -> p (c w)")
+                out=h_c[mh, b][:].bitcast(FP8X4), scales=h_s[mh, b][:], in_=h_bf[mh, b].rearrange("p c w -> p (c w)")
             )
 
         pairs_at = [sum(sizes) + 4 * T * u for u in range(2)]
         wd_pair = [place("wd_pair%d" % u, [P, T, 2], BF16, 4 * T) for u in range(2)]
-        wd_bf = [place("wd_bf%d" % u, [P, 2, 8 * P], BF16, 32 * P) for u in range(2)]
+        shared = keep.tile([P, 6 * HALF], BF16, name="shared", align_bytes=64)
+        wd_bf = [
+            shared[:, 2 * HALF : 6 * HALF].rearrange("p (b c) -> p b c", b=2),
+            keep.tile([P, 2, 8 * P], BF16, name="wd_bf1", align_bytes=64)[:],
+        ]
         wd_c = [keep.tile([P, 2, 2 * P], U32, name="wd_c%d" % u, align_bytes=64) for u in range(2)]
         wd_s = [keep.tile([P, 2, 2 * P], U8, name="wd_s%d" % u, align_bytes=64) for u in range(2)]
 
@@ -240,7 +252,7 @@ def tile_list_routed_swiglu_expert_kernel(
             nc.vector.quantize_mx(
                 out=wd_c[u][:].rearrange("p b n -> p (b n)").bitcast(FP8X4),
                 scales=wd_s[u][:].rearrange("p b n -> p (b n)"),
-                in_=wd_bf[u][:].rearrange("p b c -> p (b c)"),
+                in_=wd_bf[u].rearrange("p b c -> p (b c)"),
             )
 
         def down_sums(mh, u, v, i):
@@ -270,56 +282,62 @@ def tile_list_routed_swiglu_expert_kernel(
                 )
                 store(mh, u, v, y, c0, width)
 
-        g_ps = bank(7, [P, 4, P])
-        for b in range(2):
-            nc.tensor.transpose(g_ps[:, b, :], g_rows[:, b * P : (b + 1) * P], ident[:])
-        gain = keep.tile([P, 2, 4], F32, name="gain")
-        nc.vector.tensor_copy(out=gain[:], in_=g_ps[:, 0:2, 0:4])
-
-        opened = {(b, t): bank(4 * b + t, [P, HALF]) for b in range(2) for t in range(4)}
-        for b in range(2):
-            for a in (b, 1 - b):
-                for t in range(4):
-                    first_pass(opened[b, t][:], a, gate_w, gate_s, b, t, 0, HALF, b)
-                    if a != b:
-                        activate(0, b, t, opened[b, t])
+        opened = [bank(t, [P, HALF]) for t in range(2)]
+        for a in range(2):
+            for t in range(2):
+                first_pass(opened[t][:], a, gate_w, gate_s, 0, t, 0, HALF)
+                if a == 1:
+                    activate(0, 0, t, opened[t])
+        for t in range(2, 4):
+            activate(0, 0, t, gate_product(0, 0, t, t, 1))
+        for t in range(4):
+            activate(0, 1, t, gate_product(0, 1, t, 4 + t, 1))
         for t in range(4):
             activate(1, 0, t, gate_product(1, 0, t, t))
         for c in range(2):
             cast_wd(0, c)
-        for b in range(2):
-            for mc in range(4):
-                make_h(0, b, mc, up_product(0, b, mc, 4 * (1 - b) + mc))
-            if b == 0:
-                quantize_h(0, 0)
-        for t in range(4):
-            activate(1, 1, t, gate_product(1, 1, t, 4 + t))
+        for mc in range(4):
+            make_h(0, 0, mc, up_product(0, 0, mc, 4 + mc))
+        second = [up_product(0, 1, mc, mc) for mc in range(4)]
+        for mc in range(3):
+            make_h(0, 1, mc, second[mc])
+        h_c[0, 0] = wins.tile([P, HALF], U32, name="h_c00", offset=second_pass_at, align_bytes=64)
+        quantize_h(0, 0)
+        make_h(0, 1, 3, second[3])
+        last_gate = [gate_product(1, 1, t, 4 + t) for t in range(4)]
+        for t in range(2):
+            activate(1, 1, t, last_gate[t])
         for c in range(2):
             cast_wd(1, c)
+        for t in range(2, 4):
+            activate(1, 1, t, last_gate[t])
         picked = pick_wd(0)
-        h_c[0, 1] = wins.tile([P, HALF], U32, name="h_c01", offset=pairs_at[0] + 8 * HALF, align_bytes=64)
+        h_c[0, 1] = wins.tile([P, HALF], U32, name="h_c01", offset=raw_at[0, 1], align_bytes=64)
         quantize_h(0, 1)
-        h_bf[1, 0] = wins.tile([P, 4, 4 * P], BF16, name="h_bf10", offset=pairs_at[0], align_bytes=64)
+        h_bf[1, 0] = wins.tile([P, 4, 4 * P], BF16, name="h_bf10", offset=pairs_at[0], align_bytes=64)[:]
         third = [up_product(1, 0, mc, mc) for mc in range(4)]
-        fourth = [up_product(1, 1, mc, 4 + mc) for mc in range(2)]
-        turn_wd(0, picked, (6, 7))
+        turn_wd(0, picked, (4, 5))
         for mc in range(4):
             make_h(1, 0, mc, third[mc])
+        fourth = [up_product(1, 1, mc, mc) for mc in range(4)]
         picked = pick_wd(1)
+        h_c[1, 0] = wins.tile([P, HALF], U32, name="h_c10", offset=last_silu_at, align_bytes=64)
         quantize_h(1, 0)
-        quantize_wd(0)
-        h_bf[1, 1] = wins.tile([P, 4, 4 * P], BF16, name="h_bf11", offset=pairs_at[1] + 4 * T - 4 * HALF, align_bytes=64)
-        early = [down_sums(0, 0, v, 6 + v) for v in range(2)]
-        fourth.extend(up_product(1, 1, mc, mc - 2) for mc in range(2, 4))
-        turn_wd(1, picked, (2, 3))
-        for mc in range(4):
+        turn_wd(1, picked, (6, 7))
+        h_bf[1, 1] = shared[:, 0 : 4 * HALF].rearrange("p (c w) -> p c w", c=4)
+        for mc in range(2):
             make_h(1, 1, mc, fourth[mc])
+        quantize_wd(0)
+        early = [down_sums(0, 0, 0, 4)]
+        for mc in range(2, 4):
+            make_h(1, 1, mc, fourth[mc])
+        early.append(down_sums(0, 0, 1, 3))
         finish(0, 0, 0, early[0], 1)
         quantize_h(1, 1)
         quantize_wd(1)
         finish(0, 0, 1, early[1], 1)
         for v in range(2):
-            finish(1, 0, v, down_sums(1, 0, v, 4 + v), 1)
+            finish(1, 0, v, down_sums(1, 0, v, v), 1)
         for mh in range(2):
             for v in range(2):
-                finish(mh, 1, v, down_sums(mh, 1, v, 2 * mh + v), 1 + mh * v)
+                finish(mh, 1, v, down_sums(mh, 1, v, (2, 5, 6, 7)[2 * mh + v]), 1 + mh * v)

@@ -18,7 +18,18 @@ SILU = mybir.ActivationFunctionType.Silu
 
 P = 128
 HALF = 512
-HELD_BYTES = 2 * M + 256 + 8 * 4 * T + 3 * 4 * HALF + 4 * M
+FIRST_ROW = (12, 0)
+ROW = 4 * T
+
+GATE_AT = (0, 2 * ROW - 4 * HALF)
+X1_AT = 2 * ROW
+UP_AT = (X1_AT + 8 * HALF + ROW, GATE_AT[0])
+P_AT = UP_AT[0] + ROW
+X0_AT = P_AT + 4 * HALF
+LAST_SILU_AT = X0_AT + 8 * HALF
+PAIR_AT = (LAST_SILU_AT + 4 * HALF, LAST_SILU_AT + 4 * HALF + ROW)
+LISTED_AT = PAIR_AT[1] + ROW
+RAW_AT = {(0, 0): X1_AT + 8 * HALF, (0, 1): ROW, (1, 0): UP_AT[0], (1, 1): UP_AT[1]}
 
 
 def tile_list_routed_swiglu_expert_kernel(
@@ -28,108 +39,81 @@ def tile_list_routed_swiglu_expert_kernel(
     with ExitStack() as ctx:
         keep = ctx.enter_context(tc.tile_pool(name="keep", bufs=1))
         wins = ctx.enter_context(tc.tile_pool(name="wins", bufs=1))
-        head = ctx.enter_context(tc.tile_pool(name="head", bufs=1))
         psum = ctx.enter_context(tc.psum_pool(name="psum", bufs=1))
 
         def bank(i, shape):
             return psum.tile(shape, F32, name="bank%d" % i)
 
-        sizes = []
-
-        def place(name, shape, dtype, size):
-            at = sum(sizes)
-            sizes.append(size)
+        def place(name, shape, dtype, at):
             return wins.tile(shape, dtype, name=name, offset=at, align_bytes=64)
 
         offsets = keep.tile([P, S // 16], U16, name="offsets")
         ident = keep.tile([P, P], F32, name="ident")
-        gate_sc = keep.tile([P, T // 4], I32, name="gate_sc", align_bytes=64)
-        up_sc = head.tile([P, T // 4], I32, name="up_sc", offset=0, align_bytes=64)
+        gate_sc = place("gate_sc", [P, T // 4], I32, UP_AT[0])
+        up_sc = keep.tile([P, T // 4], I32, name="up_sc", align_bytes=64)
+        planes = [keep.tile([P, 3, S // 4], I32, name="planes%d" % a, align_bytes=64) for a in range(2)]
         g_rows = keep.tile([P, 2 * P], F32, name="g_rows")
-        first_bytes = 2 * M + 8 * T
-        zeros = [
-            wins.tile([P, first_bytes // 4 + 64], F32, name="zeros0", offset=0, align_bytes=64),
-            wins.tile([P, (HELD_BYTES - first_bytes) // 4], F32, name="zeros1", offset=first_bytes, align_bytes=64),
-        ]
-        nc.gpsimd.memset(gate_sc[:], 0)
-        nc.vector.memset(up_sc[:], 0)
-        nc.vector.memset(g_rows[:], 0.0)
-        nc.vector.memset(zeros[0][:, 0:64], 0.0)
 
-        def identity_half(i):
-            nc.gpsimd.affine_select(
-                out=ident[:, 64 * i : 64 * (i + 1)],
-                in_=zeros[i][:, 0:64],
-                compare_op=mybir.AluOpType.not_equal,
-                fill=1.0,
-                base=-64 * i,
-                pattern=[[-1, 64]],
-                channel_multiplier=1,
-            )
+        def clear_rest(engine, plane):
+            engine.memset(plane[0:96, :], 0)
 
-        identity_half(0)
-        x_sc = place("x_sc", [P, 2, M // 4], I32, 2 * M)
-        nc.gpsimd.memset(x_sc[:], 0)
-        nc.gpsimd.memset(zeros[1][:, 0:64], 0.0)
-        identity_half(1)
+        nc.gpsimd.memset(planes[1][:], 0)
+        nc.gpsimd.memset(g_rows[:], 0.0)
+        nc.gpsimd.dma_start(out=g_rows[0:4, :].rearrange("t (x r) -> t x r", r=8), in_=g.rearrange("(x t r) -> t x r", t=4, r=8))
+        nc.gpsimd.memset(ident[:], 0.0)
+        nc.gpsimd.affine_select(
+            out=ident[:],
+            in_=ident[:],
+            compare_op=mybir.AluOpType.not_equal,
+            fill=1.0,
+            base=0,
+            pattern=[[-1, P]],
+            channel_multiplier=1,
+        )
+        clear_rest(nc.vector, gate_sc)
+        clear_rest(nc.vector, up_sc)
+        clear_rest(nc.vector, planes[0][:, 2, :])
 
         def load_scales(plane, scales):
-            for q in range(4):
-                nc.sync.dma_start(out=plane[32 * q : 32 * q + 8, :], in_=scales[:, 4 * q : 4 * q + 4, :].bitcast(I32))
+            nc.sync.dma_start(out=plane[96:P, :], in_=scales.rearrange("a z t -> (a z) t").bitcast(I32))
 
-        def load_words(name, words, a):
-            win = place(name, [P, T], I32, 4 * T)
+        def load_words(name, words, a, at):
+            win = place(name, [P, T], I32, at)
             nc.sync.dma_start(out=win[:], in_=words[a].rearrange("p n i -> p (n i)").bitcast(I32))
-            return win
+            return win[:]
 
         x_all = x_words.rearrange("a p n i -> p a (n i)").bitcast(I32)
-
-        def load_x(mh, a0, passes, part):
-            nc.sync.dma_start(out=part[:], in_=x_all[:, a0 : a0 + passes, HALF * mh : HALF * (mh + 1)])
-            for a in range(passes):
-                x_w[mh, a0 + a] = part[:, a, :]
-
         x_w = {}
 
+        def load_x(mh, at):
+            part = place("x_w%d" % mh, [P, 2, HALF], I32, at)
+            nc.sync.dma_start(out=part[:], in_=x_all[:, :, HALF * mh : HALF * (mh + 1)])
+            for a in range(2):
+                x_w[mh, a] = part[:, a, :]
+
         nc.sync.dma_start(offsets[:], offs)
-        load_x(0, 0, 1, keep.tile([P, 1, HALF], I32, name="x_w00", align_bytes=64))
         load_scales(gate_sc, tab_scales)
         load_scales(up_sc, tab2_scales)
-        nc.sync.dma_start(out=g_rows[0:4, :].rearrange("t (x r) -> t x r", r=8), in_=g.rearrange("(x t r) -> t x r", t=4, r=8))
-        gate_win = [load_words("gate_win%d" % a, tab_words, a) for a in range(2)]
-        for q in range(4):
-            nc.sync.dma_start(
-                out=x_sc[32 * q : 32 * q + 4, :, :],
-                in_=x_scales[:, 4 * q : 4 * q + 4, :].rearrange("a r c -> r a c").bitcast(I32),
-            )
-        sizes.append(256)
-        second_pass_at = sum(sizes)
-        load_x(0, 1, 1, place("x_w01", [P, 1, HALF], I32, 4 * HALF))
-        up_win = [load_words("up_win0", tab2_words, 0)]
-        load_x(1, 0, 2, place("x_w1", [P, 2, HALF], I32, 8 * HALF))
-        up_win.append(load_words("up_win1", tab2_words, 1))
-        wd_raw = {}
-        raw_at = {}
-        for u in range(2):
-            rows = wdT[2 * P * u : 2 * P * (u + 1), :].rearrange("(p i) t -> p i t", i=2)
-            for c in range(2):
-                raw_at[u, c] = sum(sizes)
-                wd_raw[u, c] = place("wd_raw%d%d" % (u, c), [P, 2, T // 2], F32, 4 * T)
-                nc.sync.dma_start(out=wd_raw[u, c][:], in_=rows[:, :, T // 2 * c : T // 2 * (c + 1)])
-        p_all = place("p_all", [P, M], F32, 4 * M)
-        nc.sync.dma_start(out=p_all[:], in_=p.partition_broadcast(P))
+        load_scales(planes[0][:, 2, :], x_scales)
+        gate_win = [load_words("gate_win%d" % a, tab_words, a, GATE_AT[a]) for a in range(2)]
+        load_x(0, X0_AT)
 
-        def pick_scales(name, plane):
-            listed = keep.tile([P, S], U8, name=name + "_listed", align_bytes=64)
+        def pick_scales(listed, plane):
             nc.vector.tensor_copy(out=listed[:], in_=plane[:].bitcast(U8).indirect(offsets[:]))
             return listed
 
-        def order_scales(picked, listed):
+        def order_scales(which, listed):
             nc.vector.tensor_copy(
-                out=picked[:].rearrange("p (b t q w) -> p b t q w", b=2, t=4, w=2),
+                out=planes[0][:, which, :].rearrange("p (b t q w) -> p b t q w", b=2, t=4, w=2),
                 in_=listed[:].bitcast(I32).rearrange("p (b q t w) -> p b t q w", b=2, t=4, w=2),
             )
-            return [picked[:, P * b : P * (b + 1)] for b in range(2)]
+
+        def carry_scales():
+            for a in range(2):
+                for q in range(3 + a):
+                    row = 96 + 16 * a + 4 * q
+                    to = 32 * q + FIRST_ROW[a]
+                    nc.sync.dma_start(out=planes[a][to : to + 4, :, :], in_=planes[0][row : row + 4, :, :])
 
         def pick_half(picked, win, b):
             nc.vector.tensor_copy(
@@ -138,41 +122,52 @@ def tile_list_routed_swiglu_expert_kernel(
             )
             return picked[:]
 
-        def pick_all(name, win, dtype):
-            picked = keep.tile([P, 2, HALF], dtype, name=name, align_bytes=64)
+        def pick_all(picked, win):
             nc.vector.tensor_copy(
                 out=picked[:].bitcast(U32).rearrange("p b (t q r) -> p b q t r", t=4, r=8),
                 in_=win.bitcast(U32).indirect(offsets[:]),
             )
             return [picked[:, b, :] for b in range(2)]
 
-        gate_listed = pick_scales("gate_s", gate_sc)
-        up_listed = pick_scales("up_s", up_sc)
-        gate_s = order_scales(head.tile([P, S // 4], I32, name="gate_s", offset=0, align_bytes=64), gate_listed)
+        gate_listed = pick_scales(keep.tile([P, S], U8, name="gate_listed", align_bytes=64), gate_sc)
+        up_win = [load_words("up_win0", tab2_words, 0, UP_AT[0])]
+        up_listed = pick_scales(place("up_listed", [P, S], U8, LISTED_AT), up_sc)
+        gate_s, up_s = 0, 1
+        order_scales(gate_s, gate_listed)
         g_ps = bank(7, [P, 4, P])
         for b in range(2):
             nc.tensor.transpose(g_ps[:, b, :], g_rows[:, b * P : (b + 1) * P], ident[:])
-        gain = head.tile([P, 2, 4], F32, name="gain", offset=S, align_bytes=64)
+        gain = keep.tile([P, 2, 4], F32, name="gain", align_bytes=64)
         nc.vector.tensor_copy(out=gain[:], in_=g_ps[:, 0:2, 0:4])
+        order_scales(up_s, up_listed)
+        carry_scales()
 
-        up_s = order_scales(keep.tile([P, S // 4], I32, name="up_s", align_bytes=64), up_listed)
         def half_tile(name):
             return keep.tile([P, HALF], I32, name=name, align_bytes=64)
 
-        gate_w = {(a, b): pick_half(half_tile("gate_w%d%d" % (a, b)), gate_win[a][:], b) for a, b in ((0, 0), (1, 0), (1, 1))}
-        on_second_window = wins.tile([P, HALF], I32, name="gate_w01", offset=first_bytes - 4 * T, align_bytes=64)
-        gate_w[0, 1] = pick_half(on_second_window, gate_win[0][:], 1)
-        up_w = {(0, b): half for b, half in enumerate(pick_all("up_w0", up_win[0][:], I32))}
+        gate_w = {(0, b): half for b, half in enumerate(pick_all(place("gate_w0", [P, 2, HALF], I32, LISTED_AT), gate_win[0]))}
+        up_win.append(load_words("up_win1", tab2_words, 1, UP_AT[1]))
         for b in range(2):
-            up_w[1, b] = pick_half(half_tile("up_w1%d" % b), up_win[1][:], b)
+            gate_w[1, b] = pick_half(half_tile("gate_w1%d" % b), gate_win[1], b)
+        load_x(1, X1_AT)
+        up_w = {(0, b): half for b, half in enumerate(pick_all(keep.tile([P, 2, HALF], I32, name="up_w0", align_bytes=64), up_win[0]))}
+        for b in range(2):
+            up_w[1, b] = pick_half(half_tile("up_w1%d" % b), up_win[1], b)
+
+        wd_raw = {}
+        for u in range(2):
+            rows = wdT[2 * P * u : 2 * P * (u + 1), :].rearrange("(p i) t -> p i t", i=2)
+            for c in range(2):
+                wd_raw[u, c] = place("wd_raw%d%d" % (u, c), [P, 2, T // 2], F32, RAW_AT[u, c])
+                nc.sync.dma_start(out=wd_raw[u, c][:], in_=rows[:, :, T // 2 * c : T // 2 * (c + 1)])
 
         def first_pass(dst, a, words, scales, b, t, m0, width, opens=0):
             nc.tensor.matmul_mx(
                 out=dst,
                 lhsT=words[a, b][:, P * t : P * (t + 1)].bitcast(FP8X4),
-                lhsT_scale=scales[b].bitcast(U8)[4 * a :, P * t : P * (t + 1)],
+                lhsT_scale=planes[a][FIRST_ROW[a] :, scales, :].bitcast(U8)[:, HALF * b + P * t : HALF * b + P * (t + 1)],
                 rhs=x_w[m0 // HALF, a][:, m0 % HALF : m0 % HALF + width].bitcast(FP8X4),
-                rhs_scale=x_sc[:, a, :].bitcast(U8)[:, m0 : m0 + width],
+                rhs_scale=planes[a][FIRST_ROW[a] :, 2, :].bitcast(U8)[:, m0 : m0 + width],
                 start=(a == opens),
                 stop=(a != opens),
             )
@@ -183,8 +178,7 @@ def tile_list_routed_swiglu_expert_kernel(
         h_c = {key: keep.tile([P, HALF], U32, name="h_c%d%d" % key, align_bytes=64) for key in quarters[3:]}
         h_s = {key: keep.tile([P, HALF], U8, name="h_s%d%d" % key, align_bytes=64) for key in quarters}
 
-        last_silu_at = sum(sizes)
-        last_silu = place("last_silu", [P, HALF], F32, 4 * HALF)
+        last_silu = place("last_silu", [P, HALF], F32, LAST_SILU_AT)
 
         def activate(mh, b, t, sums):
             plain = last_silu[:] if (mh, b, t) == (1, 1, 3) else act[mh, b][:, t, :]
@@ -219,8 +213,7 @@ def tile_list_routed_swiglu_expert_kernel(
                 out=h_c[mh, b][:].bitcast(FP8X4), scales=h_s[mh, b][:], in_=h_bf[mh, b].rearrange("p c w -> p (c w)")
             )
 
-        pairs_at = [sum(sizes) + 4 * T * u for u in range(2)]
-        wd_pair = [place("wd_pair%d" % u, [P, T, 2], BF16, 4 * T) for u in range(2)]
+        wd_pair = [place("wd_pair%d" % u, [P, T, 2], BF16, PAIR_AT[u]) for u in range(2)]
         shared = keep.tile([P, 6 * HALF], BF16, name="shared", align_bytes=64)
         wd_bf = [
             shared[:, 2 * HALF : 6 * HALF].rearrange("p (b c) -> p b c", b=2),
@@ -236,7 +229,7 @@ def tile_list_routed_swiglu_expert_kernel(
             )
 
         def pick_wd(u):
-            return pick_all("wd_picked%d" % u, wd_pair[u][:].rearrange("p t i -> p (t i)"), F32)
+            return pick_all(keep.tile([P, 2, HALF], F32, name="wd_picked%d" % u, align_bytes=64), wd_pair[u][:].rearrange("p t i -> p (t i)"))
 
         def turn_wd(u, picked, banks):
             for b in range(2):
@@ -301,7 +294,9 @@ def tile_list_routed_swiglu_expert_kernel(
         second = [up_product(0, 1, mc, mc) for mc in range(4)]
         for mc in range(3):
             make_h(0, 1, mc, second[mc])
-        h_c[0, 0] = wins.tile([P, HALF], U32, name="h_c00", offset=second_pass_at, align_bytes=64)
+        h_c[0, 0] = place("h_c00", [P, HALF], U32, X0_AT + 4 * HALF)
+        p_all = place("p_all", [P, M], F32, P_AT)
+        nc.sync.dma_start(out=p_all[:], in_=p.partition_broadcast(P))
         quantize_h(0, 0)
         make_h(0, 1, 3, second[3])
         last_gate = [gate_product(1, 1, t, 4 + t) for t in range(4)]
@@ -312,16 +307,16 @@ def tile_list_routed_swiglu_expert_kernel(
         for t in range(2, 4):
             activate(1, 1, t, last_gate[t])
         picked = pick_wd(0)
-        h_c[0, 1] = wins.tile([P, HALF], U32, name="h_c01", offset=raw_at[0, 1], align_bytes=64)
+        h_c[0, 1] = place("h_c01", [P, HALF], U32, RAW_AT[0, 1])
         quantize_h(0, 1)
-        h_bf[1, 0] = wins.tile([P, 4, 4 * P], BF16, name="h_bf10", offset=pairs_at[0], align_bytes=64)[:]
+        h_bf[1, 0] = place("h_bf10", [P, 4, 4 * P], BF16, PAIR_AT[0])[:]
         third = [up_product(1, 0, mc, mc) for mc in range(4)]
         turn_wd(0, picked, (4, 5))
         for mc in range(4):
             make_h(1, 0, mc, third[mc])
         fourth = [up_product(1, 1, mc, mc) for mc in range(4)]
         picked = pick_wd(1)
-        h_c[1, 0] = wins.tile([P, HALF], U32, name="h_c10", offset=last_silu_at, align_bytes=64)
+        h_c[1, 0] = place("h_c10", [P, HALF], U32, LAST_SILU_AT)
         quantize_h(1, 0)
         turn_wd(1, picked, (6, 7))
         h_bf[1, 1] = shared[:, 0 : 4 * HALF].rearrange("p (c w) -> p c w", c=4)

@@ -18,18 +18,20 @@ SILU = mybir.ActivationFunctionType.Silu
 
 P = 128
 HALF = 512
-FIRST_ROW = (12, 0)
+UP_ROW = (12, 0)
 ROW = 4 * T
 
-GATE_AT = (0, 2 * ROW - 4 * HALF)
-X1_AT = 2 * ROW
-UP_AT = (X1_AT + 8 * HALF + ROW, GATE_AT[0])
-P_AT = UP_AT[0] + ROW
-X0_AT = P_AT + 4 * HALF
+GATE_AT = (0, ROW)
+HELD_AT = GATE_AT[1] + 2 * ROW
+X1_AT = HELD_AT + ROW
+X01_AT = X1_AT + 8 * HALF
+UP_AT = (HELD_AT, X01_AT + 4 * HALF)
+P_AT = UP_AT[1] + ROW
+X0_AT = P_AT
 LAST_SILU_AT = X0_AT + 8 * HALF
+GATE_SC_AT = LAST_SILU_AT + 4 * HALF + 2 * ROW
 PAIR_AT = (LAST_SILU_AT + 4 * HALF, LAST_SILU_AT + 4 * HALF + ROW)
-LISTED_AT = PAIR_AT[1] + ROW
-RAW_AT = {(0, 0): X1_AT + 8 * HALF, (0, 1): ROW, (1, 0): UP_AT[0], (1, 1): UP_AT[1]}
+RAW_AT = {(0, 0): GATE_AT[1] + ROW - 64, (0, 1): GATE_AT[0], (1, 0): UP_AT[0], (1, 1): UP_AT[1]}
 
 
 def tile_list_routed_swiglu_expert_kernel(
@@ -49,16 +51,18 @@ def tile_list_routed_swiglu_expert_kernel(
 
         offsets = keep.tile([P, S // 16], U16, name="offsets")
         ident = keep.tile([P, P], F32, name="ident")
-        gate_sc = place("gate_sc", [P, T // 4], I32, UP_AT[0])
-        up_sc = keep.tile([P, T // 4], I32, name="up_sc", align_bytes=64)
-        planes = [keep.tile([P, 3, S // 4], I32, name="planes%d" % a, align_bytes=64) for a in range(2)]
+        gate_sc = place("gate_sc", [P, T // 4], I32, GATE_SC_AT)
+        up_sc = place("up_sc", [P, (UP_AT[1] - UP_AT[0]) // 4], I32, UP_AT[0])[:, 0 : T // 4]
+        x_sc = keep.tile([P, 2, M // 4], I32, name="x_sc", align_bytes=64)
         g_rows = keep.tile([P, 2 * P], F32, name="g_rows")
-
-        def clear_rest(engine, plane):
-            engine.memset(plane[0:96, :], 0)
-
-        nc.gpsimd.memset(planes[1][:], 0)
-        nc.gpsimd.memset(g_rows[:], 0.0)
+        zeros = place("zeros", [P, (GATE_AT[1] + ROW) // 4], F32, GATE_AT[0])
+        up_second = keep.tile([P, S // 4], I32, name="up_second", align_bytes=64)
+        nc.gpsimd.memset(zeros[:, 0 : 2 * P], 0.0)
+        nc.gpsimd.memset(up_sc[0:96, :], 0)
+        nc.gpsimd.memset(up_second[:], 0)
+        nc.vector.memset(gate_sc[:], 0)
+        nc.vector.tensor_copy(out=g_rows[:], in_=zeros[:, 0 : 2 * P])
+        nc.vector.memset(x_sc[:], 0)
         nc.gpsimd.dma_start(out=g_rows[0:4, :].rearrange("t (x r) -> t x r", r=8), in_=g.rearrange("(x t r) -> t x r", t=4, r=8))
         nc.gpsimd.memset(ident[:], 0.0)
         nc.gpsimd.affine_select(
@@ -70,50 +74,45 @@ def tile_list_routed_swiglu_expert_kernel(
             pattern=[[-1, P]],
             channel_multiplier=1,
         )
-        clear_rest(nc.vector, gate_sc)
-        clear_rest(nc.vector, up_sc)
-        clear_rest(nc.vector, planes[0][:, 2, :])
-
-        def load_scales(plane, scales):
-            nc.sync.dma_start(out=plane[96:P, :], in_=scales.rearrange("a z t -> (a z) t").bitcast(I32))
 
         def load_words(name, words, a, at):
             win = place(name, [P, T], I32, at)
             nc.sync.dma_start(out=win[:], in_=words[a].rearrange("p n i -> p (n i)").bitcast(I32))
-            return win[:]
+            return win
 
         x_all = x_words.rearrange("a p n i -> p a (n i)").bitcast(I32)
         x_w = {}
 
-        def load_x(mh, at):
-            part = place("x_w%d" % mh, [P, 2, HALF], I32, at)
-            nc.sync.dma_start(out=part[:], in_=x_all[:, :, HALF * mh : HALF * (mh + 1)])
-            for a in range(2):
-                x_w[mh, a] = part[:, a, :]
+        def load_x(mh, a0, part):
+            passes = part.shape[1]
+            nc.sync.dma_start(out=part[:], in_=x_all[:, a0 : a0 + passes, HALF * mh : HALF * (mh + 1)])
+            for a in range(passes):
+                x_w[mh, a0 + a] = part[:, a, :]
 
         nc.sync.dma_start(offsets[:], offs)
-        load_scales(gate_sc, tab_scales)
-        load_scales(up_sc, tab2_scales)
-        load_scales(planes[0][:, 2, :], x_scales)
+        nc.sync.dma_start(out=up_sc[96:P, :], in_=tab2_scales.rearrange("a z t -> (a z) t").bitcast(I32))
+        load_x(0, 0, place("x_w00", [P, 1, HALF], I32, X0_AT))
+        for q in range(4):
+            nc.sync.dma_start(out=gate_sc[32 * q : 32 * q + 8, :], in_=tab_scales[:, 4 * q : 4 * q + 4, :].bitcast(I32))
         gate_win = [load_words("gate_win%d" % a, tab_words, a, GATE_AT[a]) for a in range(2)]
-        load_x(0, X0_AT)
+        for q in range(4):
+            nc.sync.dma_start(
+                out=x_sc[32 * q : 32 * q + 4, :, :],
+                in_=x_scales[:, 4 * q : 4 * q + 4, :].rearrange("a r c -> r a c").bitcast(I32),
+            )
+        load_x(0, 1, place("x_w01", [P, 1, HALF], I32, X01_AT))
+        up_win = [load_words("up_win0", tab2_words, 0, UP_AT[0])]
+        load_x(1, 0, place("x_w1", [P, 2, HALF], I32, X1_AT))
 
         def pick_scales(listed, plane):
-            nc.vector.tensor_copy(out=listed[:], in_=plane[:].bitcast(U8).indirect(offsets[:]))
+            nc.vector.tensor_copy(out=listed[:], in_=plane.bitcast(U8).indirect(offsets[:]))
             return listed
 
-        def order_scales(which, listed):
+        def order_scales(picked, listed):
             nc.vector.tensor_copy(
-                out=planes[0][:, which, :].rearrange("p (b t q w) -> p b t q w", b=2, t=4, w=2),
+                out=picked[:].rearrange("p (b t q w) -> p b t q w", b=2, t=4, w=2),
                 in_=listed[:].bitcast(I32).rearrange("p (b q t w) -> p b t q w", b=2, t=4, w=2),
             )
-
-        def carry_scales():
-            for a in range(2):
-                for q in range(3 + a):
-                    row = 96 + 16 * a + 4 * q
-                    to = 32 * q + FIRST_ROW[a]
-                    nc.sync.dma_start(out=planes[a][to : to + 4, :, :], in_=planes[0][row : row + 4, :, :])
 
         def pick_half(picked, win, b):
             nc.vector.tensor_copy(
@@ -122,52 +121,66 @@ def tile_list_routed_swiglu_expert_kernel(
             )
             return picked[:]
 
-        def pick_all(picked, win):
+        def pick_all(name, win, dtype):
+            picked = keep.tile([P, 2, HALF], dtype, name=name, align_bytes=64)
             nc.vector.tensor_copy(
                 out=picked[:].bitcast(U32).rearrange("p b (t q r) -> p b q t r", t=4, r=8),
                 in_=win.bitcast(U32).indirect(offsets[:]),
             )
             return [picked[:, b, :] for b in range(2)]
 
-        gate_listed = pick_scales(keep.tile([P, S], U8, name="gate_listed", align_bytes=64), gate_sc)
-        up_win = [load_words("up_win0", tab2_words, 0, UP_AT[0])]
-        up_listed = pick_scales(place("up_listed", [P, S], U8, LISTED_AT), up_sc)
-        gate_s, up_s = 0, 1
-        order_scales(gate_s, gate_listed)
+        up_listed = pick_scales(keep.tile([P, S], U8, name="up_listed", align_bytes=64), up_sc)
+        gate_listed = pick_scales(place("gate_listed", [P, S], U8, UP_AT[1]), gate_sc[:])
+        up_first = place("up_first", [P, S // 4], I32, GATE_SC_AT)
+        order_scales(up_first, up_listed)
+        gate_both = place("gate_both", [P, S // 4], I32, GATE_SC_AT + S)
+        order_scales(gate_both, gate_listed)
+
+        def carry_scales(a, plane):
+            for q in range(3 + a):
+                row = 96 + 16 * a + 4 * q
+                to = 32 * q + UP_ROW[a]
+                nc.sync.dma_start(out=plane[to : to + 4, :], in_=up_first[row : row + 4, :])
+            return plane[UP_ROW[a] :, :].bitcast(U8)
+
+        up_s = [carry_scales(0, up_first)]
+        up_win.append(load_words("up_win1", tab2_words, 1, UP_AT[1]))
+        up_s.append(carry_scales(1, up_second))
+        gate_s = [gate_both[4 * a :, :].bitcast(U8) for a in range(2)]
         g_ps = bank(7, [P, 4, P])
         for b in range(2):
             nc.tensor.transpose(g_ps[:, b, :], g_rows[:, b * P : (b + 1) * P], ident[:])
-        gain = keep.tile([P, 2, 4], F32, name="gain", align_bytes=64)
-        nc.vector.tensor_copy(out=gain[:], in_=g_ps[:, 0:2, 0:4])
-        order_scales(up_s, up_listed)
-        carry_scales()
 
         def half_tile(name):
             return keep.tile([P, HALF], I32, name=name, align_bytes=64)
 
-        gate_w = {(0, b): half for b, half in enumerate(pick_all(place("gate_w0", [P, 2, HALF], I32, LISTED_AT), gate_win[0]))}
-        up_win.append(load_words("up_win1", tab2_words, 1, UP_AT[1]))
-        for b in range(2):
-            gate_w[1, b] = pick_half(half_tile("gate_w1%d" % b), gate_win[1], b)
-        load_x(1, X1_AT)
-        up_w = {(0, b): half for b, half in enumerate(pick_all(keep.tile([P, 2, HALF], I32, name="up_w0", align_bytes=64), up_win[0]))}
-        for b in range(2):
-            up_w[1, b] = pick_half(half_tile("up_w1%d" % b), up_win[1], b)
-
+        gate_w = {(a, b): pick_half(half_tile("gate_w%d%d" % (a, b)), gate_win[a][:], b) for a, b in ((0, 0), (1, 0), (1, 1))}
+        on_second_window = place("gate_w01", [P, HALF], I32, GATE_AT[1])
+        gain = place("gain", [P, 2, 4], F32, GATE_AT[1] + ROW - 128)
+        nc.vector.tensor_copy(out=gain[:], in_=g_ps[:, 0:2, 0:4])
+        gate_w[0, 1] = pick_half(on_second_window, gate_win[0][:], 1)
         wd_raw = {}
-        for u in range(2):
+
+        def load_wd(u, c):
             rows = wdT[2 * P * u : 2 * P * (u + 1), :].rearrange("(p i) t -> p i t", i=2)
-            for c in range(2):
-                wd_raw[u, c] = place("wd_raw%d%d" % (u, c), [P, 2, T // 2], F32, RAW_AT[u, c])
-                nc.sync.dma_start(out=wd_raw[u, c][:], in_=rows[:, :, T // 2 * c : T // 2 * (c + 1)])
+            wd_raw[u, c] = place("wd_raw%d%d" % (u, c), [P, 2, T // 2], F32, RAW_AT[u, c])
+            nc.sync.dma_start(out=wd_raw[u, c][:], in_=rows[:, :, T // 2 * c : T // 2 * (c + 1)])
+
+        load_wd(0, 0)
+        load_wd(0, 1)
+        up_w = {(0, b): half for b, half in enumerate(pick_all("up_w0", up_win[0][:], I32))}
+        load_wd(1, 0)
+        for b in range(2):
+            up_w[1, b] = pick_half(half_tile("up_w1%d" % b), up_win[1][:], b)
+        load_wd(1, 1)
 
         def first_pass(dst, a, words, scales, b, t, m0, width, opens=0):
             nc.tensor.matmul_mx(
                 out=dst,
                 lhsT=words[a, b][:, P * t : P * (t + 1)].bitcast(FP8X4),
-                lhsT_scale=planes[a][FIRST_ROW[a] :, scales, :].bitcast(U8)[:, HALF * b + P * t : HALF * b + P * (t + 1)],
+                lhsT_scale=scales[a][:, HALF * b + P * t : HALF * b + P * (t + 1)],
                 rhs=x_w[m0 // HALF, a][:, m0 % HALF : m0 % HALF + width].bitcast(FP8X4),
-                rhs_scale=planes[a][FIRST_ROW[a] :, 2, :].bitcast(U8)[:, m0 : m0 + width],
+                rhs_scale=x_sc[:, a, :].bitcast(U8)[:, m0 : m0 + width],
                 start=(a == opens),
                 stop=(a != opens),
             )
@@ -178,10 +191,10 @@ def tile_list_routed_swiglu_expert_kernel(
         h_c = {key: keep.tile([P, HALF], U32, name="h_c%d%d" % key, align_bytes=64) for key in quarters[3:]}
         h_s = {key: keep.tile([P, HALF], U8, name="h_s%d%d" % key, align_bytes=64) for key in quarters}
 
-        last_silu = place("last_silu", [P, HALF], F32, LAST_SILU_AT)
+        apart = {(1, 1, 3): place("last_silu", [P, HALF], F32, LAST_SILU_AT)}
 
         def activate(mh, b, t, sums):
-            plain = last_silu[:] if (mh, b, t) == (1, 1, 3) else act[mh, b][:, t, :]
+            plain = apart[mh, b, t][:] if (mh, b, t) in apart else act[mh, b][:, t, :]
             nc.scalar.activation(out=plain, in_=sums[:], func=SILU)
             nc.gpsimd.tensor_scalar(
                 out=act[mh, b][:, t, :], in0=plain, scalar1=gain[:, b, t : t + 1], scalar2=0.0, op0=MULT, op1=ADD
@@ -229,7 +242,7 @@ def tile_list_routed_swiglu_expert_kernel(
             )
 
         def pick_wd(u):
-            return pick_all(keep.tile([P, 2, HALF], F32, name="wd_picked%d" % u, align_bytes=64), wd_pair[u][:].rearrange("p t i -> p (t i)"))
+            return pick_all("wd_picked%d" % u, wd_pair[u][:].rearrange("p t i -> p (t i)"), F32)
 
         def turn_wd(u, picked, banks):
             for b in range(2):
@@ -294,7 +307,7 @@ def tile_list_routed_swiglu_expert_kernel(
         second = [up_product(0, 1, mc, mc) for mc in range(4)]
         for mc in range(3):
             make_h(0, 1, mc, second[mc])
-        h_c[0, 0] = place("h_c00", [P, HALF], U32, X0_AT + 4 * HALF)
+        h_c[0, 0] = place("h_c00", [P, HALF], U32, X01_AT)
         p_all = place("p_all", [P, M], F32, P_AT)
         nc.sync.dma_start(out=p_all[:], in_=p.partition_broadcast(P))
         quantize_h(0, 0)
@@ -304,6 +317,7 @@ def tile_list_routed_swiglu_expert_kernel(
             activate(1, 1, t, last_gate[t])
         for c in range(2):
             cast_wd(1, c)
+        apart[1, 1, 2] = place("silu112", [P, HALF], F32, RAW_AT[1, 1])
         for t in range(2, 4):
             activate(1, 1, t, last_gate[t])
         picked = pick_wd(0)

@@ -22,16 +22,16 @@ UP_ROW = (12, 0)
 ROW = 4 * T
 
 GATE_AT = (0, ROW)
-HELD_AT = GATE_AT[1] + 2 * ROW
-X1_AT = HELD_AT + ROW
-X01_AT = X1_AT + 8 * HALF
-UP_AT = (HELD_AT, X01_AT + 4 * HALF)
-P_AT = UP_AT[1] + ROW
-X0_AT = P_AT
-LAST_SILU_AT = X0_AT + 8 * HALF
+GAIN_AT = GATE_AT[1] + 4 * HALF
+X0_AT = 2 * ROW + 8 * HALF
+P_AT = X0_AT - 4 * HALF
+X1_AT = X0_AT + 8 * HALF
+UP_AT = (X1_AT + 8 * HALF, X1_AT + 8 * HALF + ROW)
+LAST_SILU_AT = UP_AT[1] + ROW + 4 * HALF
 GATE_SC_AT = LAST_SILU_AT + 4 * HALF + 2 * ROW
 PAIR_AT = (LAST_SILU_AT + 4 * HALF, LAST_SILU_AT + 4 * HALF + ROW)
-RAW_AT = {(0, 0): GATE_AT[1] + ROW - 64, (0, 1): GATE_AT[0], (1, 0): UP_AT[0], (1, 1): UP_AT[1]}
+LISTED_AT = GATE_SC_AT + 4 * HALF + S
+RAW_AT = {(0, 0): LISTED_AT + 64, (0, 1): GATE_AT[0], (1, 0): UP_AT[1] + 4 * HALF, (1, 1): UP_AT[0]}
 
 
 def tile_list_routed_swiglu_expert_kernel(
@@ -52,14 +52,12 @@ def tile_list_routed_swiglu_expert_kernel(
         offsets = keep.tile([P, S // 16], U16, name="offsets")
         ident = keep.tile([P, P], F32, name="ident")
         gate_sc = place("gate_sc", [P, T // 4], I32, GATE_SC_AT)
-        up_sc = place("up_sc", [P, (UP_AT[1] - UP_AT[0]) // 4], I32, UP_AT[0])[:, 0 : T // 4]
+        up_sc = place("up_sc", [P, (UP_AT[1] + ROW - X1_AT) // 4], I32, X1_AT)[:, 0 : T // 4]
         x_sc = keep.tile([P, 2, M // 4], I32, name="x_sc", align_bytes=64)
         g_rows = keep.tile([P, 2 * P], F32, name="g_rows")
-        zeros = place("zeros", [P, (GATE_AT[1] + ROW) // 4], F32, GATE_AT[0])
-        up_second = keep.tile([P, S // 4], I32, name="up_second", align_bytes=64)
+        zeros = place("zeros", [P, (X1_AT - GATE_AT[1]) // 4], F32, GATE_AT[1])
         nc.gpsimd.memset(zeros[:, 0 : 2 * P], 0.0)
         nc.gpsimd.memset(up_sc[0:96, :], 0)
-        nc.gpsimd.memset(up_second[:], 0)
         nc.vector.memset(gate_sc[:], 0)
         nc.vector.tensor_copy(out=g_rows[:], in_=zeros[:, 0 : 2 * P])
         nc.vector.memset(x_sc[:], 0)
@@ -91,18 +89,23 @@ def tile_list_routed_swiglu_expert_kernel(
 
         nc.sync.dma_start(offsets[:], offs)
         nc.sync.dma_start(out=up_sc[96:P, :], in_=tab2_scales.rearrange("a z t -> (a z) t").bitcast(I32))
-        load_x(0, 0, place("x_w00", [P, 1, HALF], I32, X0_AT))
+        gate_win = [load_words("gate_win0", tab_words, 0, GATE_AT[0])]
         for q in range(4):
             nc.sync.dma_start(out=gate_sc[32 * q : 32 * q + 8, :], in_=tab_scales[:, 4 * q : 4 * q + 4, :].bitcast(I32))
-        gate_win = [load_words("gate_win%d" % a, tab_words, a, GATE_AT[a]) for a in range(2)]
+        load_x(0, 0, place("x_w0", [P, 2, HALF], I32, X0_AT))
+        gate_win.append(load_words("gate_win1", tab_words, 1, GATE_AT[1]))
         for q in range(4):
             nc.sync.dma_start(
                 out=x_sc[32 * q : 32 * q + 4, :, :],
                 in_=x_scales[:, 4 * q : 4 * q + 4, :].rearrange("a r c -> r a c").bitcast(I32),
             )
-        load_x(0, 1, place("x_w01", [P, 1, HALF], I32, X01_AT))
-        up_win = [load_words("up_win0", tab2_words, 0, UP_AT[0])]
-        load_x(1, 0, place("x_w1", [P, 2, HALF], I32, X1_AT))
+
+        wd_raw = {}
+
+        def load_wd(u, c):
+            rows = wdT[2 * P * u : 2 * P * (u + 1), :].rearrange("(p i) t -> p i t", i=2)
+            wd_raw[u, c] = place("wd_raw%d%d" % (u, c), [P, 2, T // 2], F32, RAW_AT[u, c])
+            nc.sync.dma_start(out=wd_raw[u, c][:], in_=rows[:, :, T // 2 * c : T // 2 * (c + 1)])
 
         def pick_scales(listed, plane):
             nc.vector.tensor_copy(out=listed[:], in_=plane.bitcast(U8).indirect(offsets[:]))
@@ -130,7 +133,9 @@ def tile_list_routed_swiglu_expert_kernel(
             return [picked[:, b, :] for b in range(2)]
 
         up_listed = pick_scales(keep.tile([P, S], U8, name="up_listed", align_bytes=64), up_sc)
-        gate_listed = pick_scales(place("gate_listed", [P, S], U8, UP_AT[1]), gate_sc[:])
+        up_win = [load_words("up_win%d" % a, tab2_words, a, UP_AT[a]) for a in range(2)]
+        load_x(1, 0, place("x_w1", [P, 2, HALF], I32, X1_AT))
+        gate_listed = pick_scales(place("gate_listed", [P, S], U8, LISTED_AT), gate_sc[:])
         up_first = place("up_first", [P, S // 4], I32, GATE_SC_AT)
         order_scales(up_first, up_listed)
         gate_both = place("gate_both", [P, S // 4], I32, GATE_SC_AT + S)
@@ -144,7 +149,9 @@ def tile_list_routed_swiglu_expert_kernel(
             return plane[UP_ROW[a] :, :].bitcast(U8)
 
         up_s = [carry_scales(0, up_first)]
-        up_win.append(load_words("up_win1", tab2_words, 1, UP_AT[1]))
+        load_wd(0, 0)
+        up_second = place("up_second", [P, S // 4], I32, LISTED_AT + 64 - S)
+        nc.gpsimd.memset(up_second[:], 0)
         up_s.append(carry_scales(1, up_second))
         gate_s = [gate_both[4 * a :, :].bitcast(U8) for a in range(2)]
         g_ps = bank(7, [P, 4, P])
@@ -156,22 +163,13 @@ def tile_list_routed_swiglu_expert_kernel(
 
         gate_w = {(a, b): pick_half(half_tile("gate_w%d%d" % (a, b)), gate_win[a][:], b) for a, b in ((0, 0), (1, 0), (1, 1))}
         on_second_window = place("gate_w01", [P, HALF], I32, GATE_AT[1])
-        gain = place("gain", [P, 2, 4], F32, GATE_AT[1] + ROW - 128)
+        gain = place("gain", [P, 2, 4], F32, GAIN_AT)
         nc.vector.tensor_copy(out=gain[:], in_=g_ps[:, 0:2, 0:4])
         gate_w[0, 1] = pick_half(on_second_window, gate_win[0][:], 1)
-        wd_raw = {}
-
-        def load_wd(u, c):
-            rows = wdT[2 * P * u : 2 * P * (u + 1), :].rearrange("(p i) t -> p i t", i=2)
-            wd_raw[u, c] = place("wd_raw%d%d" % (u, c), [P, 2, T // 2], F32, RAW_AT[u, c])
-            nc.sync.dma_start(out=wd_raw[u, c][:], in_=rows[:, :, T // 2 * c : T // 2 * (c + 1)])
-
-        load_wd(0, 0)
         load_wd(0, 1)
-        up_w = {(0, b): half for b, half in enumerate(pick_all("up_w0", up_win[0][:], I32))}
+        up_w = {(a, b): pick_half(half_tile("up_w%d%d" % (a, b)), up_win[a][:], b) for a, b in ((0, 0), (1, 0), (1, 1))}
+        up_w[0, 1] = pick_half(place("up_w01", [P, HALF], I32, UP_AT[1]), up_win[0][:], 1)
         load_wd(1, 0)
-        for b in range(2):
-            up_w[1, b] = pick_half(half_tile("up_w1%d" % b), up_win[1][:], b)
         load_wd(1, 1)
 
         def first_pass(dst, a, words, scales, b, t, m0, width, opens=0):
@@ -206,11 +204,11 @@ def tile_list_routed_swiglu_expert_kernel(
                 first_pass(sums[:], a, gate_w, gate_s, b, t, HALF * mh, HALF, opens)
             return sums
 
-        def up_product(mh, b, mc, i):
+        def up_product(mh, b, mc, i, opens=0):
             sums = bank(i, [P, 4, P])
             for t in range(4):
-                for a in range(2):
-                    first_pass(sums[:, t, :], a, up_w, up_s, b, t, HALF * mh + P * mc, P)
+                for a in (opens, 1 - opens):
+                    first_pass(sums[:, t, :], a, up_w, up_s, b, t, HALF * mh + P * mc, P, opens)
             return sums
 
         def make_h(mh, b, mc, sums):
@@ -298,55 +296,58 @@ def tile_list_routed_swiglu_expert_kernel(
             activate(0, 0, t, gate_product(0, 0, t, t, 1))
         for t in range(4):
             activate(0, 1, t, gate_product(0, 1, t, 4 + t, 1))
-        for t in range(4):
+        for t in range(2):
             activate(1, 0, t, gate_product(1, 0, t, t))
         for c in range(2):
             cast_wd(0, c)
         for mc in range(4):
-            make_h(0, 0, mc, up_product(0, 0, mc, 4 + mc))
-        second = [up_product(0, 1, mc, mc) for mc in range(4)]
+            make_h(0, 0, mc, up_product(0, 0, mc, 2 + mc))
+        second = [up_product(0, 1, mc, (6 + mc) % 8, 1) for mc in range(4)]
         for mc in range(3):
             make_h(0, 1, mc, second[mc])
-        h_c[0, 0] = place("h_c00", [P, HALF], U32, X01_AT)
+        h_c[0, 0] = place("h_c00", [P, HALF], U32, X0_AT + 4 * HALF)
         p_all = place("p_all", [P, M], F32, P_AT)
         nc.sync.dma_start(out=p_all[:], in_=p.partition_broadcast(P))
         quantize_h(0, 0)
         make_h(0, 1, 3, second[3])
-        last_gate = [gate_product(1, 1, t, 4 + t) for t in range(4)]
-        for t in range(2):
-            activate(1, 1, t, last_gate[t])
+        apart[1, 0, 2] = place("silu102", [P, HALF], F32, RAW_AT[0, 1] + 4 * HALF)
+        for t in range(2, 4):
+            activate(1, 0, t, gate_product(1, 0, t, t))
+        last_gate = [gate_product(1, 1, t, 4 + t) for t in range(2)]
+        third = [up_product(1, 0, mc, (6 + mc) % 8) for mc in range(4)]
+        last_gate.extend(gate_product(1, 1, t, t) for t in range(2, 4))
         for c in range(2):
             cast_wd(1, c)
-        apart[1, 1, 2] = place("silu112", [P, HALF], F32, RAW_AT[1, 1])
-        for t in range(2, 4):
-            activate(1, 1, t, last_gate[t])
+            apart[1, 1, 2 * c] = place("silu11%d" % c, [P, HALF], F32, RAW_AT[1, c])
+            for t in range(2 * c, 2 * c + 2):
+                activate(1, 1, t, last_gate[t])
         picked = pick_wd(0)
         h_c[0, 1] = place("h_c01", [P, HALF], U32, RAW_AT[0, 1])
         quantize_h(0, 1)
         h_bf[1, 0] = place("h_bf10", [P, 4, 4 * P], BF16, PAIR_AT[0])[:]
-        third = [up_product(1, 0, mc, mc) for mc in range(4)]
-        turn_wd(0, picked, (4, 5))
         for mc in range(4):
             make_h(1, 0, mc, third[mc])
-        fourth = [up_product(1, 1, mc, mc) for mc in range(4)]
+        fourth = [up_product(1, 1, mc, 4 + mc) for mc in range(2)]
+        turn_wd(0, picked, (2, 3))
+        fourth.extend(up_product(1, 1, mc, 4 + mc) for mc in range(2, 4))
         picked = pick_wd(1)
         h_c[1, 0] = place("h_c10", [P, HALF], U32, LAST_SILU_AT)
         quantize_h(1, 0)
-        turn_wd(1, picked, (6, 7))
+        turn_wd(1, picked, (0, 1))
         h_bf[1, 1] = shared[:, 0 : 4 * HALF].rearrange("p (c w) -> p c w", c=4)
         for mc in range(2):
             make_h(1, 1, mc, fourth[mc])
         quantize_wd(0)
-        early = [down_sums(0, 0, 0, 4)]
+        early = [down_sums(0, 0, 0, 2)]
         for mc in range(2, 4):
             make_h(1, 1, mc, fourth[mc])
-        early.append(down_sums(0, 0, 1, 3))
+        early.append(down_sums(0, 0, 1, 7))
         finish(0, 0, 0, early[0], 1)
         quantize_h(1, 1)
         quantize_wd(1)
         finish(0, 0, 1, early[1], 1)
         for v in range(2):
-            finish(1, 0, v, down_sums(1, 0, v, v), 1)
+            finish(1, 0, v, down_sums(1, 0, v, 4 + v), 1)
         for mh in range(2):
             for v in range(2):
-                finish(mh, 1, v, down_sums(mh, 1, v, (2, 5, 6, 7)[2 * mh + v]), 1 + mh * v)
+                finish(mh, 1, v, down_sums(mh, 1, v, (6, 3, 0, 1)[2 * mh + v]), 1 + mh * v)

@@ -55,7 +55,7 @@ def tile_list_routed_swiglu_expert_kernel(
         up_sc = place("up_sc", [P, (UP_AT[1] + ROW - X1_AT) // 4], I32, X1_AT)[:, 0 : T // 4]
         x_sc = keep.tile([P, 2, M // 4], I32, name="x_sc", align_bytes=64)
         g_rows = keep.tile([P, 2 * P], F32, name="g_rows")
-        zeros = place("zeros", [P, (X1_AT - GATE_AT[1]) // 4], F32, GATE_AT[1])
+        zeros = place("zeros", [P, 2 * ROW // 4], F32, GATE_AT[0])
         nc.gpsimd.memset(zeros[:, 0 : 2 * P], 0.0)
         nc.gpsimd.memset(up_sc[0:96, :], 0)
         nc.vector.memset(gate_sc[:], 0)
@@ -89,11 +89,10 @@ def tile_list_routed_swiglu_expert_kernel(
 
         nc.sync.dma_start(offsets[:], offs)
         nc.sync.dma_start(out=up_sc[96:P, :], in_=tab2_scales.rearrange("a z t -> (a z) t").bitcast(I32))
-        gate_win = [load_words("gate_win0", tab_words, 0, GATE_AT[0])]
+        load_x(0, 0, place("x_w0", [P, 2, HALF], I32, X0_AT))
         for q in range(4):
             nc.sync.dma_start(out=gate_sc[32 * q : 32 * q + 8, :], in_=tab_scales[:, 4 * q : 4 * q + 4, :].bitcast(I32))
-        load_x(0, 0, place("x_w0", [P, 2, HALF], I32, X0_AT))
-        gate_win.append(load_words("gate_win1", tab_words, 1, GATE_AT[1]))
+        gate_win = [load_words("gate_win%d" % a, tab_words, a, GATE_AT[a]) for a in range(2)]
         for q in range(4):
             nc.sync.dma_start(
                 out=x_sc[32 * q : 32 * q + 4, :, :],

@@ -56,11 +56,11 @@ def tile_list_routed_swiglu_expert_kernel(
         x_sc = keep.tile([P, 2, M // 4], I32, name="x_sc", align_bytes=64)
         g_rows = keep.tile([P, 2 * P], F32, name="g_rows")
         zeros = place("zeros", [P, 2 * ROW // 4], F32, GATE_AT[0])
+        nc.gpsimd.memset(gate_sc[:], 0)
         nc.gpsimd.memset(zeros[:, 0 : 2 * P], 0.0)
-        nc.gpsimd.memset(up_sc[0:96, :], 0)
-        nc.vector.memset(gate_sc[:], 0)
+        nc.vector.memset(up_sc[0:96, :], 0)
         nc.vector.tensor_copy(out=g_rows[:], in_=zeros[:, 0 : 2 * P])
-        nc.vector.memset(x_sc[:], 0)
+        nc.gpsimd.memset(x_sc[:], 0)
         nc.gpsimd.dma_start(out=g_rows[0:4, :].rearrange("t (x r) -> t x r", r=8), in_=g.rearrange("(x t r) -> t x r", t=4, r=8))
         nc.gpsimd.memset(ident[:], 0.0)
         nc.gpsimd.affine_select(

@@ -57,11 +57,10 @@ def tile_list_routed_swiglu_expert_kernel(
         g_rows = keep.tile([P, 2 * P], F32, name="g_rows")
         zeros = place("zeros", [P, 2 * ROW // 4], F32, GATE_AT[0])
         nc.gpsimd.memset(gate_sc[:], 0)
+        nc.gpsimd.memset(up_sc[0:96, :], 0)
         nc.gpsimd.memset(zeros[:, 0 : 2 * P], 0.0)
-        nc.vector.memset(up_sc[0:96, :], 0)
-        nc.vector.tensor_copy(out=g_rows[:], in_=zeros[:, 0 : 2 * P])
+        nc.gpsimd.tensor_copy(out=g_rows[:], in_=zeros[:, 0 : 2 * P])
         nc.gpsimd.memset(x_sc[:], 0)
-        nc.gpsimd.dma_start(out=g_rows[0:4, :].rearrange("t (x r) -> t x r", r=8), in_=g.rearrange("(x t r) -> t x r", t=4, r=8))
         nc.gpsimd.memset(ident[:], 0.0)
         nc.gpsimd.affine_select(
             out=ident[:],
@@ -92,6 +91,7 @@ def tile_list_routed_swiglu_expert_kernel(
         load_x(0, 0, place("x_w0", [P, 2, HALF], I32, X0_AT))
         for q in range(4):
             nc.sync.dma_start(out=gate_sc[32 * q : 32 * q + 8, :], in_=tab_scales[:, 4 * q : 4 * q + 4, :].bitcast(I32))
+        nc.sync.dma_start(out=g_rows[0:4, :].rearrange("t (x r) -> t x r", r=8), in_=g.rearrange("(x t r) -> t x r", t=4, r=8))
         gate_win = [load_words("gate_win%d" % a, tab_words, a, GATE_AT[a]) for a in range(2)]
         for q in range(4):
             nc.sync.dma_start(

from contextlib import ExitStack

import concourse.mybir as mybir

K, T, S, M, N = 1024, 2048, 1024, 1024, 512
FLOPS = 2 * K * S * M * 2 + 2 * S * N * M

F32 = mybir.dt.float32
BF16 = mybir.dt.bfloat16
I32 = mybir.dt.int32
U32 = mybir.dt.uint32
U16 = mybir.dt.uint16
U8 = mybir.dt.uint8
FP8X4 = mybir.dt.float8_e4m3fn_x4
MULT = mybir.AluOpType.mult
ADD = mybir.AluOpType.add
SILU = mybir.ActivationFunctionType.Silu

P = 128
HALF = 512
UP_ROW = (12, 0)
ROW = 4 * T

GATE_AT = (0, ROW)
GAIN_AT = GATE_AT[1] + 4 * HALF
X0_AT = 2 * ROW + 8 * HALF
P_AT = X0_AT - 4 * HALF
X1_AT = X0_AT + 8 * HALF
UP_AT = (X1_AT + 8 * HALF, X1_AT + 8 * HALF + ROW)
LAST_SILU_AT = UP_AT[1] + ROW + 4 * HALF
GATE_SC_AT = LAST_SILU_AT + 4 * HALF + 2 * ROW
PAIR_AT = (LAST_SILU_AT + 4 * HALF, LAST_SILU_AT + 4 * HALF + ROW)
LISTED_AT = GATE_SC_AT + 4 * HALF + S
RAW_AT = {(0, 0): LISTED_AT + 64, (0, 1): GATE_AT[0], (1, 0): UP_AT[1] + 4 * HALF, (1, 1): UP_AT[0]}


def tile_list_routed_swiglu_expert_kernel(
    tc, tab_words, tab_scales, tab2_words, tab2_scales, offs, x_words, x_scales, wdT, g, p, out
):
    nc = tc.nc
    with ExitStack() as ctx:
        keep = ctx.enter_context(tc.tile_pool(name="keep", bufs=1))
        wins = ctx.enter_context(tc.tile_pool(name="wins", bufs=1))
        psum = ctx.enter_context(tc.psum_pool(name="psum", bufs=1))

        def bank(i, shape):
            return psum.tile(shape, F32, name="bank%d" % i)

        def place(name, shape, dtype, at):
            return wins.tile(shape, dtype, name=name, offset=at, align_bytes=64)

        offsets = keep.tile([P, S // 16], U16, name="offsets")
        ident = keep.tile([P, P], F32, name="ident")
        gate_sc = place("gate_sc", [P, T // 4], I32, GATE_SC_AT)
        up_sc = place("up_sc", [P, (UP_AT[1] + ROW - X1_AT) // 4], I32, X1_AT)[:, 0 : T // 4]
        x_sc = keep.tile([P, 2, M // 4], I32, name="x_sc", align_bytes=64)
        g_rows = keep.tile([P, 2 * P], F32, name="g_rows")
        zeros = place("zeros", [P, 2 * ROW // 4], F32, GATE_AT[0])
        nc.gpsimd.memset(gate_sc[:], 0)
        nc.gpsimd.memset(up_sc[0:96, :], 0)
        nc.gpsimd.memset(zeros[:, 0 : 2 * P], 0.0)
        nc.gpsimd.tensor_copy(out=g_rows[:], in_=zeros[:, 0 : 2 * P])
        nc.gpsimd.memset(x_sc[:], 0)
        nc.gpsimd.memset(ident[:], 0.0)
        nc.gpsimd.affine_select(
            out=ident[:],
            in_=ident[:],
            compare_op=mybir.AluOpType.not_equal,
            fill=1.0,
            base=0,
            pattern=[[-1, P]],
            channel_multiplier=1,
        )

        def load_words(name, words, a, at):
            win = place(name, [P, T], I32, at)
            nc.sync.dma_start(out=win[:], in_=words[a].rearrange("p n i -> p (n i)").bitcast(I32))
            return win

        x_all = x_words.rearrange("a p n i -> p a (n i)").bitcast(I32)
        x_w = {}

        def load_x(mh, a0, part):
            passes = part.shape[1]
            nc.sync.dma_start(out=part[:], in_=x_all[:, a0 : a0 + passes, HALF * mh : HALF * (mh + 1)])
            for a in range(passes):
                x_w[mh, a0 + a] = part[:, a, :]

        nc.sync.dma_start(offsets[:], offs)
        nc.sync.dma_start(out=up_sc[96:P, :], in_=tab2_scales.rearrange("a z t -> (a z) t").bitcast(I32))
        load_x(0, 0, place("x_w0", [P, 2, HALF], I32, X0_AT))
        for q in range(4):
            nc.sync.dma_start(out=gate_sc[32 * q : 32 * q + 8, :], in_=tab_scales[:, 4 * q : 4 * q + 4, :].bitcast(I32))
        nc.sync.dma_start(out=g_rows[0:4, :].rearrange("t (x r) -> t x r", r=8), in_=g.rearrange("(x t r) -> t x r", t=4, r=8))
        gate_win = [load_words("gate_win%d" % a, tab_words, a, GATE_AT[a]) for a in range(2)]
        for q in range(4):
            nc.sync.dma_start(
                out=x_sc[32 * q : 32 * q + 4, :, :],
                in_=x_scales[:, 4 * q : 4 * q + 4, :].rearrange("a r c -> r a c").bitcast(I32),
            )

        wd_raw = {}

        def load_wd(u, c):
            rows = wdT[2 * P * u : 2 * P * (u + 1), :].rearrange("(p i) t -> p i t", i=2)
            wd_raw[u, c] = place("wd_raw%d%d" % (u, c), [P, 2, T // 2], F32, RAW_AT[u, c])
            nc.sync.dma_start(out=wd_raw[u, c][:], in_=rows[:, :, T // 2 * c : T // 2 * (c + 1)])

        def pick_scales(listed, plane):
            nc.vector.tensor_copy(out=listed[:], in_=plane.bitcast(U8).indirect(offsets[:]))
            return listed

        def order_scales(picked, listed):
            nc.vector.tensor_copy(
                out=picked[:].rearrange("p (b t q w) -> p b t q w", b=2, t=4, w=2),
                in_=listed[:].bitcast(I32).rearrange("p (b q t w) -> p b t q w", b=2, t=4, w=2),
            )

        def pick_half(picked, win, b):
            nc.vector.tensor_copy(
                out=picked[:].bitcast(U32).rearrange("p (t q r) -> p q t r", t=4, r=8),
                in_=win.bitcast(U32).indirect(offsets[:, 32 * b : 32 * (b + 1)]),
            )
            return picked[:]

        def pick_all(name, win, dtype):
            picked = keep.tile([P, 2, HALF], dtype, name=name, align_bytes=64)
            nc.vector.tensor_copy(
                out=picked[:].bitcast(U32).rearrange("p b (t q r) -> p b q t r", t=4, r=8),
                in_=win.bitcast(U32).indirect(offsets[:]),
            )
            return [picked[:, b, :] for b in range(2)]

        up_listed = pick_scales(keep.tile([P, S], U8, name="up_listed", align_bytes=64), up_sc)
        up_win = [load_words("up_win%d" % a, tab2_words, a, UP_AT[a]) for a in range(2)]
        load_x(1, 0, place("x_w1", [P, 2, HALF], I32, X1_AT))
        gate_listed = pick_scales(place("gate_listed", [P, S], U8, LISTED_AT), gate_sc[:])
        up_first = place("up_first", [P, S // 4], I32, GATE_SC_AT)
        order_scales(up_first, up_listed)
        gate_both = place("gate_both", [P, S // 4], I32, GATE_SC_AT + S)
        order_scales(gate_both, gate_listed)

        def carry_scales(a, plane):
            for q in range(3 + a):
                row = 96 + 16 * a + 4 * q
                to = 32 * q + UP_ROW[a]
                nc.sync.dma_start(out=plane[to : to + 4, :], in_=up_first[row : row + 4, :])
            return plane[UP_ROW[a] :, :].bitcast(U8)

        up_s = [carry_scales(0, up_first)]
        load_wd(0, 0)
        up_second = place("up_second", [P, S // 4], I32, LISTED_AT + 64 - S)
        nc.gpsimd.memset(up_second[:], 0)
        up_s.append(carry_scales(1, up_second))
        gate_s = [gate_both[4 * a :, :].bitcast(U8) for a in range(2)]
        g_ps = bank(7, [P, 4, P])
        for b in range(2):
            nc.tensor.transpose(g_ps[:, b, :], g_rows[:, b * P : (b + 1) * P], ident[:])

        def half_tile(name):
            return keep.tile([P, HALF], I32, name=name, align_bytes=64)

        gate_w = {(a, b): pick_half(half_tile("gate_w%d%d" % (a, b)), gate_win[a][:], b) for a, b in ((0, 0), (1, 0), (1, 1))}
        on_second_window = place("gate_w01", [P, HALF], I32, GATE_AT[1])
        gain = place("gain", [P, 2, 4], F32, GAIN_AT)
        nc.vector.tensor_copy(out=gain[:], in_=g_ps[:, 0:2, 0:4])
        gate_w[0, 1] = pick_half(on_second_window, gate_win[0][:], 1)
        load_wd(0, 1)
        up_w = {(a, b): pick_half(half_tile("up_w%d%d" % (a, b)), up_win[a][:], b) for a, b in ((0, 0), (1, 0), (1, 1))}
        up_w[0, 1] = pick_half(place("up_w01", [P, HALF], I32, UP_AT[1]), up_win[0][:], 1)
        load_wd(1, 0)
        load_wd(1, 1)

        def first_pass(dst, a, words, scales, b, t, m0, width, opens=0):
            nc.tensor.matmul_mx(
                out=dst,
                lhsT=words[a, b][:, P * t : P * (t + 1)].bitcast(FP8X4),
                lhsT_scale=scales[a][:, HALF * b + P * t : HALF * b + P * (t + 1)],
                rhs=x_w[m0 // HALF, a][:, m0 % HALF : m0 % HALF + width].bitcast(FP8X4),
                rhs_scale=x_sc[:, a, :].bitcast(U8)[:, m0 : m0 + width],
                start=(a == opens),
                stop=(a != opens),
            )

        quarters = [(mh, b) for mh in range(2) for b in range(2)]
        act = {key: keep.tile([P, 4, HALF], F32, name="act%d%d" % key) for key in quarters}
        h_bf = {key: keep.tile([P, 4, 4 * P], BF16, name="h_bf%d%d" % key, align_bytes=64)[:] for key in quarters[:2]}
        h_c = {key: keep.tile([P, HALF], U32, name="h_c%d%d" % key, align_bytes=64) for key in quarters[3:]}
        h_s = {key: keep.tile([P, HALF], U8, name="h_s%d%d" % key, align_bytes=64) for key in quarters}

        apart = {(1, 1, 3): place("last_silu", [P, HALF], F32, LAST_SILU_AT)}

        def activate(mh, b, t, sums):
            plain = apart[mh, b, t][:] if (mh, b, t) in apart else act[mh, b][:, t, :]
            nc.scalar.activation(out=plain, in_=sums[:], func=SILU)
            nc.gpsimd.tensor_scalar(
                out=act[mh, b][:, t, :], in0=plain, scalar1=gain[:, b, t : t + 1], scalar2=0.0, op0=MULT, op1=ADD
            )

        def gate_product(mh, b, t, i, opens=0):
            sums = bank(i, [P, HALF])
            for a in (opens, 1 - opens):
                first_pass(sums[:], a, gate_w, gate_s, b, t, HALF * mh, HALF, opens)
            return sums

        def up_product(mh, b, mc, i, opens=0):
            sums = bank(i, [P, 4, P])
            for t in range(4):
                for a in (opens, 1 - opens):
                    first_pass(sums[:, t, :], a, up_w, up_s, b, t, HALF * mh + P * mc, P, opens)
            return sums

        def make_h(mh, b, mc, sums):
            nc.vector.tensor_tensor(
                out=h_bf[mh, b][:, mc, :].rearrange("p (c i t) -> p c t i", i=2, t=4),
                in0=sums[:].rearrange("p t (c i) -> p c t i", i=2),
                in1=act[mh, b][:, :, P * mc : P * (mc + 1)].rearrange("p t (c i) -> p c t i", i=2),
                op=MULT,
            )

        def quantize_h(mh, b):
            nc.vector.quantize_mx(
                out=h_c[mh, b][:].bitcast(FP8X4), scales=h_s[mh, b][:], in_=h_bf[mh, b].rearrange("p c w -> p (c w)")
            )

        wd_pair = [place("wd_pair%d" % u, [P, T, 2], BF16, PAIR_AT[u]) for u in range(2)]
        shared = keep.tile([P, 6 * HALF], BF16, name="shared", align_bytes=64)
        wd_bf = [
            shared[:, 2 * HALF : 6 * HALF].rearrange("p (b c) -> p b c", b=2),
            keep.tile([P, 2, 8 * P], BF16, name="wd_bf1", align_bytes=64)[:],
        ]
        wd_c = [keep.tile([P, 2, 2 * P], U32, name="wd_c%d" % u, align_bytes=64) for u in range(2)]
        wd_s = [keep.tile([P, 2, 2 * P], U8, name="wd_s%d" % u, align_bytes=64) for u in range(2)]

        def cast_wd(u, c):
            nc.scalar.copy(
                out=wd_pair[u][:, T // 2 * c : T // 2 * (c + 1), :].rearrange("p (x k) i -> p x i k", k=4),
                in_=wd_raw[u, c][:].rearrange("p i (x k) -> p x i k", k=4),
            )

        def pick_wd(u):
            return pick_all("wd_picked%d" % u, wd_pair[u][:].rearrange("p t i -> p (t i)"), F32)

        def turn_wd(u, picked, banks):
            for b in range(2):
                turned = bank(banks[b], [P, 4, P])
                for t in range(4):
                    nc.tensor.transpose(turned[:, t, :], picked[b][:, P * t : P * (t + 1)], ident[:])
                nc.scalar.copy(
                    out=wd_bf[u][:, b, :].rearrange("p (c i t) -> p c t i", i=4, t=4),
                    in_=turned[:].bitcast(BF16).rearrange("p t (c i) -> p c t i", i=4),
                )

        def quantize_wd(u):
            nc.vector.quantize_mx(
                out=wd_c[u][:].rearrange("p b n -> p (b n)").bitcast(FP8X4),
                scales=wd_s[u][:].rearrange("p b n -> p (b n)"),
                in_=wd_bf[u].rearrange("p b c -> p (b c)"),
            )

        def down_sums(mh, u, v, i):
            sums = bank(i, [P, HALF])
            for b in range(2):
                nc.tensor.matmul_mx(
                    out=sums[:],
                    lhsT=wd_c[u][:, b, P * v : P * (v + 1)].bitcast(FP8X4),
                    lhsT_scale=wd_s[u][:, b, P * v : P * (v + 1)],
                    rhs=h_c[mh, b][:].bitcast(FP8X4),
                    rhs_scale=h_s[mh, b][:],
                    start=(b == 0),
                    stop=(b == 1),
                )
            return sums

        def store(mh, u, v, y, c0, width):
            row = P * (2 * u + v)
            nc.sync.dma_start(out=out[row : row + P, HALF * mh + c0 : HALF * mh + c0 + width], in_=y[:])

        def finish(mh, u, v, sums, parts):
            width = HALF // parts
            for c0 in range(0, HALF, width):
                y = keep.tile([P, width], F32, name="y%d%d%d_%d" % (mh, u, v, c0))
                nc.vector.tensor_tensor(
                    out=y[:], in0=sums[:, c0 : c0 + width], in1=p_all[:, HALF * mh + c0 : HALF * mh + c0 + width], op=MULT
                )
                store(mh, u, v, y, c0, width)

        opened = [bank(t, [P, HALF]) for t in range(2)]
        for a in range(2):
            for t in range(2):
                first_pass(opened[t][:], a, gate_w, gate_s, 0, t, 0, HALF)
                if a == 1:
                    activate(0, 0, t, opened[t])
        for t in range(2, 4):
            activate(0, 0, t, gate_product(0, 0, t, t, 1))
        for t in range(4):
            activate(0, 1, t, gate_product(0, 1, t, 4 + t, 1))
        for t in range(2):
            activate(1, 0, t, gate_product(1, 0, t, t))
        for c in range(2):
            cast_wd(0, c)
        for mc in range(4):
            make_h(0, 0, mc, up_product(0, 0, mc, 2 + mc))
        second = [up_product(0, 1, mc, (6 + mc) % 8, 1) for mc in range(4)]
        for mc in range(3):
            make_h(0, 1, mc, second[mc])
        h_c[0, 0] = place("h_c00", [P, HALF], U32, X0_AT + 4 * HALF)
        p_all = place("p_all", [P, M], F32, P_AT)
        nc.sync.dma_start(out=p_all[:], in_=p.partition_broadcast(P))
        quantize_h(0, 0)
        make_h(0, 1, 3, second[3])
        apart[1, 0, 2] = place("silu102", [P, HALF], F32, RAW_AT[0, 1] + 4 * HALF)
        for t in range(2, 4):
            activate(1, 0, t, gate_product(1, 0, t, t))
        last_gate = [gate_product(1, 1, t, 4 + t) for t in range(2)]
        third = [up_product(1, 0, mc, (6 + mc) % 8) for mc in range(4)]
        last_gate.extend(gate_product(1, 1, t, t) for t in range(2, 4))
        for c in range(2):
            cast_wd(1, c)
            apart[1, 1, 2 * c] = place("silu11%d" % c, [P, HALF], F32, RAW_AT[1, c])
            for t in range(2 * c, 2 * c + 2):
                activate(1, 1, t, last_gate[t])
        picked = pick_wd(0)
        h_c[0, 1] = place("h_c01", [P, HALF], U32, RAW_AT[0, 1])
        quantize_h(0, 1)
        h_bf[1, 0] = place("h_bf10", [P, 4, 4 * P], BF16, PAIR_AT[0])[:]
        for mc in range(4):
            make_h(1, 0, mc, third[mc])
        fourth = [up_product(1, 1, mc, 4 + mc) for mc in range(2)]
        turn_wd(0, picked, (2, 3))
        fourth.extend(up_product(1, 1, mc, 4 + mc) for mc in range(2, 4))
        picked = pick_wd(1)
        h_c[1, 0] = place("h_c10", [P, HALF], U32, LAST_SILU_AT)
        quantize_h(1, 0)
        turn_wd(1, picked, (0, 1))
        h_bf[1, 1] = shared[:, 0 : 4 * HALF].rearrange("p (c w) -> p c w", c=4)
        for mc in range(2):
            make_h(1, 1, mc, fourth[mc])
        quantize_wd(0)
        early = [down_sums(0, 0, 0, 2)]
        for mc in range(2, 4):
            make_h(1, 1, mc, fourth[mc])
        early.append(down_sums(0, 0, 1, 7))
        finish(0, 0, 0, early[0], 1)
        quantize_h(1, 1)
        quantize_wd(1)
        finish(0, 0, 1, early[1], 1)
        for v in range(2):
            finish(1, 0, v, down_sums(1, 0, v, 4 + v), 1)
        for mh in range(2):
            for v in range(2):
                finish(mh, 1, v, down_sums(mh, 1, v, (6, 3, 0, 1)[2 * mh + v]), 1 + mh * v)
